import numpy as np, ml_dtypes
CORES = [48,51,52,55]
N = 4
BF = ml_dtypes.bfloat16
H, H0, L, CAP, S, JS, T = 4096, 3584, 1024, 128, 1, 4, 3
TB = 4 * 2 ** JS
def edges(rng, late=False):
    nt = H // TB; m = H0 // TB; half = (m // 2) * TB; w = np.arange(H) // TB
    t = rng.integers(0, nt, (N, 8, nt))
    if late: t[:, :, :m // 2] = rng.integers(0, m, (N, 8, m // 2))
    base = t[:, :, w] * TB
    x = base + rng.integers(0, TB, (N, 8, H)); y = base + rng.integers(0, TB, (N, 8, H))
    odd = rng.random((N, 8, H)) < 0.1
    if late: odd = odd & (np.arange(H) >= half)
    return x, np.where(odd, rng.integers(0, H, (N, 8, H)), y)
def packets(rng, alive, pb):
    on = rng.random((N, 8, L)) < alive; j = rng.integers(0, 16, (N, 8, 1, L))
    live = on[:, :, None] & ((rng.random((N, 8, 16, L)) < np.broadcast_to(pb, (N, 8, L))[:, :, None]) | (np.arange(16)[:, None] == j))
    a = (1 + 0.5 * rng.random((N, 8, 16, L))) * (1 - 2 * rng.integers(0, 2, (N, 8, 16, L)))
    q = rng.choice(np.array([0.0, 0.15, 0.5, 0.5, 0.85, 1.0]), (N, 8, 1, L))
    c = rng.random((N, 8, 16, L)) * np.where(rng.random((N, 8, 16, L)) < q, 1.0, -1.0)
    return live, a, c, rng.integers(0, H, (N, 8, L))
def pack(rng, live, a, c, h, x, y, kap=None, dam=None):
    if kap is None: kap = 0.5 + 0.5 * rng.random((N, 128, H), dtype=np.float32)
    if dam is None: dam = 1.5 + 2.5 * rng.random((N, 128, H), dtype=np.float32)
    c = np.where(np.abs(c) < 2.0 ** -20, 0.0 * c, c)
    return {"kap": kap.astype(BF), "dam": dam.astype(BF), "lf": x.astype(np.int32), "rt": y.astype(np.int32), "place": h.astype(np.int32),
            "cro": c.reshape(N, 128, L).astype(BF), "amp": np.where(live, np.abs(a), 0.0 * a).reshape(N, 128, L).astype(BF)}
def ends(rng, v, share):
    return np.where(rng.random(v.shape) < share, (H - 1) * rng.integers(0, 2, v.shape), v)
def setup_inputs(rng):
    x, y = edges(rng)
    alive = rng.permuted(np.tile(np.array([0.08, 0.12, 0.2, 0.25, 0.35, 0.45, 0.5, 0.6]), (N, 1)), axis=1)[:, :, None]
    live, a, c, h = packets(rng, alive, rng.choice(np.array([0.5, 0.8, 1.0]), (N, 8, L)))
    return pack(rng, live, a, c, h, x, y)
def setup_inputs_calm(rng):
    x, y = edges(rng); live, a, c, h = packets(rng, 0.6, 0.9); o = int(rng.integers(0, 8))
    for r in range(N):
        for k in range(5):
            g = (o + k) % 8
            x[r, g] = np.where(rng.random(H) < 0.002, rng.integers(H0, H, H), x[r, g] % H0); y[r, g] = np.where(rng.random(H) < 0.002, rng.integers(H0, H, H), y[r, g] % H0)
            live[r, g] = np.arange(16)[:, None] == rng.integers(0, 16, L)
            p = rng.permutation(L); h[r, g] = rng.integers(0, H0, L)
            two = p[:4]; live[r, g][:, two] = False
            for l in two:
                b = rng.permutation(16)[:2]; live[r, g, b, l] = True; c[r, g, b[0], l] = 0.5; c[r, g, b[1], l] = -0.5
            nd = (r + k) % 4; h[r, g, p[4:4 + nd]] = rng.integers(H0, H, nd)
            nf = (k + 2 * r + 1) % 4; live[r, g][:, p[8:8 + nf]] = False
    return pack(rng, live, a, c, h, x, y)
def setup_inputs_corners(rng):
    x, y = edges(rng, True); live, a, c, h = packets(rng, 1.0, 0.9); half = (H0 // TB // 2) * TB; n2 = (H - H0) // 2
    g0 = int(rng.integers(0, 8)); cell = {}
    for j in range(4):
        g = (g0 + (0, 4, 2, 6)[j]) % 8
        cell[0, g] = ((L - 2 * CAP, L - 2 * CAP + 1, (L - 2 * CAP) // 2, 0)[j], 0, 0)
        cell[N - 1, g] = (L // 2, (CAP + 1, L // 2, L // 2, 0)[j], 0)
        cell[N - S, (g - 1) % 8] = (L // 2, (CAP + 2, L // 2, L // 2, 0)[j], 1)
    for r in range(N):
        for g in range(8):
            n = (0, 1, L, L - 1, L - 2, L - 3, L // 2, L // 4)[(r + g) % 8]; v = (3 * r + g) % 8
            k = min(n, (CAP, CAP + 1, 1, 0, L, CAP - 1, 2, 3)[v]); odd = {0: 0, 1: 0, 5: 1}.get(v)
            if (r, g) in cell: n, k, odd = cell[r, g]
            p = rng.permutation(L)[:n] if n != 1 else np.array([L - 1])
            keep = np.zeros(L, bool); keep[p] = True; live[r, g] &= keep
            if (r, g) in cell and k == 0: live[r, g] = keep & (np.arange(16)[:, None] == rng.integers(0, 16, L))
            h[r, g] = rng.integers(0, half, L)
            par = rng.integers(0, 2, k) if odd is None else np.full(k, odd)
            h[r, g, p[:k]] = H0 + 2 * rng.integers(0, n2, k) + par
    g = (g0 + 2) % 8; o = rng.permutation(half); p, s, u = int(o[0]), int(o[1]), int(o[2])
    x[0, g, p] = s; x[0, g, s] = u; y[0, g, s] = (u + 2 ** JS) % half
    l = np.flatnonzero(np.any(live[0, g], axis=0)); b = rng.integers(0, 16, len(l)); b2 = (b + rng.integers(1, 16, len(l))) % 16
    live[0, g] = False; live[0, g, b, l] = True; live[0, g, b2, l] = True; h[0, g] = p
    c[0, g, b, l] = 1.0; c[0, g, b2, l] = 0.125 + 0.25 * rng.random(len(l))
    g = (g0 + 6) % 8
    for r, k, odd in ((N - 1, g, 0), (N - S, (g - 1) % 8, 1)):
        o = rng.permutation(half); p, s = int(o[0]), int(o[1]); door = H0 + 2 * int(rng.integers(0, n2)) + odd
        h[r, k] = p; x[r, k, p] = s; y[r, k, p] = s; x[r, k, s] = door; y[r, k, s] = door
    return pack(rng, live, a, c, h, x, y)
def setup_inputs_crowd(rng):
    x, y = edges(rng); live, a, c, h = packets(rng, 0.5, 1.0); i = (np.arange(16)[:, None] + np.arange(L)) % 16
    for r in range(N):
        for g in range(8):
            u = (r + g) % 8
            if u == 7: continue
            p = int(rng.integers(0, H0)); door = int(rng.integers(H0, H))
            h[r, g] = door if u in (3, 4) else p
            if u in (0, 1, 3, 4): live[r, g] = True
            if u in (1, 4): live[r, g][:, int(rng.integers(0, L))] = False
            if u == 4: h[r, g, int(rng.integers(0, L))] = p
            left = (16, 15, 8, 16, 1, 8, 7)[u]
            c[r, g] = np.abs(c[r, g]) * np.where(i < left, 1.0, -1.0)
            j = int(rng.integers(0, H0 // TB)) * TB
            if u in (0, 1, 2, 5, 6): x[r, g, p] = j; y[r, g, p] = j + (2 ** JS - 1 if u == 2 else 2 ** JS)
    g = int(rng.integers(0, 8)); e = 2 * int(rng.integers(0, (H - H0) // 2)); o = rng.permutation(H0); p = int(o[0]); s = int(o[1])
    live[N - 1, g] = True; h[N - 1, g] = H0 + e
    m = (e >> JS << JS) + rng.integers(0, 2 ** JS, 2)
    x[0, g, p] = s; y[0, g, p] = int(rng.integers(H0, H)); x[0, g, s] = m[0]; y[0, g, s] = m[1]
    l = rng.permutation(L)[:CAP]; b = rng.integers(0, 16, CAP); b2 = (b + rng.integers(1, 16, CAP)) % 16
    live[0, g] = False; live[0, g, b, l] = True; live[0, g, b2, l] = True; h[0, g] = p
    c[0, g, b, l] = 0.25 + 0.5 * rng.random(CAP); c[0, g, b2, l] = -0.25 - 0.5 * rng.random(CAP)
    return pack(rng, live, a, c, h, x, y)
def setup_inputs_ends(rng):
    x, y = edges(rng); x = ends(rng, x, 0.8); y = ends(rng, y, 0.8); k = (np.arange(N)[:, None] + np.arange(8)) % 4
    x[:, :, 0] = np.array([0, H - 1, 0, H0 - 1])[k]; y[:, :, 0] = np.array([H - 1, 0, 0, H - 1])[k]
    x[:, :, H - H0 - 1] = 0; y[:, :, H - H0 - 1] = H - 1; x[:, :, H - 1] = 0; y[:, :, H - 1] = H - 1
    live, a, c, h = packets(rng, 0.5, rng.integers(0, 2, (N, 8, L)).astype(np.float64)); h = ends(rng, h, 0.8)
    big = rng.random(a.shape) < rng.choice(np.array([0.0, 0.5, 1.0]), (N, 8, 1, L))
    a = np.where(a < 0, -1.0, 1.0) * np.where(big, 4.0, 0.25)
    e = rng.choice(np.array([-1.0, -2.0 ** -20, -0.0, 0.0, 2.0 ** -20, 1.0]), c.shape); c = np.where(rng.random(c.shape) < 0.7, e, c)
    h[:, :, 0] = 0; h[:, :, L - 1] = H - 1; h[N - 1, 7, L - 1] = 0; h[0, :4, L - 1] = 0
    tie = np.where(np.arange(16) < 8, 2.0 ** -20, -2.0 ** -20)
    for l in (0, L - 1): live[:, :, :, l] = True; c[:, :, :, l] = tie
    return pack(rng, live, a, c, h, x, y, np.where(rng.random((N, 128, H)) < 0.5, 0.5, 1.0), np.where(rng.random((N, 128, H)) < 0.25, 0.0, 4.0))
def setup_inputs_spread(rng):
    x, y = edges(rng); live, a, c, h = packets(rng, 0.5, 0.95)
    a = a * np.exp2(rng.integers(-1, 2, (N, 8, 1, L))); h = np.minimum((H * rng.random((N, 8, L)) ** 2).astype(np.int64), H - 1)
    low = rng.random((N, 1, H)) < 0.25
    dam = np.where(low, 1.4 * rng.random((N, 1, H)), 1.5 + 2 * rng.random((N, 1, H))) + 0.5 * rng.random((N, 128, H))
    kap = 0.5 + 0.5 * rng.random((N, 128, H), dtype=np.float32); i = np.arange(16) % 2
    for r in range(N):
        g = int(rng.integers(0, 8)); o = rng.permutation(H0); p, s, v = int(o[0]), int(o[1]), int(o[2]); l = rng.permutation(L)[:32]
        kap[r, 16 * g:16 * g + 16, p] = np.where(i == 0, 155, 205) * 2.0 ** -8; kap[r, 16 * g:16 * g + 16, s] = 132 * 2.0 ** -8
        x[r, g, p] = s; y[r, g, s] = v; h[r, g, l] = p
        live[r, g][:, l] = True; c[r, g][:, l] = (np.where(i == 0, 205, 155) * 2.0 ** -13)[:, None]
    return pack(rng, live, a, c, h, x, y, kap, dam)
def check_ranges(d):
    bad = []
    for k, lo, hi in (("lf", 0, H - 1), ("rt", 0, H - 1), ("place", 0, H - 1), ("kap", 0.5, 1.0), ("dam", 0.0, 4.0)):
        v = np.asarray(d[k], np.float64)
        if not (np.min(v) >= lo and np.max(v) <= hi): bad.append("range of " + k)
    for k, lo, hi in (("cro", 2.0 ** -20, 1.0), ("amp", 0.25, 4.0)):
        v = np.asarray(d[k], np.float64)
        if k == "cro": v = np.abs(v)
        if not np.all((v == 0) | ((v >= lo) & (v <= hi))): bad.append("range of " + k)
    return bad
def at(t, ix):
    return np.take_along_axis(t, ix, t.ndim - 1)
def reference(kap, dam, lf, rt, place, cro, amp):
    kf = kap.astype(np.float32).reshape(N, 8, 16, H)
    sg = np.reciprocal(1.0 + np.exp(-dam.astype(np.float64))).reshape(N, 8, 16, H)
    xt = lf.astype(np.int64); yt = rt.astype(np.int64); h = place.astype(np.int64)
    a = amp.astype(np.float64).reshape(N, 8, 16, L); one = np.float32(1); nil = np.float32(0)
    c = np.where(a != 0, cro.astype(np.float32).reshape(N, 8, 16, L), nil)
    own = np.arange(L); tw = np.tile(own, (N, 8, 1)); box = {}
    for step in range(T):
        live = a != 0; on = np.any(live, axis=2); go = on & (h < H0); moves = live & go[:, :, None]
        k = at(kf, h[:, :, None]) * c
        left = moves & (k >= 0); right = moves & (k < 0); k = np.float32(2) * k
        c = np.where(left, k - one, np.where(right, k + one, c))
        xl = at(xt, h); xr = at(yt, h)
        a = np.where(left, a * at(sg, xl[:, :, None]), np.where(right, a * at(sg, xr[:, :, None]), a))
        lw = np.sum(left, axis=2) >= np.sum(right, axis=2)
        out = np.where(lw[:, :, None], right, left); dis = np.any(out, axis=2)
        h = np.where(go, np.where(lw, xl, xr), h); other = np.where(lw, xr, xl)
        da = np.where(out, a, 0.0); dc = np.where(out, c, nil)
        a = np.where(out, 0.0, a); c = np.where(out, nil, c)
        for r in range(N):
            for g in range(8):
                w = np.flatnonzero(~on[r, g]); d = np.flatnonzero(dis[r, g])
                nh = [other[r, g, d]]; na = [da[r, g][:, d]]; nc = [dc[r, g][:, d]]; m = 0
                if step > 0:
                    e0, a0, c0 = box[(r - 1) % N, g]; e1, a1, c1 = box[(r - S) % N, (g - 1) % 8]
                    i0 = e0 % 2 == 0; i1 = e1 % 2 == 1
                    nh = [e0[i0], e1[i1]] + nh; na = [a0[:, i0], a1[:, i1]] + na; nc = [c0[:, i0], c1[:, i1]] + nc
                    m = len(nh[0]) + len(nh[1])
                nh = np.concatenate(nh); na = np.concatenate(na, axis=1); nc = np.concatenate(nc, axis=1)
                n = min(len(w), len(nh)); w = w[:n]
                h[r, g, w] = nh[:n]; a[r, g][:, w] = na[:, :n]; c[r, g][:, w] = nc[:, :n]
                tw[r, g, w[:m]] = w[:m]; born = w[m:]; par = d[:len(born)]
                tw[r, g, born] = par; tw[r, g, par] = born
        on = np.any(a != 0, axis=2)
        f = on & at(on, tw) & (at(tw, tw) == own) & (tw != own) & ((h >> JS) == (at(h, tw) >> JS))
        lo = (f & (own < tw))[:, :, None]; up = (f & (own > tw))[:, :, None]; ix = tw[:, :, None]
        a = np.where(lo, a + at(a, ix), np.where(up, 0.0, a)); c = np.where(lo, c + at(c, ix), np.where(up, nil, c))
        if step < T - 1:
            on = np.any(a != 0, axis=2)
            for r in range(N):
                for g in range(8):
                    e = np.flatnonzero(on[r, g] & (h[r, g] >= H0))[:CAP]
                    box[r, g] = (h[r, g, e] - H0, a[r, g][:, e], c[r, g][:, e])
                    a[r, g][:, e] = 0.0; c[r, g][:, e] = nil
    y = a * at(kf, h[:, :, None])
    return {"ya": y.reshape(N, 128, L).astype(np.float32), "yc": c.reshape(N, 128, L).astype(np.float32)}

def check_inputs(d):
    bad = list(check_ranges(d))
    if not bad:
        for name, y in reference(**d).items():
            for q in range(N):
                v = np.abs(np.asarray(y[q], np.float64)); s = np.sqrt(np.mean(v * v))
                if v.max() > 7 * s or s < 2.0 ** -4: bad.append('%s of rank %d is uneven or too small' % (name, q))
    return bad

@@ -1,0 +1,671 @@
+import numpy as np
+from concourse.bass import DstId, RemoteDMATransfer
+from concourse.mybir import AluOpType as A, AxisListType, ActivationFunctionType as F
+
+NF, NI, NU, NB = 72, 24, 24, 24
+SCRATCH = {
+    "KT": ("sbuf", [128, 5120], "bfloat16"), "DT": ("sbuf", [128, 4096], "bfloat16"), "XT": ("sbuf", [128, 5120], "bfloat16"),
+    "am": ("sbuf", [128, 1024], "bfloat16"), "cr": ("sbuf", [128, 1024], "bfloat16"), "c8": ("sbuf", [128, 1024], "bfloat16"),
+    "Z0": ("sbuf", [128, 1024], "bfloat16"),
+    "cmp": ("sbuf", [128, 512], "int32"), "ci": ("sbuf", [128, 1024], "int32"), "cb": ("sbuf", [128, 1024], "bfloat16"),
+    "pl": ("sbuf", [128, 64], "int32"),
+    "CW0": ("sbuf", [128, 3088], "float32"), "CW1": ("sbuf", [128, 3584], "float32"), "CW2": ("sbuf", [128, 3584], "float32"),
+    "AW0": ("sbuf", [128, 3088], "float32"), "AW1": ("sbuf", [128, 3584], "float32"), "AW2": ("sbuf", [128, 3584], "float32"),
+    "RW0": ("sbuf", [128, 4608], "bfloat16"), "RW1": ("sbuf", [128, 4608], "bfloat16"), "RW2": ("sbuf", [128, 4608], "bfloat16"),
+    "Z": ("sbuf", [128, 1024], "float32"), "G1": ("sbuf", [128, 1024], "float32"), "G2": ("sbuf", [128, 1024], "float32"),
+    "SL": ("sbuf", [128, 1024], "float32"), "SR": ("sbuf", [128, 1024], "float32"),
+    "sg": ("sbuf", [128, 1024], "bfloat16"), "dd": ("sbuf", [128, 1024], "bfloat16"), "X": ("sbuf", [128, 1024], "bfloat16"),
+    "RG": ("sbuf", [128, 1024], "bfloat16"), "IDT": ("sbuf", [128, 1024], "bfloat16"),
+    "MT": ("sbuf", [128, 128 * 13], "bfloat16"), "ZZ": ("sbuf", [128, 144 * 7], "bfloat16"), "OF": ("sbuf", [128, 128], "float32"),
+    "Q": ("sbuf", [128, 144], "float32"), "QG": ("sbuf", [128, 128], "float32"),
+    "WR": ("sbuf", [128, 192], "bfloat16"), "WO": ("sbuf", [128, 128], "float32"), "WP": ("sbuf", [128, 144], "bfloat16"),
+    "col": ("sbuf", [128, 96], "float32"), "coi": ("sbuf", [128, 8], "int32"),
+    "st": ("sbuf", [128, 64 * 4], "float32"), "Pc": ("sbuf", [128, 136], "float32"),
+    "cs1": ("sbuf", [128, 4], "float32"), "cs2": ("sbuf", [128, 4], "float32"),
+    "cn1": ("sbuf", [128, 4], "float32"), "cn2": ("sbuf", [128, 4], "float32"),
+    "bc1": ("sbuf", [128, 256], "float32"), "bc2": ("sbuf", [128, 256], "float32"),
+    "ba1": ("sbuf", [128, 256], "float32"), "ba2": ("sbuf", [128, 256], "float32"),
+    "br1": ("sbuf", [128, 256], "bfloat16"), "br2": ("sbuf", [128, 256], "bfloat16"),
+    "PF": ("sbuf", [128, 64 * NF], "float32"), "PI": ("sbuf", [128, 64 * NI], "int32"),
+    "PU": ("sbuf", [128, 64 * NU], "uint16"), "PB": ("sbuf", [128, 64 * NB], "bfloat16"),
+}
+for _b in range(8):
+    SCRATCH["P%d" % _b] = ("psum", [128, 512], "float32")
+NDMA = 40
+SEMAPHORES = ["V", "S", "P", "G", "sent"] + ["d%d" % _k for _k in range(NDMA)] + ["rc1", "rc2", "rr1", "rr2", "rd1", "rd2", "ra1", "ra2"]
+
+B = 8191
+FL, DUMP, EO, LT = 1280, 2304, 3328, 3584
+REST, DEAD, RIGHT = 1024, 2048, 2064
+MARK, THR = 1024.0, 32.0
+
+
+def v(name, c0, c1, step=1, p=None):
+    return (name, c0, c1, step, p)
+
+
+def sub(x, a, b, step=1):
+    return (x[0], x[1] + a, x[1] + b, step, x[4])
+
+
+def width(x):
+    return (x[2] - x[1] + x[3] - 1) // x[3]
+
+
+def plan(T, g, core, topo):
+    ops = []
+    rank = T.rank_of(core)
+    nxt = T.cores[(rank + 1) % len(T.cores)]
+    rid, pid = topo.addr(nxt)[0], topo.addr(nxt)[1]
+    eng = topo.engines(core, nxt)
+
+    def bits(es):
+        m = 0
+        for e in es:
+            m |= 1 << e
+        return m
+
+    def ap(x):
+        if not isinstance(x, tuple):
+            return x
+        p = x[4] or (0, 128, 1)
+        ps = slice(p[0], p[1], p[2]) if p[2] != 1 else slice(p[0], p[1])
+        cs = slice(x[1], x[2], x[3]) if x[3] != 1 else slice(x[1], x[2])
+        return T[x[0]][ps, cs]
+
+    def src(x):
+        return ap(x[1]).indirect(ap(x[2])) if x[0] == "ind" else ap(x)
+
+    def ind(win, off):
+        return ("ind", win, off)
+
+    def parts(*xs):
+        r = []
+        for x in xs:
+            if isinstance(x, tuple):
+                r += [x[1], x[2]] if x[0] == "ind" else [x]
+        return r
+
+    def two(x):
+        return SCRATCH[x[0]][2] in ("bfloat16", "uint16")
+
+    def psum(x):
+        return SCRATCH[x[0]][0] == "psum"
+
+    def add(q, fn, rd, wr, ns, **kw):
+        o = {"q": q, "fn": fn, "rd": rd, "wr": wr, "ns": ns}
+        o.update(kw)
+        ops.append(o)
+        return o
+
+    def vns(out, a, b=None):
+        if a[0] == "ind":
+            return 60 + width(out) * 1.56
+        n = width(out)
+        if b is not None:
+            return 60 + max(64, n * (1 if psum(a) or psum(b) else 2))
+        return 60 + max(64, n * (0.5 if two(a) and two(out) else 1))
+
+    def ts(out, a, s1, op0, s2=None, op1=None):
+        if op1 is None:
+            fn = lambda: g.vector.tensor_scalar(ap(out), src(a), ap(s1), None, op0)
+        else:
+            fn = lambda: g.vector.tensor_scalar(ap(out), src(a), ap(s1), ap(s2), op0, op1)
+        add("V", fn, parts(a, s1, s2), [out], vns(out, a))
+        return out
+
+    def tt(out, a, b, op):
+        add("V", lambda: g.vector.tensor_tensor(ap(out), src(a), ap(b), op), parts(a, b), [out], vns(out, a, b))
+        return out
+
+    def cp(out, a):
+        add("V", lambda: g.vector.tensor_copy(ap(out), src(a)), parts(a), [out], vns(out, a))
+        return out
+
+    def fill(out, c):
+        add("V", lambda: g.vector.memset(ap(out), c), [], [out], 60 + max(64, width(out) * (0.5 if two(out) else 1)))
+        return out
+
+    def scan(out, a):
+        one = sub(ONE, 0, width(a))
+        add("V", lambda: g.vector.tensor_tensor_scan(ap(out), ap(one), ap(a), 0.0, A.mult, A.add), [one, a], [out], 60 + max(64, width(a) * 0.5))
+        return out
+
+    def act(out, a, f, bias=None, scale=None, acc=None):
+        kw = {}
+        if bias is not None:
+            kw["bias"] = ap(bias)
+        if scale is not None:
+            kw["scale"] = ap(scale)
+        if acc is not None:
+            kw["accum_out"] = ap(acc)
+        add("S", lambda: g.scalar.activation(ap(out), src(a), f, **kw), parts(a, bias, scale), [out] + parts(acc),
+            100 + max(64, width(out) * (1.56 if a[0] == "ind" else 1)))
+        return out
+
+    def mm(out, pairs, first=True, last=True, slow=1):
+        def fn():
+            for k, (l, r) in enumerate(pairs):
+                i = g.tensor.matmul(ap(out), ap(l), ap(r), first and k == 0, last and k == len(pairs) - 1)
+            return i
+        add("P", fn, [x for pr in pairs for x in pr], [out], 30 + len(pairs) * max(64, width(out)) * slow)
+        return out
+
+    def wrap(out, z, wide):
+        n = width(wide)
+        return mm(out, [(sub(z, 15 - i, 143 - i), sub(wide, i, n, 16)) for i in range(16)])
+
+    def iota(out, pat, base, cm):
+        kw = {} if SCRATCH[out[0]][2] == "int32" else {"allow_small_or_imprecise_dtypes": True}
+        add("G", lambda: g.iota(ap(out), pat, base, cm, **kw), [], [out], 160 + 2 * width(out))
+        return out
+
+    nd = [0]
+
+    def dma(q, out, a, rd, wr, lat):
+        k = nd[0]
+        nd[0] += 1
+        if q == "G":
+            return add(q, lambda: g.dma_start(out, a, accum_op=A.add), rd + wr, wr, 1000, sem="d%d" % k, inc=16, lat=lat)
+        e = g.sync if q == "Y" else g.scalar
+        return add(q, lambda: e.dma_start(out, a), rd, wr, 60, sem="d%d" % k, inc=16, lat=lat)
+
+    def send(pairs, es, rsem):
+        k = len(es) // len(pairs)
+
+        def fn():
+            if len(pairs) == 1:
+                return g.remote_dma(ap(pairs[0][0]), ap(pairs[0][1]), T.sem[rsem], T.sem.sent, pid, rid, bits(es))
+            return g.remote_dma_fused([RemoteDMATransfer(dst_ids=[DstId(rid=rid, pnc=pid)], dma_engine_mask=bits(es[j * k:j * k + k]),
+                                                         remote_sem=T.sem[rsem], src=ap(s), dst=ap(d))
+                                       for j, (d, s) in enumerate(pairs)], local_sem=T.sem.sent)
+        o = add("G", fn, [s for d, s in pairs], [], 500, sent=len(es))
+        add("R", None, [], [d for d, s in pairs], 0, sem=rsem, inc=len(es), lat=2200, after=o)
+
+    ring = {"PF": [0, NF], "PI": [0, NI], "PU": [0, NU], "PB": [0, NB], "col": [32, 96]}
+
+    def new(pool, n=64):
+        r = ring[pool]
+        k = (n + 63) // 64
+        if r[0] + k > r[1]:
+            r[0] = 0
+        x = v(pool, 64 * r[0], 64 * r[0] + n)
+        r[0] += k
+        return x
+
+    def f():
+        return new("PF")
+
+    def c():
+        r = ring["col"]
+        r[0] += 1
+        return v("col", r[0] - 1, r[0])
+
+    H = [(0, 512), (512, 1024)]
+
+    def wide(name, h, base=0):
+        return v(name, base + H[h][0], base + H[h][1])
+
+    def half(off, h):
+        return sub(off, 32 * h, 32 * h + 32)
+
+    def bank(b, a=0, n=512):
+        return v("P%d" % b, a, a + n)
+
+    dma("Y", T.cmp[:, 0:256], T.lf[:, :], [], [v("cmp", 0, 256)], 2300)
+    dma("Y", T.cmp[:, 256:512], T.rt[:, :], [], [v("cmp", 256, 512)], 2300)
+    dma("S", T.am[:, :], T.amp[:, :], [], [v("am", 0, 1024)], 2500)
+    dma("S", T.cr[:, :], T.cro[:, :], [], [v("cr", 0, 1024)], 2600)
+    for b in range(2):
+        for u in range(2):
+            a = 32 * b + 16 * u
+            dma("Y", T.pl[:, a:a + 16], T.place[u::2, 512 * b:512 * b + 512], [], [v("pl", a, a + 16)], 2400)
+    dma("S", T.KT[:, 0:4096], T.kap[:, :], [], [v("KT", 0, 4096)], 4300)
+    dma("S", T.DT[:, :], T.dam[:, :], [], [v("DT", 0, 4096)], 5800)
+
+    fill(v("XT", 0, 4096), 0.0)
+    pi, pl16, pg = v("coi", 0, 1), v("coi", 1, 2), v("coi", 2, 3)
+    pcol, icol, g16, g15, gsh, psh = [v("col", k, k + 1) for k in range(6)]
+    iota(pi, [[0, 1]], 0, 1)
+    Q, QG = iota(v("Q", 0, 144), [[1, 144]], 0, 0), iota(v("QG", 0, 128), [[16, 8], [0, 16]], 0, 0)
+    JW = v("Q", 0, 128)
+    iota(v("IDT", 0, 512, 1, (0, 64, 1)), [[1, 32], [0, 16]], 0, 0)
+    iota(v("IDT", 0, 512, 1, (64, 128, 1)), [[0, 32], [1, 16]], 0, 0)
+    ts(pl16, pi, 15, A.bitwise_and)
+    cp(pcol, pi)
+    act(v("IDT", 512, 1024), v("IDT", 0, 512), F.Identity, bias=ts(v("col", 7, 8), pcol, 64.0, A.is_lt, 32.0, A.mult))
+    cp(icol, pl16)
+    ts(g16, pcol, icol, A.subtract)
+    ts(g15, g16, 15.0, A.add)
+    wrapc = ts(v("col", 6, 7), pcol, 112.0, A.is_ge, -128.0, A.mult)
+    ts(gsh, g16, wrapc, A.add, 16.0, A.add)
+    ts(psh, pcol, wrapc, A.add, 16.0, A.add)
+    l16 = iota(v("st", 192, 256), [[16, 64]], 0, 0)
+    lane = ts(v("st", 0, 64), l16, icol, A.add)
+    lane1 = act(v("st", 64, 128), lane, F.Identity, bias=float(DUMP - B))
+    lane2 = act(v("st", 128, 192), lane, F.Identity, bias=float(LT - FL - B))
+    jb = act(v("col", 8, 16), sub(lane, 0, 8), F.Identity, bias=0.5)
+    M = [v("MT", 128 * k, 128 * k + 128) for k in range(13)]
+    ONES, ID, NUS, NBG, SO, SH, MX, NSO, MR, MD, MI, MJ, MD1 = M
+    ONE = fill(v("PB", 64 * (NB - 2), 64 * NB), 1.0)
+    ring["PB"][1] = NB - 2
+    ts(ONES, QG, g16, A.is_equal)
+    ts(ID, JW, pcol, A.is_equal)
+    t0 = ts(new("PB", 128), JW, pcol, A.is_lt, -1.0, A.mult)
+    tt(NUS, t0, ONES, A.mult)
+    t1 = act(new("PB", 128), ID, F.Identity, scale=-(B + 1.0))
+    tt(NBG, t1, NUS, A.add)
+    fill(v("MT", 128 * 8, 128 * 12), 0.0)
+    for m, r, w in ((MR, 2, 1.0), (MR, 3, -0.5), (MR, 5, 0.5), (MD, 2, -1 / MARK), (MD, 5, -1 / MARK)):
+        act(sub(m, r, 128, 8), sub(ONES, r, 128, 8), F.Identity, scale=w)
+    fill(v("MT", MI[1] + 6, MI[2], 16, (0, 1, 1)), 1.0)
+    fill(v("MT", MI[1] + 14, MI[2], 16, (64, 65, 1)), 1.0)
+    fill(v("MT", MJ[1], MJ[2], 8, (0, 1, 1)), 16.0)
+    fill(v("MT", MJ[1] + 4, MJ[2], 8, (64, 65, 1)), 1.0)
+    p0, p16 = (0, 1, 1), (0, 16, 1)
+    fill(v("WR", 0, 192, 1, p0), 0.0)
+    AB, FG, DQ, QM, XL, XR, BR, BG, BD, XM, C1, BR1 = range(12)
+    for z, r0, r1, w0, w1 in ((BR, 3, 11, 8, 7), (BR, 5, 13, 8, 7), (AB, 3, 11, 1, -1), (AB, 5, 13, 1, -1),
+                              (FG, 6, 14, 16, 1), (FG, 3, 11, -2048, 2048), (FG, 5, 13, -2048, 2048), (FG, 2, 10, 8192, -8192),
+                              (FG, 7, 9, 2048, 6144)):
+        iota(v("WR", 16 * z + r0, 16 * z + r1 + 1, r1 - r0, p0), [[w1 - w0, 2]], w0, 0)
+    for k, (z, r0, r1, d, w) in enumerate((
+            (BG, 1, 8, 6, 1), (BD, 0, 9, 8, 3584), (XL, 0, 5, 4, 1), (XR, 8, 13, 4, 1), (BR, 2, 10, 7, 1), (DQ, 0, 5, 4, 1),
+            (DQ, 8, 13, 4, -1), (QM, 0, 13, 4, 0.5), (XM, 0, 13, 4, 1), (BD, 1, 2, 1, 1), (C1, 1, 2, 1, -100),
+            (DQ, 1, 2, 1, RIGHT * 4096), (DQ, 9, 10, 1, -RIGHT * 4096), (QM, 6, 7, 1, 65536), (QM, 14, 15, 1, 4096),
+            (QM, 9, 10, 1, (RIGHT // 2 - DEAD) * 4096), (QM, 1, 2, 1, (REST - RIGHT // 2) * 4096))):
+        x = v("WR", 16 * z + r0, 16 * z + r1, d, p0)
+        if k % 4 == 3:
+            fill(x, float(w))
+        else:
+            act(x, x, F.Identity, bias=float(w))
+    rep = iota(v("WO", 0, 128, 1, p16), [[0, 8], [1, 16]], 0, -1)
+    rep = ts(v("WP", 0, 128, 1, p16), rep, 0.0, A.is_equal)
+    for z in range(12):
+        mm(v("P4", z, z + 1, 1, p16), [(v("WR", 16 * z, 16 * z + 16, 1, p0), v("PB", ONE[1], ONE[1] + 1, 1, p0))])
+    act(v("WP", 128, 140, 1, p16), v("P4", 0, 12, 1, p16), F.Identity)
+    mm(bank(4, 16, 12), [(rep, v("WP", 128, 140, 1, p16))])
+    act(v("col", 16, 28), bank(4, 16, 12), F.Identity)
+    W = [v("col", 16 + z, 17 + z) for z in range(12)]
+    ZM = [v("ZZ", 144 * z, 144 * z + 144) for z in range(7)]
+    ZS = ts(ZM[6], Q, g15, A.is_equal)
+    for z in range(6):
+        ts(ZM[z], ZS, W[z], A.mult)
+    act(MX, ID, F.Identity)
+    act(sub(MX, 3, 128, 8), sub(ONES, 3, 128, 8), F.Identity, scale=W[C1])
+    act(sub(MX, 5, 128, 8), sub(ONES, 5, 128, 8), F.Identity, scale=W[C1])
+    ts(SO, QG, gsh, A.is_equal)
+    act(NSO, SO, F.Identity, scale=-1.0)
+    ts(SH, JW, psh, A.is_equal)
+    OF = act(v("OF", 0, 128), ONES, F.Identity)
+    act(v("KT", 4096, 5120), v("am", 0, 1024), F.Identity, scale=0.0, bias=0.5)
+    fill(v("Pc", 128, 136), 0.0)
+    for t in range(3):
+        fill(v("CW%d" % t, DEAD, DEAD + 8), MARK)
+        fill(v("AW%d" % t, DEAD, DEAD + 8), 0.0)
+    mm(bank(6), [(MJ, v("IDT", 0, 512))])
+    act(v("XT", 4096, 4608), bank(6), F.Identity, bias=W[BD])
+    act(v("XT", 4608, 5120), bank(6), F.Identity, bias=W[BG])
+    ts(v("cb", 0, 512), v("cmp", 0, 512), -8.0, A.add, 0.0, A.max)
+    for k, r in ((0, 0), (1, 8)):
+        dma("Y", T.XT[r::16, 0:4096], T.cb[:, 256 * k:256 * k + 256], [v("cb", 256 * k, 256 * k + 256)], [v("XT", 0, 4096, 1, (r, 128, 16))], 2600)
+    tt(v("cb", 512, 1024), v("cmp", 0, 512), v("cb", 0, 512), A.subtract)
+    for k, r in ((2, 4), (3, 12)):
+        dma("Y", T.XT[r::16, 0:4096], T.cb[:, 256 * k:256 * k + 256], [v("cb", 256 * k, 256 * k + 256)], [v("XT", 0, 4096, 1, (r, 128, 16))], 2600)
+    iota(v("RW0", 0, FL), [[0, FL]], 0, 0)
+
+    pf = cp(f(), v("pl", 0, 64))
+    hf = f()
+    add("V", lambda: g.vector.transpose(ap(hf), ap(pf)), [pf], [hf], 124)
+    d5 = ts(f(), hf, 3584.0, A.is_ge, 512.0, A.mult)
+    hx = cp(new("PU"), tt(f(), hf, d5, A.add))
+    ts(v("dd", 0, 1024), v("am", 0, 1024), 0.0, A.is_equal, MARK, A.mult)
+    for h in range(2):
+        act(bank(2 + h), wide("cr", h), F.Identity, scale=8.0)
+        tt(wide("Z0", h), bank(2 + h), wide("dd", h), A.add)
+    act(v("AW0", REST, REST + 1024), v("am", 0, 1024), F.Identity)
+    wrap(bank(7, 0, 64), ZS, v("dd", 0, 1024))
+    occ = ts(f(), bank(7, 0, 64), 16 * MARK - 1, A.is_lt)
+    tw, npo = lane2, None
+
+    for t in range(3):
+        CW, AW, RW = "CW%d" % t, "AW%d" % t, "RW%d" % t
+        zn = "Z0" if t == 0 else "Z"
+        e = float(4 >> t)
+        last = t == 2
+        for h in range(2):
+            act(wide("X", h), ind(v("XT", 0, 5120), half(hx, h)), F.Identity)
+            act(wide("sg", h), wide(zn, h), F.Sign, bias=2.0 ** -40)
+            if t:
+                ts(wide("dd", h), wide(zn, h), THR, A.is_ge, MARK, A.mult)
+        for h in range(2):
+            mm(bank(h), [(MI, wide("IDT", h))], last=False)
+            mm(bank(h), [(MR, wide("sg", h))], first=False, last=False)
+            mm(bank(h), [(MD, wide("dd", h))], first=False, last=False)
+            mm(bank(h), [(MX, wide("X", h))], first=False)
+            act(wide(RW, h, LT), bank(h), F.Relu, bias=W[BR])
+        if t:
+            br = "br%d" % t
+            act(v(br, 0, 128), ind(v("X", 0, 1024), lvl), F.Identity, scale=W[XM])
+            mm(bank(7, 0, 128), [(SH, v(br, 0, 128))])
+            act(v(br, 128, 256), bank(7, 0, 128), F.Identity)
+            send([(v(RW, EO, EO + 256), v(br, 0, 256))], eng[0:4], "rr%d" % t)
+        fr = act(new("PB"), occ, F.Identity, scale=-1.0, bias=1.0)
+        sc = scan(new("PB"), fr)
+        mm(bank(5, 0, 64), [(ONES, sc), (NBG, fr)])
+        mm(bank(5, 64, 1), [(ONES, sub(sc, 63, 64))])
+        jf = act(f(), bank(5, 0, 64), F.Identity, bias=-float(FL))
+        fc = act(c(), bank(5, 64, 1), F.Identity, bias=-float(B))
+        js = act(f(), bank(5, 0, 64), F.Identity, bias=float(FL))
+        more = []
+        if t:
+            cn = "cn%d" % t
+            ca, cb, c1, d1 = [v(cn, k, k + 1) for k in range(4)]
+            more = [(ID, act(new("PB"), sub(ONE, 0, 64), F.Identity, scale=float(B + FL), bias=cb))]
+            a1 = ts(f(), jf, ca, A.is_lt, c1, A.mult)
+            a2 = ts(f(), jf, cb, A.is_lt, d1, A.mult)
+            vv = tt(f(), tt(f(), a1, a2, A.add), jf, A.add)
+            arr = ts(f(), jf, cb, A.is_lt)
+            e2 = tt(f(), act(f(), vv, F.Identity, scale=4096.0, bias=(FL + B - DEAD) * 4096.0), arr, A.mult)
+        else:
+            cb, vv = -float(B + FL), jf
+        base1 = tt(f(), js, lane1, A.min)
+        base2 = tt(f(), vv, tw, A.min)
+        wrap(bank(4, 0, 64), ZM[XL], v("X", 0, 1024))
+        wrap(bank(4, 64, 64), ZM[XR], v("X", 0, 1024))
+        xlr = cp(new("PU", 128), bank(4, 0, 128))
+        xl, xr = sub(xlr, 0, 64), sub(xlr, 64, 128)
+        rec = v(RW, LT, LT + 1024)
+        wrap(bank(7, 0, 64), ZM[AB], rec)
+        dis = ts(new("PB"), bank(7, 0, 64), 2.0, A.is_ge)
+        sc = scan(new("PB"), dis)
+        xq = mm(bank(6, 0, 64), more + [(NBG, dis), (ONES, sc)])
+        ndc = mm(bank(5, 0, 1), [(ONES, sub(sc, 63, 64))])
+        off1 = ts(new("PU"), tt(f(), xq, base1, A.min), float(B), A.add)
+        nsb = ts(f(), xq, fc, A.is_ge, 16384.0, A.mult)
+        bb = tt(f(), xq, nsb, A.add)
+        ns = act(f(), nsb, F.Identity, scale=1 / 16384.0)
+        succ = act(f(), nsb, F.Identity, scale=-1 / 16384.0, bias=1.0)
+        cnw = act(c(), ndc, F.Identity, bias=cb)
+        off2 = ts(new("PU"), tt(f(), bb, base2, A.min), float(FL + B), A.add)
+        add("V", (lambda RW, rec, off1: lambda: g.vector.tensor_copy(ap(v(RW, 0, EO)).indirect(ap(off1)), ap(rec)))(RW, rec, off1),
+            [rec, off1], [v(RW, 0, EO)], 60 + 1024 * 3.8)
+        for h in range(2):
+            act(wide("RG", h), ind(v(RW, 0, 4608), half(off2, h)), F.Identity)
+        if t < 2:
+            iota(v("RW%d" % (t + 1), 0, FL), [[0, FL]], 0, 0)
+        wrap(bank(7, 0, 64), ZM[FG], rec)
+        wrap(bank(0, 0, 64), ZM[DQ], rec)
+        wrap(bank(1, 0, 64), ZM[QM], rec)
+        if t:
+            mm(bank(5, 64, 64), more + [(NUS, dis), (ONES, sc)])
+            lb = act(c(), fc, F.Identity, bias=B + 0.5)
+            acc = c()
+            act(f(), bank(5, 64, 64), F.Sign, bias=lb, scale=-1.0, acc=acc)
+            mm(bank(5, 128, 1), [(OF, acc)], slow=4)
+            lst = act(c(), bank(5, 128, 1), F.Identity, bias=512.0 + 2048, scale=0.5)
+        lw = ts(f(), bank(7, 0, 64), 8192.0, A.is_ge, -0.5, A.add)
+        tq = tt(f(), lw, bank(0, 0, 64), A.mult)
+        qw = tt(f(), bank(1, 0, 64), tq, A.add)
+        qo = tt(f(), bank(1, 0, 64), tq, A.subtract)
+        newc = ts(f(), jf, cnw, A.is_lt)
+        ep = tt(f(), occ, qw, A.mult)
+        sqo = tt(f(), succ, qo, A.mult)
+        pair = tt(f(), succ, newc, A.add)
+        if t:
+            ep = tt(f(), ep, e2, A.add)
+            pair = tt(f(), pair, arr, A.subtract)
+        if not last:
+            on0 = tt(f(), occ, newc, A.add)
+        for h in range(2):
+            tt(wide(CW, h, REST), ind(v("KT", 0, 5120), half(hx, h)), wide(zn, h), A.mult)
+        act(v(CW, 0, 1024), v("sg", 0, 1024), F.Identity, bias=(MARK - e) / 2, scale=-(MARK + e) / 2)
+        act(v(CW, RIGHT, RIGHT + 1024), v("sg", 0, 1024), F.Identity, bias=(MARK + e) / 2, scale=(MARK - e) / 2)
+        for a in (0, RIGHT):
+            dma("G", ap(v(CW, a, a + 1024)), ap(v(CW, REST, REST + 1024)), [v(CW, REST, REST + 1024)], [v(CW, a, a + 1024)], 4000)
+        for h in range(2):
+            act(wide("SL", h), ind(v("DT", 0, 4096), half(xl, h)), F.Sigmoid)
+            act(wide("SR", h), ind(v("DT", 0, 4096), half(xr, h)), F.Sigmoid)
+            mm(bank(2), [(ID, wide("sg", h))])
+            tt(bank(3), wide(AW, h, REST), bank(2), A.mult)
+            act(bank(2), bank(3), F.Identity, scale=-1.0)
+            tt(wide(AW, h), wide("SL", h), bank(3), A.mult)
+            tt(wide(AW, h, RIGHT), wide("SR", h), bank(2), A.mult)
+        rg = v("RG", 0, 1024)
+        pf_, pd, pr = bank(7, 0, 64), bank(0, 0, 64), bank(1, 0, 64)
+        wrap(pf_, ZM[FG], rg)
+        wrap(pd, ZM[DQ], rg)
+        wrap(pr, ZM[QM], rg)
+        lw = ts(f(), pf_, 8192.0, A.is_ge, -0.5, A.add)
+        idi = cp(new("PI"), pf_)
+        if t:
+            key = ts(new("PI"), idi, 8191, A.bitwise_and)
+            old = tt(f(), ts(f(), key, lst, A.is_ge), npo, A.mult)
+            pair = tt(f(), pair, old, A.max)
+        idn = ts(new("PI"), idi, 1023, A.bitwise_and)
+        gt = tt(f(), idn, lane, A.is_gt)
+        tq = tt(f(), lw, pd, A.mult)
+        qq = new("PF", 128)
+        qo = tt(f(), pr, tq, A.subtract)
+        qw = tt(f(), pr, tq, A.add)
+        tt(sub(qq, 0, 64), tt(f(), newc, qo, A.mult), ep, A.add)
+        tt(sub(qq, 64, 128), tt(f(), ns, qw, A.mult), sqo, A.add)
+        qi = cp(new("PI", 128), qq)
+        jj = ts(new("PI", 128), qi, 4, A.arith_shift_right, 255, A.bitwise_and)
+        sr = ts(new("PI", 128), qi, 12, A.arith_shift_right)
+        hi = ts(new("PI"), sub(qi, 0, 64), 4095, A.bitwise_and)
+        fuse = tt(f(), tt(f(), sub(jj, 0, 64), sub(jj, 64, 128), A.is_equal), pair, A.mult)
+        mk = new("PF", 128)
+        lo = tt(sub(mk, 64, 128), fuse, gt, A.mult)
+        nup = tt(sub(mk, 0, 64), fuse, gt, A.is_le)
+        s16 = ts(new("PU", 128), tt(new("PF", 128), sr, mk, A.mult), float(DEAD), A.add)
+        sa, sb = sub(s16, 0, 64), sub(s16, 64, 128)
+        wn = SCRATCH[CW][1][1]
+        an = ("G1", 0) if last else ("AW%d" % (t + 1), REST)
+        for h in range(2):
+            act(wide("G1", h), ind(v(CW, 0, wn), half(sa, h)), F.Identity)
+        for h in range(2):
+            tt(wide("Z", h), ind(v(CW, 0, wn), half(sb, h)), wide("G1", h), A.min)
+        if last:
+            h16 = cp(new("PU"), hi)
+            for h in range(2):
+                act(wide("G2", h), ind(v(AW, 0, wn), half(sa, h)), F.Relu)
+                act(bank(4 + h), wide("Z", h), F.Sigmoid, bias=THR, scale=-1.0)
+            for h in range(2):
+                tt(wide("SL", h), wide("Z", h), bank(4 + h), A.mult)
+                dma("Y", T.yc[:, H[h][0]:H[h][1]], ap(wide("SL", h)), [wide("SL", h)], [], 2400)
+                tt(wide("G1", h), ind(v(AW, 0, wn), half(sb, h)), wide("G2", h), A.max)
+                tt(wide("SR", h), ind(v("KT", 0, 4096), half(h16, h)), wide("G1", h), A.mult)
+                dma("Y", T.ya[:, H[h][0]:H[h][1]], ap(wide("SR", h)), [wide("SR", h)], [], 2400)
+            break
+        d5 = ts(f(), hi, 3584.0, A.is_ge, 512.0, A.mult)
+        on = tt(f(), on0, nup, A.mult)
+        dr = tt(new("PB"), d5, on, A.mult)
+        sc = scan(new("PB"), dr)
+        y = mm(bank(6, 0, 64), [(NBG, dr), (ONES, sc)])
+        hd = tt(f(), hi, d5, A.add)
+        l5 = ts(f(), y, 512.0 * (128 - B), A.is_lt, 512.0, A.mult)
+        lv = act(f(), l5, F.Identity, scale=1 / 512.0)
+        hx = cp(new("PU"), tt(f(), hd, l5, A.add))
+        occ = tt(f(), on, lv, A.subtract)
+        npo = tt(f(), tt(f(), pair, fuse, A.subtract), occ, A.mult)
+        tw = tt(f(), tt(f(), npo, tt(f(), idn, lane, A.subtract), A.mult), lane2, A.add)
+        an1 = v(an[0], an[1], an[1] + 1024)
+        act(an1, ind(v(AW, 0, wn), sa), F.Relu)
+        act(v("G2", 0, 1024), ind(v(AW, 0, wn), sb), F.Relu)
+        dma("G", ap(an1), ap(v("G2", 0, 1024)), [v("G2", 0, 1024)], [an1], 4000)
+        x2 = new("PB", 128)
+        od = tt(sub(x2, 64, 128), ts(new("PI"), hi, 1, A.bitwise_and), lv, A.mult)
+        tt(sub(x2, 0, 64), lv, od, A.subtract)
+        sc = scan(new("PB", 128), x2)
+        e0, e1 = sub(sc, 63, 64), sub(sc, 127, 128)
+        mm(bank(6, 128, 128), [(ONES, sc)])
+        mm(bank(4, 0, 1), [(ONES, e0)])
+        mm(bank(4, 1, 1), [(ONES, e0), (SO, e1), (NSO, e0)])
+        mm(bank(4, 2, 1), [(ONES, e0), (NSO, e0)])
+        mm(bank(7, 128, 128), [(NUS, x2), (ONES, sc)])
+        cs = "cs%d" % (t + 1)
+        act(v(cs, 0, 2), bank(4, 0, 2), F.Identity, bias=-float(B + FL))
+        act(v(cs, 2, 3), bank(4, 2, 1), F.Identity, bias=-128.0)
+        act(v(cs, 3, 4), bank(4, 2, 1), F.Identity, scale=-1.0, bias=EO + 128.0)
+        send([(v("cn%d" % (t + 1), 0, 4), v(cs, 0, 4))], eng[0:4], "rc%d" % (t + 1))
+        act(v("Pc", 0, 128), bank(7, 128, 128), F.Identity)
+        acc = new("PF", 8)
+        for j in range(8):
+            act(v("RG", 128 * j, 128 * j + 128), bank(6, 128, 128), F.Sign, bias=sub(jb, j, j + 1), scale=-1.0, acc=sub(acc, j, j + 1))
+        b16 = ts(new("PU", 8), acc, 0.5, A.mult, 64.0, A.add)
+        cm = tt(new("PB", 128), ind(v("Pc", 0, 136), b16), JW, A.is_le)
+        b6 = tt(new("PF", 8), ts(new("PF", 8), acc, 0.0, A.is_ge, -1024.0, A.mult), act(new("PF", 8), acc, F.Identity, scale=8.0, bias=1024.0), A.add)
+        wrap(bank(7, 0, 8), ZS, cm)
+        lvl = ts(new("PU", 8), tt(new("PF", 8), b6, bank(7, 0, 8), A.add), 1023.0, A.min)
+        bc, ba = "bc%d" % (t + 1), "ba%d" % (t + 1)
+        act(v(bc, 0, 128), ind(v("Z", 0, 1024), lvl), F.Identity, scale=0.5)
+        act(v(ba, 0, 128), ind(v(an[0], an[1], an[1] + 1024), lvl), F.Identity)
+        for n in (bc, ba):
+            dma("Y", T[n][16:128, 128:256], T[n][0:112, 0:128], [v(n, 0, 128)], [v(n, 128, 256, 1, (16, 128, 1))], 2200)
+            dma("Y", T[n][0:16, 128:256], T[n][112:128, 0:128], [v(n, 0, 128)], [v(n, 128, 256, 1, (0, 16, 1))], 2200)
+        send([(v("CW%d" % (t + 1), EO, EO + 256), v(bc, 0, 256))], eng[0:4], "rd%d" % (t + 1))
+        send([(v("AW%d" % (t + 1), EO, EO + 256), v(ba, 0, 256))], eng[0:4], "ra%d" % (t + 1))
+    return ops
+
+
+HOP, TRIES, FOUND = 80, 4000, {}
+
+
+def meet(a, b):
+    if a[0] != b[0] or a[2] <= b[1] or b[2] <= a[1]:
+        return False
+    if a[3] == b[3] and a[3] > 1 and (a[1] - b[1]) % a[3]:
+        return False
+    if a[4] and b[4]:
+        if a[4][1] <= b[4][0] or b[4][1] <= a[4][0]:
+            return False
+        if a[4][2] == b[4][2] and (a[4][0] - b[4][0]) % a[4][2]:
+            return False
+    return True
+
+
+def order(ops):
+    n = len(ops)
+    pre = [dict() for _ in ops]
+    seen = {}
+    for j, o in enumerate(ops):
+        if "after" in o:
+            pre[j][ops.index(o["after"])] = False
+        for x, w in [(x, False) for x in o["rd"]] + [(x, True) for x in o["wr"]]:
+            ps = SCRATCH[x[0]][0] == "psum"
+            for i, y, wy in seen.get(x[0], []):
+                if i == j:
+                    continue
+                same = ops[i]["q"] == o["q"] and "sem" not in ops[i]
+                if ps and not same:
+                    pre[j][i] = True
+                elif (w or wy) and meet(x, y):
+                    pre[j][i] = pre[j].get(i, False) or not same or o["q"] != "P"
+                elif ps and w and wy:
+                    pre[j][i] = pre[j].get(i, False)
+        for x, w in [(x, False) for x in o["rd"]] + [(x, True) for x in o["wr"]]:
+            seen.setdefault(x[0], []).append((j, x, w))
+    post = [[] for _ in ops]
+    for j in range(n):
+        for i in pre[j]:
+            post[i].append(j)
+    tail = [0.0] * n
+    for i in range(n - 1, -1, -1):
+        tail[i] = ops[i]["ns"] + ops[i].get("lat", 0) + max([tail[j] + HOP for j in post[i]] or [0])
+    if n not in FOUND:
+        rng = np.random.RandomState(7)
+        best, pr = None, list(tail)
+        for k in range(TRIES):
+            tr = list(pr)
+            if k:
+                a = int(rng.randint(n))
+                for i in rng.randint(max(0, a - 60), min(n, a + 60), int(rng.randint(1, 12))):
+                    tr[i] += float(rng.normal()) * (300, 1000, 3000)[k % 3]
+            seq, start = issue(ops, pre, post, tr, 0.5)
+            end = max(start[i] + ops[i]["ns"] + ops[i].get("lat", 0) for i in seq) + 1e-4 * sum(start)
+            if best is None or end <= best[0]:
+                best, pr = (end, seq, start), tr
+        FOUND[n] = best
+    return pre, post, FOUND[n][1], FOUND[n][2]
+
+
+def issue(ops, pre, post, tail, look):
+    n = len(ops)
+    left = [len(p) for p in pre]
+    ready = [0.0] * n
+    free = {}
+    pool = [i for i in range(n) if not left[i]]
+    seq, start = [], [0.0] * n
+    while pool:
+        when = min(max(ready[i], free.get(ops[i]["q"], 0)) for i in pool)
+        cand = [i for i in pool if max(ready[i], free.get(ops[i]["q"], 0)) <= when + 1]
+        q = ops[max(cand, key=lambda i: tail[i])]["q"]
+        i = max([k for k in cand if ops[k]["q"] == q], key=lambda k: tail[k])
+        soon = [k for k in pool if ops[k]["q"] == q and ready[k] < when + ops[i]["ns"] * look and tail[k] > tail[i] + ops[i]["ns"]]
+        if soon:
+            i = max(soon, key=lambda k: tail[k])
+        s = max(ready[i], free.get(q, 0))
+        start[i] = s
+        free[q] = s + ops[i]["ns"]
+        pool.remove(i)
+        seq.append(i)
+        for j in post[i]:
+            ready[j] = max(ready[j], s + ops[i]["ns"] + ops[i].get("lat", 0) + (HOP if pre[j][i] else -ops[i].get("lat", 0) * ("after" not in ops[j])))
+            left[j] -= 1
+            if not left[j]:
+                pool.append(j)
+    return seq, start
+
+
+def rank_program(g, core, T, topo):
+    if T.rank_of(core) is None:
+        return
+    ops = plan(T, g, core, topo)
+    pre, post, seq, start = order(ops)
+    queue = {"V": g.vector, "S": g.scalar, "P": g.tensor, "G": g, "Y": g.sync}
+    count = {"V": 0, "S": 0, "P": 0, "G": 0}
+    mark, known, clock = {}, {q: {} for q in queue}, {}
+    sent = 0
+    for j in seq:
+        o = ops[j]
+        q = o["q"]
+        if q == "R":
+            mark[j] = (o["sem"], o["inc"])
+            clock[j] = {o["sem"]: o["inc"]}
+            continue
+        need = {}
+        for i in pre[j]:
+            if pre[j][i]:
+                s, k = mark[i]
+                if known[q].get(s, 0) < k and need.get(s, (0, 0))[0] < k:
+                    need[s] = (k, i)
+        for s in sorted(need, key=lambda s: -start[need[s][1]]):
+            k, i = need[s]
+            if known[q].get(s, 0) < k:
+                queue[q].wait_ge(T.sem[s], k)
+                for s2, k2 in clock[i].items():
+                    known[q][s2] = max(known[q].get(s2, 0), k2)
+        if q == "G" and known[q].get(q, 0) < count[q]:
+            g.wait_ge(T.sem[q], count[q])
+            known[q][q] = count[q]
+        ins = o["fn"]()
+        clock[j] = dict(known[q])
+        if "sem" in o:
+            ins.then_inc(T.sem[o["sem"]], o["inc"])
+            mark[j] = (o["sem"], o["inc"])
+            clock[j][o["sem"]] = o["inc"]
+        elif "sent" in o:
+            sent += o["sent"]
+        elif q == "G" or any(pre[k][j] for k in post[j]):
+            count[q] += 1
+            ins.then_inc(T.sem[q], 1)
+            mark[j] = (q, count[q])
+            clock[j][q] = count[q]
+    for q in count:
+        if count[q]:
+            g.wait_ge(T.sem[q], count[q])
+    g.wait_ge(T.sem.sent, sent)
+    for o in ops:
+        if "sem" in o:
+            g.sync.wait_ge(T.sem[o["sem"]], o["inc"])

@@ -139,8 +139,15 @@ def plan(T, g, core, topo):
             kw["scale"] = ap(scale)
         if acc is not None:
             kw["accum_out"] = ap(acc)
-        add("S", lambda: g.scalar.activation(ap(out), src(a), f, **kw), parts(a, bias, scale), [out] + parts(acc),
-            100 + max(64, width(out) * (1.56 if a[0] == "ind" else 1)))
+        o = add("S", lambda: g.scalar.activation(ap(out), src(a), f, **kw), parts(a, bias, scale), [out] + parts(acc),
+                100 + max(64, width(out) * (1.56 if a[0] == "ind" else 1)))
+        if acc is None and (f == F.Identity or (f == F.Relu and scale is None)):
+            b = 0.0 if bias is None else bias
+            if f == F.Relu:
+                fn = lambda: g.vector.tensor_scalar(ap(out), src(a), ap(b), 0.0, A.add, A.max)
+            else:
+                fn = lambda: g.vector.tensor_scalar(ap(out), src(a), ap(1.0 if scale is None else scale), ap(b), A.mult, A.add)
+            o["alt"] = {"S": (o["fn"], o["ns"]), "V": (fn, vns(out, a))}
         return out
 
     def mm(out, pairs, first=True, last=True, slow=1):
@@ -195,6 +202,14 @@ def plan(T, g, core, topo):
 
     def f():
         return new("PF")
+
+    slot = [0]
+
+    def p(n=64):
+        if slot[0] + n > 512:
+            slot[0] = 0
+        slot[0] += n
+        return v("P4", slot[0] - n, slot[0])
 
     def c():
         r = ring["col"]
@@ -258,10 +273,13 @@ def plan(T, g, core, topo):
     fill(v("MT", 128 * 8, 128 * 12), 0.0)
     for m, r, w in ((MR, 2, 1.0), (MR, 3, -0.5), (MR, 5, 0.5), (MD, 2, -1 / MARK), (MD, 5, -1 / MARK)):
         act(sub(m, r, 128, 8), sub(ONES, r, 128, 8), F.Identity, scale=w)
-    fill(v("MT", MI[1] + 6, MI[2], 16, (0, 1, 1)), 1.0)
-    fill(v("MT", MI[1] + 14, MI[2], 16, (64, 65, 1)), 1.0)
+    iota(v("MT", MI[1] + 6, MI[2], 16, (0, 1, 1)), [[0, 8]], 1, 0)
+    iota(v("MT", MI[1] + 14, MI[2], 16, (64, 65, 1)), [[0, 8]], 1, 0)
     fill(v("MT", MJ[1], MJ[2], 8, (0, 1, 1)), 16.0)
     fill(v("MT", MJ[1] + 4, MJ[2], 8, (64, 65, 1)), 1.0)
+    ID8 = act(MD1, ID, F.Identity, scale=8.0)
+    MD2 = act(v("c8", 128, 256), MD, F.Identity, scale=MARK)
+    C80 = iota(v("c8", 0, 64), [[0, 64]], FL // 16, 0)
     p0, p16 = (0, 1, 1), (0, 16, 1)
     fill(v("WR", 0, 192, 1, p0), 0.0)
     AB, FG, DQ, QM, XL, XR, BR, BG, BD, XM, C1, BR1 = range(12)
@@ -282,15 +300,15 @@ def plan(T, g, core, topo):
     rep = iota(v("WO", 0, 128, 1, p16), [[0, 8], [1, 16]], 0, -1)
     rep = ts(v("WP", 0, 128, 1, p16), rep, 0.0, A.is_equal)
     for z in range(12):
-        mm(v("P4", z, z + 1, 1, p16), [(v("WR", 16 * z, 16 * z + 16, 1, p0), v("PB", ONE[1], ONE[1] + 1, 1, p0))])
-    act(v("WP", 128, 140, 1, p16), v("P4", 0, 12, 1, p16), F.Identity)
-    mm(bank(4, 16, 12), [(rep, v("WP", 128, 140, 1, p16))])
-    act(v("col", 16, 28), bank(4, 16, 12), F.Identity)
+        mm(v("P5", z, z + 1, 1, p16), [(v("WR", 16 * z, 16 * z + 16, 1, p0), v("PB", ONE[1], ONE[1] + 1, 1, p0))])
+    act(v("WP", 128, 140, 1, p16), v("P5", 0, 12, 1, p16), F.Identity)
+    mm(bank(5, 16, 12), [(rep, v("WP", 128, 140, 1, p16))])
+    act(v("col", 16, 28), bank(5, 16, 12), F.Identity)
     W = [v("col", 16 + z, 17 + z) for z in range(12)]
     ZM = [v("ZZ", 144 * z, 144 * z + 144) for z in range(7)]
     ZS = ts(ZM[6], Q, g15, A.is_equal)
     for z in range(6):
-        ts(ZM[z], ZS, W[z], A.mult)
+        act(ZM[z], ZS, F.Identity, scale=W[z])
     act(MX, ID, F.Identity)
     act(sub(MX, 3, 128, 8), sub(ONES, 3, 128, 8), F.Identity, scale=W[C1])
     act(sub(MX, 5, 128, 8), sub(ONES, 5, 128, 8), F.Identity, scale=W[C1])
@@ -299,10 +317,10 @@ def plan(T, g, core, topo):
     ts(SH, JW, psh, A.is_equal)
     OF = act(v("OF", 0, 128), ONES, F.Identity)
     act(v("KT", 4096, 5120), v("am", 0, 1024), F.Identity, scale=0.0, bias=0.5)
-    fill(v("Pc", 128, 136), 0.0)
+    iota(v("Pc", 128, 136), [[0, 8]], 0, 0)
     for t in range(3):
-        fill(v("CW%d" % t, DEAD, DEAD + 8), MARK)
-        fill(v("AW%d" % t, DEAD, DEAD + 8), 0.0)
+        iota(v("CW%d" % t, DEAD, DEAD + 8), [[0, 8]], int(MARK), 0)
+        iota(v("AW%d" % t, DEAD, DEAD + 8), [[0, 8]], 0, 0)
     mm(bank(6), [(MJ, v("IDT", 0, 512))])
     act(v("XT", 4096, 4608), bank(6), F.Identity, bias=W[BD])
     act(v("XT", 4608, 5120), bank(6), F.Identity, bias=W[BG])
@@ -321,8 +339,9 @@ def plan(T, g, core, topo):
     hx = cp(new("PU"), tt(f(), hf, d5, A.add))
     ts(v("dd", 0, 1024), v("am", 0, 1024), 0.0, A.is_equal, MARK, A.mult)
     for h in range(2):
-        act(bank(2 + h), wide("cr", h), F.Identity, scale=8.0)
-        tt(wide("Z0", h), bank(2 + h), wide("dd", h), A.add)
+        mm(bank(2 + h), [(ID8, wide("cr", h)), (ID, wide("dd", h))])
+        act(wide("sg", h), bank(2 + h), F.Sign, bias=2.0 ** -40)
+        act(wide("Z0", h), bank(2 + h), F.Identity)
     act(v("AW0", REST, REST + 1024), v("am", 0, 1024), F.Identity)
     wrap(bank(7, 0, 64), ZS, v("dd", 0, 1024))
     occ = ts(f(), bank(7, 0, 64), 16 * MARK - 1, A.is_lt)
@@ -335,13 +354,16 @@ def plan(T, g, core, topo):
         last = t == 2
         for h in range(2):
             act(wide("X", h), ind(v("XT", 0, 5120), half(hx, h)), F.Identity)
-            act(wide("sg", h), wide(zn, h), F.Sign, bias=2.0 ** -40)
             if t:
-                ts(wide("dd", h), wide(zn, h), THR, A.is_ge, MARK, A.mult)
+                act(wide("sg", h), wide(zn, h), F.Sign, bias=2.0 ** -40)
+                act(wide("dd", h), wide(zn, h), F.Sigmoid, scale=8.0, bias=-8 * THR)
+                o = ops[-1]
+                ts(wide("dd", h), wide(zn, h), THR, A.is_ge)
+                o["alt"] = {"S": (o["fn"], o["ns"]), "V": (ops[-1]["fn"], ops.pop()["ns"])}
         for h in range(2):
             mm(bank(h), [(MI, wide("IDT", h))], last=False)
             mm(bank(h), [(MR, wide("sg", h))], first=False, last=False)
-            mm(bank(h), [(MD, wide("dd", h))], first=False, last=False)
+            mm(bank(h), [(MD2 if t else MD, wide("dd", h))], first=False, last=False)
             mm(bank(h), [(MX, wide("X", h))], first=False)
             act(wide(RW, h, LT), bank(h), F.Relu, bias=W[BR])
         if t:
@@ -352,29 +374,24 @@ def plan(T, g, core, topo):
             send([(v(RW, EO, EO + 256), v(br, 0, 256))], eng[0:4], "rr%d" % t)
         fr = act(new("PB"), occ, F.Identity, scale=-1.0, bias=1.0)
         sc = scan(new("PB"), fr)
-        mm(bank(5, 0, 64), [(ONES, sc), (NBG, fr)])
+        js = mm(bank(5, 0, 64), [(ONES, C80), (NBG, fr), (ONES, sc)])
         mm(bank(5, 64, 1), [(ONES, sub(sc, 63, 64))])
-        jf = act(f(), bank(5, 0, 64), F.Identity, bias=-float(FL))
+        jf = act(f(), js, F.Identity, bias=-2.0 * FL)
         fc = act(c(), bank(5, 64, 1), F.Identity, bias=-float(B))
-        js = act(f(), bank(5, 0, 64), F.Identity, bias=float(FL))
+        base1 = tt(f(), js, lane1, A.min)
         more = []
         if t:
             cn = "cn%d" % t
             ca, cb, c1, d1 = [v(cn, k, k + 1) for k in range(4)]
             more = [(ID, act(new("PB"), sub(ONE, 0, 64), F.Identity, scale=float(B + FL), bias=cb))]
-            a1 = ts(f(), jf, ca, A.is_lt, c1, A.mult)
+            a1 = ts(p(), jf, ca, A.is_lt, c1, A.mult)
             a2 = ts(f(), jf, cb, A.is_lt, d1, A.mult)
-            vv = tt(f(), tt(f(), a1, a2, A.add), jf, A.add)
+            vv = tt(f(), tt(p(), a1, a2, A.add), jf, A.add)
             arr = ts(f(), jf, cb, A.is_lt)
             e2 = tt(f(), act(f(), vv, F.Identity, scale=4096.0, bias=(FL + B - DEAD) * 4096.0), arr, A.mult)
         else:
             cb, vv = -float(B + FL), jf
-        base1 = tt(f(), js, lane1, A.min)
         base2 = tt(f(), vv, tw, A.min)
-        wrap(bank(4, 0, 64), ZM[XL], v("X", 0, 1024))
-        wrap(bank(4, 64, 64), ZM[XR], v("X", 0, 1024))
-        xlr = cp(new("PU", 128), bank(4, 0, 128))
-        xl, xr = sub(xlr, 0, 64), sub(xlr, 64, 128)
         rec = v(RW, LT, LT + 1024)
         wrap(bank(7, 0, 64), ZM[AB], rec)
         dis = ts(new("PB"), bank(7, 0, 64), 2.0, A.is_ge)
@@ -383,7 +400,7 @@ def plan(T, g, core, topo):
         ndc = mm(bank(5, 0, 1), [(ONES, sub(sc, 63, 64))])
         off1 = ts(new("PU"), tt(f(), xq, base1, A.min), float(B), A.add)
         nsb = ts(f(), xq, fc, A.is_ge, 16384.0, A.mult)
-        bb = tt(f(), xq, nsb, A.add)
+        bb = tt(p(), xq, nsb, A.add)
         ns = act(f(), nsb, F.Identity, scale=1 / 16384.0)
         succ = act(f(), nsb, F.Identity, scale=-1 / 16384.0, bias=1.0)
         cnw = act(c(), ndc, F.Identity, bias=cb)
@@ -406,26 +423,29 @@ def plan(T, g, core, topo):
             lst = act(c(), bank(5, 128, 1), F.Identity, bias=512.0 + 2048, scale=0.5)
         lw = ts(f(), bank(7, 0, 64), 8192.0, A.is_ge, -0.5, A.add)
         tq = tt(f(), lw, bank(0, 0, 64), A.mult)
-        qw = tt(f(), bank(1, 0, 64), tq, A.add)
-        qo = tt(f(), bank(1, 0, 64), tq, A.subtract)
+        qw = tt(p(), bank(1, 0, 64), tq, A.add)
+        qo = tt(p(), bank(1, 0, 64), tq, A.subtract)
         newc = ts(f(), jf, cnw, A.is_lt)
-        ep = tt(f(), occ, qw, A.mult)
+        ep = tt(p() if t else f(), occ, qw, A.mult)
         sqo = tt(f(), succ, qo, A.mult)
-        pair = tt(f(), succ, newc, A.add)
+        pair = tt(p() if t else f(), succ, newc, A.add)
+        wrap(bank(6, 0, 64), ZM[XL], v("X", 0, 1024))
+        wrap(bank(6, 64, 64), ZM[XR], v("X", 0, 1024))
+        xlr = cp(new("PU", 128), bank(6, 0, 128))
+        xl, xr = sub(xlr, 0, 64), sub(xlr, 64, 128)
         if t:
             ep = tt(f(), ep, e2, A.add)
             pair = tt(f(), pair, arr, A.subtract)
         if not last:
             on0 = tt(f(), occ, newc, A.add)
-        for h in range(2):
-            tt(wide(CW, h, REST), ind(v("KT", 0, 5120), half(hx, h)), wide(zn, h), A.mult)
+        tt(v(CW, REST, REST + 1024), ind(v("KT", 0, 5120), hx), v(zn, 0, 1024), A.mult)
         act(v(CW, 0, 1024), v("sg", 0, 1024), F.Identity, bias=(MARK - e) / 2, scale=-(MARK + e) / 2)
         act(v(CW, RIGHT, RIGHT + 1024), v("sg", 0, 1024), F.Identity, bias=(MARK + e) / 2, scale=(MARK - e) / 2)
         for a in (0, RIGHT):
             dma("G", ap(v(CW, a, a + 1024)), ap(v(CW, REST, REST + 1024)), [v(CW, REST, REST + 1024)], [v(CW, a, a + 1024)], 4000)
+        act(v("SL", 0, 1024), ind(v("DT", 0, 4096), xl), F.Sigmoid)
+        act(v("SR", 0, 1024), ind(v("DT", 0, 4096), xr), F.Sigmoid)
         for h in range(2):
-            act(wide("SL", h), ind(v("DT", 0, 4096), half(xl, h)), F.Sigmoid)
-            act(wide("SR", h), ind(v("DT", 0, 4096), half(xr, h)), F.Sigmoid)
             mm(bank(2), [(ID, wide("sg", h))])
             tt(bank(3), wide(AW, h, REST), bank(2), A.mult)
             act(bank(2), bank(3), F.Identity, scale=-1.0)
@@ -440,22 +460,22 @@ def plan(T, g, core, topo):
         idi = cp(new("PI"), pf_)
         if t:
             key = ts(new("PI"), idi, 8191, A.bitwise_and)
-            old = tt(f(), ts(f(), key, lst, A.is_ge), npo, A.mult)
+            old = tt(p(), ts(p(), key, lst, A.is_ge), npo, A.mult)
             pair = tt(f(), pair, old, A.max)
         idn = ts(new("PI"), idi, 1023, A.bitwise_and)
         gt = tt(f(), idn, lane, A.is_gt)
         tq = tt(f(), lw, pd, A.mult)
-        qq = new("PF", 128)
-        qo = tt(f(), pr, tq, A.subtract)
-        qw = tt(f(), pr, tq, A.add)
-        tt(sub(qq, 0, 64), tt(f(), newc, qo, A.mult), ep, A.add)
-        tt(sub(qq, 64, 128), tt(f(), ns, qw, A.mult), sqo, A.add)
-        qi = cp(new("PI", 128), qq)
+        qi = new("PI", 128)
+        qo = tt(p(), pr, tq, A.subtract)
+        qw = tt(p(), pr, tq, A.add)
+        tt(sub(qi, 0, 64), tt(p(), newc, qo, A.mult), ep, A.add)
+        tt(sub(qi, 64, 128), tt(p(), ns, qw, A.mult), sqo, A.add)
         jj = ts(new("PI", 128), qi, 4, A.arith_shift_right, 255, A.bitwise_and)
         sr = ts(new("PI", 128), qi, 12, A.arith_shift_right)
         hi = ts(new("PI"), sub(qi, 0, 64), 4095, A.bitwise_and)
-        fuse = tt(f(), tt(f(), sub(jj, 0, 64), sub(jj, 64, 128), A.is_equal), pair, A.mult)
-        mk = new("PF", 128)
+        slot[0] = 0
+        fuse = tt(p(), tt(p(), sub(jj, 0, 64), sub(jj, 64, 128), A.is_equal), pair, A.mult)
+        mk = p(128)
         lo = tt(sub(mk, 64, 128), fuse, gt, A.mult)
         nup = tt(sub(mk, 0, 64), fuse, gt, A.is_le)
         s16 = ts(new("PU", 128), tt(new("PF", 128), sr, mk, A.mult), float(DEAD), A.add)
@@ -470,26 +490,27 @@ def plan(T, g, core, topo):
             h16 = cp(new("PU"), hi)
             for h in range(2):
                 act(wide("G2", h), ind(v(AW, 0, wn), half(sa, h)), F.Relu)
-                act(bank(4 + h), wide("Z", h), F.Sigmoid, bias=THR, scale=-1.0)
+                act(bank(h), wide("Z", h), F.Sigmoid, bias=THR, scale=-1.0)
             for h in range(2):
-                tt(wide("SL", h), wide("Z", h), bank(4 + h), A.mult)
+                tt(wide("SL", h), wide("Z", h), bank(h), A.mult)
                 dma("Y", T.yc[:, H[h][0]:H[h][1]], ap(wide("SL", h)), [wide("SL", h)], [], 2400)
                 tt(wide("G1", h), ind(v(AW, 0, wn), half(sb, h)), wide("G2", h), A.max)
                 tt(wide("SR", h), ind(v("KT", 0, 4096), half(h16, h)), wide("G1", h), A.mult)
                 dma("Y", T.ya[:, H[h][0]:H[h][1]], ap(wide("SR", h)), [wide("SR", h)], [], 2400)
             break
         d5 = ts(f(), hi, 3584.0, A.is_ge, 512.0, A.mult)
-        on = tt(f(), on0, nup, A.mult)
+        on = tt(p(), on0, nup, A.mult)
+        npair = tt(p(), pair, fuse, A.subtract)
         dr = tt(new("PB"), d5, on, A.mult)
         sc = scan(new("PB"), dr)
         y = mm(bank(6, 0, 64), [(NBG, dr), (ONES, sc)])
-        hd = tt(f(), hi, d5, A.add)
+        hd = tt(p(), hi, d5, A.add)
         l5 = ts(f(), y, 512.0 * (128 - B), A.is_lt, 512.0, A.mult)
         lv = act(f(), l5, F.Identity, scale=1 / 512.0)
         hx = cp(new("PU"), tt(f(), hd, l5, A.add))
         occ = tt(f(), on, lv, A.subtract)
-        npo = tt(f(), tt(f(), pair, fuse, A.subtract), occ, A.mult)
-        tw = tt(f(), tt(f(), npo, tt(f(), idn, lane, A.subtract), A.mult), lane2, A.add)
+        npo = tt(f(), npair, occ, A.mult)
+        tw = tt(f(), tt(p(), npo, tt(p(), idn, lane, A.subtract), A.mult), lane2, A.add)
         an1 = v(an[0], an[1], an[1] + 1024)
         act(an1, ind(v(AW, 0, wn), sa), F.Relu)
         act(v("G2", 0, 1024), ind(v(AW, 0, wn), sb), F.Relu)
@@ -500,14 +521,14 @@ def plan(T, g, core, topo):
         sc = scan(new("PB", 128), x2)
         e0, e1 = sub(sc, 63, 64), sub(sc, 127, 128)
         mm(bank(6, 128, 128), [(ONES, sc)])
-        mm(bank(4, 0, 1), [(ONES, e0)])
-        mm(bank(4, 1, 1), [(ONES, e0), (SO, e1), (NSO, e0)])
-        mm(bank(4, 2, 1), [(ONES, e0), (NSO, e0)])
+        mm(bank(7, 0, 1), [(ONES, e0)])
+        mm(bank(7, 1, 1), [(ONES, e0), (SO, e1), (NSO, e0)])
+        mm(bank(7, 2, 1), [(ONES, e0), (NSO, e0)])
         mm(bank(7, 128, 128), [(NUS, x2), (ONES, sc)])
         cs = "cs%d" % (t + 1)
-        act(v(cs, 0, 2), bank(4, 0, 2), F.Identity, bias=-float(B + FL))
-        act(v(cs, 2, 3), bank(4, 2, 1), F.Identity, bias=-128.0)
-        act(v(cs, 3, 4), bank(4, 2, 1), F.Identity, scale=-1.0, bias=EO + 128.0)
+        act(v(cs, 0, 2), bank(7, 0, 2), F.Identity, bias=-float(B + FL))
+        act(v(cs, 2, 3), bank(7, 2, 1), F.Identity, bias=-128.0)
+        act(v(cs, 3, 4), bank(7, 2, 1), F.Identity, scale=-1.0, bias=EO + 128.0)
         send([(v("cn%d" % (t + 1), 0, 4), v(cs, 0, 4))], eng[0:4], "rc%d" % (t + 1))
         act(v("Pc", 0, 128), bank(7, 128, 128), F.Identity)
         acc = new("PF", 8)
@@ -529,7 +550,7 @@ def plan(T, g, core, topo):
     return ops
 
 
-HOP, TRIES, FOUND = 80, 4000, {}
+HOP, TRIES, FOUND = 80, 12000, {}
 
 
 def meet(a, b):
@@ -558,7 +579,7 @@ def order(ops):
                 if i == j:
                     continue
                 same = ops[i]["q"] == o["q"] and "sem" not in ops[i]
-                if ps and not same:
+                if ps and (not same or "alt" in o or "alt" in ops[i]):
                     pre[j][i] = True
                 elif (w or wy) and meet(x, y):
                     pre[j][i] = pre[j].get(i, False) or not same or o["q"] != "P"
@@ -566,6 +587,19 @@ def order(ops):
                     pre[j][i] = pre[j].get(i, False)
         for x, w in [(x, False) for x in o["rd"]] + [(x, True) for x in o["wr"]]:
             seen.setdefault(x[0], []).append((j, x, w))
+    done = [0] * n
+    for j in range(n):
+        far = 0
+        for i in pre[j]:
+            if pre[j][i] and ops[i]["q"] != "R":
+                far |= done[i]
+        for i in list(pre[j]):
+            if far >> i & 1:
+                del pre[j][i]
+        done[j] = far
+        for i in pre[j]:
+            if pre[j][i]:
+                done[j] |= 1 << i
     post = [[] for _ in ops]
     for j in range(n):
         for i in pre[j]:
@@ -575,46 +609,84 @@ def order(ops):
         tail[i] = ops[i]["ns"] + ops[i].get("lat", 0) + max([tail[j] + HOP for j in post[i]] or [0])
     if n not in FOUND:
         rng = np.random.RandomState(7)
-        best, pr = None, list(tail)
+        best, pr = None, dict(enumerate(tail))
+        flex = [i for i in range(n) if "alt" in ops[i]]
+        top, lat = None, [o.get("lat", 0) for o in ops]
+        fore = [[(j, lat[i] + HOP if pre[j][i] else 0) for j in post[i]] for i in range(n)]
+        back = [[(i, lat[i] + HOP if pre[j][i] else 0) for i in pre[j]] for j in range(n)]
+
+        def flip(i):
+            ops[i]["q"] = "V" if ops[i]["q"] == "S" else "S"
+            ops[i]["fn"], ops[i]["ns"] = ops[i]["alt"][ops[i]["q"]]
         for k in range(TRIES):
-            tr = list(pr)
-            if k:
+            tr, fl = dict(pr), []
+            if k % 2:
                 a = int(rng.randint(n))
                 for i in rng.randint(max(0, a - 60), min(n, a + 60), int(rng.randint(1, 12))):
-                    tr[i] += float(rng.normal()) * (300, 1000, 3000)[k % 3]
-            seq, start = issue(ops, pre, post, tr, 0.5)
-            end = max(start[i] + ops[i]["ns"] + ops[i].get("lat", 0) for i in seq) + 1e-4 * sum(start)
-            if best is None or end <= best[0]:
+                    tr[int(i)] += float(rng.normal()) * (300, 1000, 3000)[k % 3]
+            elif k:
+                a = int(rng.randint(len(flex)))
+                fl = set(flex[int(i)] for i in rng.randint(max(0, a - 8), min(len(flex), a + 8), int(rng.randint(1, 4))))
+                for i in fl:
+                    flip(i)
+            if k % 4 == 1 and best:
+                seq, start = issue(ops, back, lat, {i: best[2][i] + ops[i]["ns"] + (tr[i] - pr[i]) for i in range(n)}, 0.3)
+                tr = {i: start[i] + ops[i]["ns"] for i in range(n)}
+            seq, start = issue(ops, fore, [0] * n, tr, 0.5)
+            end = max(start[i] + ops[i]["ns"] + lat[i] for i in seq) + 2e-4 * sum(start)
+            if best is None or end <= best[0] + 300.0 * (1 - k / TRIES) * float(rng.rand()) ** 2:
                 best, pr = (end, seq, start), tr
-        FOUND[n] = best
+                if top is None or end < top[0]:
+                    top = best + ([o["q"] for o in ops],)
+            else:
+                for i in fl:
+                    flip(i)
+        FOUND[n] = top
+    for o, q in zip(ops, FOUND[n][3]):
+        if "alt" in o:
+            o["q"] = q
+            o["fn"], o["ns"] = o["alt"][q]
     return pre, post, FOUND[n][1], FOUND[n][2]
 
 
-def issue(ops, pre, post, tail, look):
+def issue(ops, post, first, tail, look):
     n = len(ops)
-    left = [len(p) for p in pre]
-    ready = [0.0] * n
-    free = {}
-    pool = [i for i in range(n) if not left[i]]
+    left = [0] * n
+    for p in post:
+        for j, d in p:
+            left[j] += 1
+    ready = list(first)
+    qs, ns = [o["q"] for o in ops], [o["ns"] for o in ops]
+    free = {q: 0.0 for q in qs}
+    pool = {q: [] for q in free}
+    soonest = {q: 1e18 for q in free}
+    for i in range(n):
+        if not left[i]:
+            pool[qs[i]].append(i)
+            soonest[qs[i]] = min(soonest[qs[i]], ready[i])
     seq, start = [], [0.0] * n
-    while pool:
-        when = min(max(ready[i], free.get(ops[i]["q"], 0)) for i in pool)
-        cand = [i for i in pool if max(ready[i], free.get(ops[i]["q"], 0)) <= when + 1]
-        q = ops[max(cand, key=lambda i: tail[i])]["q"]
-        i = max([k for k in cand if ops[k]["q"] == q], key=lambda k: tail[k])
-        soon = [k for k in pool if ops[k]["q"] == q and ready[k] < when + ops[i]["ns"] * look and tail[k] > tail[i] + ops[i]["ns"]]
+    for _ in range(n):
+        when, q = min((max(soonest[q], free[q]), q) for q in free)
+        mine = pool[q]
+        i = max([k for k in mine if ready[k] <= when + 1], key=tail.get)
+        a, b = when + ns[i] * look, tail[i] + ns[i]
+        soon = [k for k in mine if ready[k] < a and tail[k] > b]
         if soon:
-            i = max(soon, key=lambda k: tail[k])
-        s = max(ready[i], free.get(q, 0))
+            i = max(soon, key=tail.get)
+        s = max(ready[i], free[q])
         start[i] = s
-        free[q] = s + ops[i]["ns"]
-        pool.remove(i)
+        e = free[q] = s + ns[i]
+        mine.remove(i)
+        soonest[q] = min([ready[k] for k in mine] or [1e18])
         seq.append(i)
-        for j in post[i]:
-            ready[j] = max(ready[j], s + ops[i]["ns"] + ops[i].get("lat", 0) + (HOP if pre[j][i] else -ops[i].get("lat", 0) * ("after" not in ops[j])))
+        for j, d in post[i]:
+            if e + d > ready[j]:
+                ready[j] = e + d
             left[j] -= 1
             if not left[j]:
-                pool.append(j)
+                pool[qs[j]].append(j)
+                if ready[j] < soonest[qs[j]]:
+                    soonest[qs[j]] = ready[j]
     return seq, start
 
 

@@ -2,42 +2,85 @@ import numpy as np
 from concourse.bass import DstId, RemoteDMATransfer
 from concourse.mybir import AluOpType as A, AxisListType, ActivationFunctionType as F
 
-NF, NI, NU, NB = 72, 24, 24, 24
+NF, NI, NU, NB = 100, 40, 40, 60
+B = 8191
+PAR, FREE, NONE, LANE, RN = 256, 1280, 2304, 2320, 3344
+ARR, LEFT, RIGHT, REST = 16, 1024, 2048, 3072
+MARK, THR = 1024.0, 32.0
 SCRATCH = {
-    "KT": ("sbuf", [128, 5120], "bfloat16"), "DT": ("sbuf", [128, 4096], "bfloat16"), "XT": ("sbuf", [128, 5120], "bfloat16"),
-    "am": ("sbuf", [128, 1024], "bfloat16"), "cr": ("sbuf", [128, 1024], "bfloat16"), "c8": ("sbuf", [128, 1024], "bfloat16"),
-    "Z0": ("sbuf", [128, 1024], "bfloat16"),
-    "cmp": ("sbuf", [128, 512], "int32"), "ci": ("sbuf", [128, 1024], "int32"), "cb": ("sbuf", [128, 1024], "bfloat16"),
+    "KT": ("sbuf", [128, 4624], "bfloat16"), "DT": ("sbuf", [128, 4608], "bfloat16"), "XT": ("sbuf", [128, 4608], "bfloat16"),
+    "cmp": ("sbuf", [128, 512], "int32"), "ci": ("sbuf", [128, 512], "float32"), "cb": ("sbuf", [128, 1024], "bfloat16"),
     "pl": ("sbuf", [128, 64], "int32"),
-    "CW0": ("sbuf", [128, 3088], "float32"), "CW1": ("sbuf", [128, 3584], "float32"), "CW2": ("sbuf", [128, 3584], "float32"),
-    "AW0": ("sbuf", [128, 3088], "float32"), "AW1": ("sbuf", [128, 3584], "float32"), "AW2": ("sbuf", [128, 3584], "float32"),
-    "RW0": ("sbuf", [128, 4608], "bfloat16"), "RW1": ("sbuf", [128, 4608], "bfloat16"), "RW2": ("sbuf", [128, 4608], "bfloat16"),
-    "Z": ("sbuf", [128, 1024], "float32"), "G1": ("sbuf", [128, 1024], "float32"), "G2": ("sbuf", [128, 1024], "float32"),
-    "SL": ("sbuf", [128, 1024], "float32"), "SR": ("sbuf", [128, 1024], "float32"),
-    "sg": ("sbuf", [128, 1024], "bfloat16"), "dd": ("sbuf", [128, 1024], "bfloat16"), "X": ("sbuf", [128, 1024], "bfloat16"),
-    "RG": ("sbuf", [128, 1024], "bfloat16"), "IDT": ("sbuf", [128, 1024], "bfloat16"),
-    "MT": ("sbuf", [128, 128 * 13], "bfloat16"), "ZZ": ("sbuf", [128, 144 * 7], "bfloat16"), "OF": ("sbuf", [128, 128], "float32"),
-    "Q": ("sbuf", [128, 144], "float32"), "QG": ("sbuf", [128, 128], "float32"),
-    "WR": ("sbuf", [128, 192], "bfloat16"), "WO": ("sbuf", [128, 128], "float32"), "WP": ("sbuf", [128, 144], "bfloat16"),
+    "AW1": ("sbuf", [128, 1296], "float32"), "AW2": ("sbuf", [128, 1296], "float32"), "AW3": ("sbuf", [128, 1040], "float32"),
+    "MT": ("sbuf", [128, 144 * 3 + 128 * 6], "bfloat16"), "ZZ": ("sbuf", [128, 144 * 11], "bfloat16"),
+    "Q": ("sbuf", [128, 160], "float32"), "QG": ("sbuf", [128, 144], "float32"), "SF": ("sbuf", [128, 128], "float32"),
+    "WR": ("sbuf", [128, 320], "bfloat16"), "OH": ("sbuf", [128, 144 + 256], "bfloat16"), "raw": ("sbuf", [128, 1024], "bfloat16"),
     "col": ("sbuf", [128, 96], "float32"), "coi": ("sbuf", [128, 8], "int32"),
-    "st": ("sbuf", [128, 64 * 4], "float32"), "Pc": ("sbuf", [128, 136], "float32"),
-    "cs1": ("sbuf", [128, 4], "float32"), "cs2": ("sbuf", [128, 4], "float32"),
-    "cn1": ("sbuf", [128, 4], "float32"), "cn2": ("sbuf", [128, 4], "float32"),
-    "bc1": ("sbuf", [128, 256], "float32"), "bc2": ("sbuf", [128, 256], "float32"),
-    "ba1": ("sbuf", [128, 256], "float32"), "ba2": ("sbuf", [128, 256], "float32"),
-    "br1": ("sbuf", [128, 256], "bfloat16"), "br2": ("sbuf", [128, 256], "bfloat16"),
+    "st": ("sbuf", [128, 64 * 4], "float32"), "Pc": ("sbuf", [128, 136], "float32"), "CB": ("sbuf", [128, 64 * 6], "bfloat16"),
+    "junk": ("sbuf", [128, 1024], "bfloat16"),
     "PF": ("sbuf", [128, 64 * NF], "float32"), "PI": ("sbuf", [128, 64 * NI], "int32"),
     "PU": ("sbuf", [128, 64 * NU], "uint16"), "PB": ("sbuf", [128, 64 * NB], "bfloat16"),
 }
+SPARE, STEP, LAT = [False, False, False], 18500, 0.8
+for _n in ("am", "cr", "Z0", "sg", "dd", "X", "W", "RG", "IDT", "DG", "MG"):
+    SCRATCH[_n] = ("sbuf", [128, 1024], "bfloat16")
+for _n in ("Z", "G1", "FP", "FM", "Y1", "Y2"):
+    SCRATCH[_n] = ("sbuf", [128, 1024], "float32")
+for _t in range(3):
+    SCRATCH["CW%d" % _t] = ("sbuf", [128, 4096], "float32")
+    SCRATCH["RW%d" % _t] = ("sbuf", [128, RN], "bfloat16")
+for _t in (1, 2):
+    SCRATCH["cs%d" % _t] = SCRATCH["cn%d" % _t] = ("sbuf", [128, 4], "float32")
+    SCRATCH["bc%d" % _t] = SCRATCH["ba%d" % _t] = ("sbuf", [128, 256], "float32")
+    SCRATCH["br%d" % _t] = ("sbuf", [128, 384], "bfloat16")
 for _b in range(8):
     SCRATCH["P%d" % _b] = ("psum", [128, 512], "float32")
-NDMA = 40
+NDMA = 44
 SEMAPHORES = ["V", "S", "P", "G", "sent"] + ["d%d" % _k for _k in range(NDMA)] + ["rc1", "rc2", "rr1", "rr2", "rd1", "rd2", "ra1", "ra2"]
 
-B = 8191
-FL, DUMP, EO, LT = 1280, 2304, 3328, 3584
-REST, DEAD, RIGHT = 1024, 2048, 2064
-MARK, THR = 1024.0, 32.0
+SC, BI, BX, S1, P6, AB, LW, DF, RT, DJ, QO, JN, TW, CP, GS, GB, PO = range(17)
+NW = 17
+K4, M4, ROUND = 4096, 1 << 22, 1.5 * 2 ** 27
+WEIGHTS = {
+    AB: {5: 1, 7: 1}, LW: {1: 1024},
+    DF: {0: 2 ** -10, 2: 2 ** -10, 4: -2 ** -10, 10: -2 ** -10, 1: -K4},
+    RT: {4: 1, 10: 1, 6: K4, 14: K4, 1: -M4, 3: 3 * M4},
+    DJ: {0: 1, 4: -1},
+    QO: {0: 1, 2: 1, 4: 1, 10: 1, 6: K4, 14: K4, 9: K4, 11: K4, 1: M4, 3: M4},
+    JN: {8: 1, 12: 1, 3: K4}, TW: {6: 1, 14: 1, 3: 16},
+    CP: {6: 1, 14: 1, 3: 7168, 1: -1024, 13: -1024},
+    SC: {4: 256, 8: 256, 10: 256, 1: 256, 0: -256, 12: -256, 2: -256, 5: 128, 7: -128, 15: None},
+    BI: {4: 128, 8: 128, 10: 128, 1: 128, 0: -128, 12: -128, 2: -128, 5: 1920, 7: 1920, 6: 128, 14: 128, 3: 128,
+         9: -128, 11: -128, 13: 128, 15: None},
+    BX: {0: 3584, 4: 3584, 8: 3584, 12: 3584, 3: 1, 6: 1, 14: 1, 5: None, 7: None, 9: None, 11: None, 15: None},
+    GS: {0: 1, 2: 1}, GB: {0: -3584}, PO: {9: 16}, S1: {6: 1, 14: 1}, P6: {6: 512},
+}
+
+
+def cover(w):
+    at = {NW * r + z: x for z in w for r, x in w[z].items()}
+    vals = sorted(set(at.values()) - {None}, key=lambda x: (-list(at.values()).count(x), x))
+    runs = []
+    for k, x in enumerate(vals):
+        need = {i for i in at if at[i] == x}
+        free = {i for i in at if at[i] is None or at[i] in vals[k:]}
+        while need:
+            best = (0,)
+            for a in sorted(need):
+                for d in range(1, 16 * NW):
+                    b, hit, last = a, 0, a
+                    while b in free:
+                        if b in need:
+                            hit, last = hit + 1, b
+                        b += d
+                    best = max(best, (hit, a - last, a, last, -d))
+            runs.append((best[2], best[3] + 1, -best[4], x))
+            need -= set(range(best[2], best[3] + 1, -best[4]))
+    return runs
+
+
+EARLY = 6
+RUNS = cover({z: WEIGHTS[z] for z in range(EARLY)}) + cover({z: WEIGHTS[z] for z in range(EARLY, NW)})
 
 
 def v(name, c0, c1, step=1, p=None):
@@ -53,7 +96,7 @@ def width(x):
 
 
 def plan(T, g, core, topo):
-    ops = []
+    ops, tag, when = [], [0], [0, "S"]
     rank = T.rank_of(core)
     nxt = T.cores[(rank + 1) % len(T.cores)]
     rid, pid = topo.addr(nxt)[0], topo.addr(nxt)[1]
@@ -93,10 +136,22 @@ def plan(T, g, core, topo):
         return SCRATCH[x[0]][0] == "psum"
 
     def add(q, fn, rd, wr, ns, **kw):
-        o = {"q": q, "fn": fn, "rd": rd, "wr": wr, "ns": ns}
+        o = {"q": q, "fn": fn, "rd": rd, "wr": wr, "ns": ns, "tag": tag[0], "when": when[0]}
+        when[0] += 10
         o.update(kw)
         ops.append(o)
         return o
+
+    def either():
+        b = ops.pop()
+        a = ops[-1]
+        a.setdefault("alt", {a["q"]: (a["fn"], a["ns"])})[b["q"]] = (b["fn"], b["ns"])
+        if b["q"] == when[1]:
+            a["q"], a["fn"], a["ns"] = b["q"], b["fn"], b["ns"]
+
+    def at(ns, q="S"):
+        when[0], when[1] = ns, q
+        tag[0] += 1
 
     def vns(out, a, b=None):
         if a[0] == "ind":
@@ -115,7 +170,7 @@ def plan(T, g, core, topo):
         return out
 
     def tt(out, a, b, op):
-        add("V", lambda: g.vector.tensor_tensor(ap(out), src(a), ap(b), op), parts(a, b), [out], vns(out, a, b))
+        add("V", lambda: g.vector.tensor_tensor(ap(out), src(a), ap(b), op), parts(a, b), [out], vns(out, a, b), ind=width(out) * (a[0] == "ind"))
         return out
 
     def cp(out, a):
@@ -139,32 +194,44 @@ def plan(T, g, core, topo):
             kw["scale"] = ap(scale)
         if acc is not None:
             kw["accum_out"] = ap(acc)
-        o = add("S", lambda: g.scalar.activation(ap(out), src(a), f, **kw), parts(a, bias, scale), [out] + parts(acc),
-                100 + max(64, width(out) * (1.56 if a[0] == "ind" else 1)))
-        if acc is None and (f == F.Identity or (f == F.Relu and scale is None)):
-            b = 0.0 if bias is None else bias
-            if f == F.Relu:
-                fn = lambda: g.vector.tensor_scalar(ap(out), src(a), ap(b), 0.0, A.add, A.max)
-            else:
-                fn = lambda: g.vector.tensor_scalar(ap(out), src(a), ap(1.0 if scale is None else scale), ap(b), A.mult, A.add)
-            o["alt"] = {"S": (o["fn"], o["ns"]), "V": (fn, vns(out, a))}
+        add("S", lambda: g.scalar.activation(ap(out), src(a), f, **kw), parts(a, bias, scale), [out] + parts(acc),
+            100 + max(64, width(out) * (1.56 if a[0] == "ind" else 1)), ind=width(out) * (a[0] == "ind"), sig=f == F.Sigmoid)
+        if f == F.Identity:
+            ts(out, a, 1.0 if scale is None else scale, A.mult, 0.0 if bias is None else bias, A.add)
+            either()
         return out
 
-    def mm(out, pairs, first=True, last=True, slow=1):
+    def step(out, a, up):
+        act(out, a, F.Sigmoid, scale=8.0 if up else -8.0, bias=-8 * THR if up else 8 * THR)
+        ts(out, a, THR, A.is_ge if up else A.is_lt)
+        either()
+        return out
+
+    def mm(out, pairs, slow=1):
         def fn():
             for k, (l, r) in enumerate(pairs):
-                i = g.tensor.matmul(ap(out), ap(l), ap(r), first and k == 0, last and k == len(pairs) - 1)
+                i = g.tensor.matmul(ap(out), ap(l), ap(r), k == 0, k == len(pairs) - 1)
             return i
-        add("P", fn, [x for pr in pairs for x in pr], [out], 30 + len(pairs) * max(64, width(out)) * slow)
+        add("P", fn, [x for pr in pairs for x in pr], [out], 30 + len(pairs) * (6 + max(64, width(out)) * slow))
         return out
 
-    def wrap(out, z, wide):
+    def wrap(out, z, wide, more=()):
         n = width(wide)
-        return mm(out, [(sub(z, 15 - i, 143 - i), sub(wide, i, n, 16)) for i in range(16)])
+        return mm(out, list(more) + [(sub(z, 15 - i, 143 - i), sub(wide, i, n, 16)) for i in range(16)])
 
     def iota(out, pat, base, cm):
         kw = {} if SCRATCH[out[0]][2] == "int32" else {"allow_small_or_imprecise_dtypes": True}
-        add("G", lambda: g.iota(ap(out), pat, base, cm, **kw), [], [out], 160 + 2 * width(out))
+        add("G", lambda: g.iota(ap(out), pat, base, cm, **kw), [], [out], 330 + 2 * width(out))
+        return out
+
+    def select(out, a, pat, op, other, base, cm):
+        add("G", lambda: g.affine_select(ap(out), ap(a), pat, op, other, base, cm), [a], [out], 380 + 2 * width(out))
+        return out
+
+    def const(out, c):
+        iota(out, [[0, width(out)]], int(c), 0)
+        fill(out, float(c))
+        either()
         return out
 
     nd = [0]
@@ -173,31 +240,19 @@ def plan(T, g, core, topo):
         k = nd[0]
         nd[0] += 1
         if q == "G":
-            return add(q, lambda: g.dma_start(out, a, accum_op=A.add), rd + wr, wr, 1000, sem="d%d" % k, inc=16, lat=lat)
+            return add(q, lambda: g.dma_start(out, a, accum_op=A.add), rd + wr, wr, 1100, sem="d%d" % k, inc=16, lat=lat * LAT)
         e = g.sync if q == "Y" else g.scalar
-        return add(q, lambda: e.dma_start(out, a), rd, wr, 60, sem="d%d" % k, inc=16, lat=lat)
+        return add(q, lambda: e.dma_start(out, a), rd, wr, 150, sem="d%d" % k, inc=16, lat=lat * LAT)
 
-    def send(pairs, es, rsem):
-        k = len(es) // len(pairs)
+    def send(d, s, es, rsem):
+        add("G", lambda: g.remote_dma(ap(d), ap(s), T.sem[rsem], T.sem.sent, pid, rid, bits(es)), [s], [], 600, sent=len(es))
+        add("R", None, [], [d], 0, sem=rsem, inc=len(es), lat=2200 * LAT, after=len(ops) - 1)
 
-        def fn():
-            if len(pairs) == 1:
-                return g.remote_dma(ap(pairs[0][0]), ap(pairs[0][1]), T.sem[rsem], T.sem.sent, pid, rid, bits(es))
-            return g.remote_dma_fused([RemoteDMATransfer(dst_ids=[DstId(rid=rid, pnc=pid)], dma_engine_mask=bits(es[j * k:j * k + k]),
-                                                         remote_sem=T.sem[rsem], src=ap(s), dst=ap(d))
-                                       for j, (d, s) in enumerate(pairs)], local_sem=T.sem.sent)
-        o = add("G", fn, [s for d, s in pairs], [], 500, sent=len(es))
-        add("R", None, [], [d for d, s in pairs], 0, sem=rsem, inc=len(es), lat=2200, after=o)
-
-    ring = {"PF": [0, NF], "PI": [0, NI], "PU": [0, NU], "PB": [0, NB], "col": [32, 96]}
+    ring = {"PF": 0, "PI": 0, "PU": 0, "PB": 0, "col": 40}
 
     def new(pool, n=64):
-        r = ring[pool]
-        k = (n + 63) // 64
-        if r[0] + k > r[1]:
-            r[0] = 0
-        x = v(pool, 64 * r[0], 64 * r[0] + n)
-        r[0] += k
+        x = v(pool, 64 * ring[pool], 64 * ring[pool] + n)
+        ring[pool] += (n + 63) // 64
         return x
 
     def f():
@@ -212,14 +267,16 @@ def plan(T, g, core, topo):
         return v("P4", slot[0] - n, slot[0])
 
     def c():
-        r = ring["col"]
-        r[0] += 1
-        return v("col", r[0] - 1, r[0])
+        ring["col"] += 1
+        return v("col", ring["col"] - 1, ring["col"])
 
     H = [(0, 512), (512, 1024)]
 
     def wide(name, h, base=0):
         return v(name, base + H[h][0], base + H[h][1])
+
+    def full(name, base=0):
+        return v(name, base, base + 1024)
 
     def half(off, h):
         return sub(off, 32 * h, 32 * h + 32)
@@ -229,334 +286,368 @@ def plan(T, g, core, topo):
 
     dma("Y", T.cmp[:, 0:256], T.lf[:, :], [], [v("cmp", 0, 256)], 2300)
     dma("Y", T.cmp[:, 256:512], T.rt[:, :], [], [v("cmp", 256, 512)], 2300)
-    dma("S", T.am[:, :], T.amp[:, :], [], [v("am", 0, 1024)], 2500)
-    dma("S", T.cr[:, :], T.cro[:, :], [], [v("cr", 0, 1024)], 2600)
+    dma("S", T.am[:, :], T.amp[:, :], [], [full("am")], 2500)
+    dma("S", T.cr[:, :], T.cro[:, :], [], [full("cr")], 2600)
     for b in range(2):
         for u in range(2):
             a = 32 * b + 16 * u
             dma("Y", T.pl[:, a:a + 16], T.place[u::2, 512 * b:512 * b + 512], [], [v("pl", a, a + 16)], 2400)
     dma("S", T.KT[:, 0:4096], T.kap[:, :], [], [v("KT", 0, 4096)], 4300)
-    dma("S", T.DT[:, :], T.dam[:, :], [], [v("DT", 0, 4096)], 5800)
+    dma("S", T.DT[:, 0:4096], T.dam[:, :], [], [v("DT", 0, 4096)], 5800)
 
-    fill(v("XT", 0, 4096), 0.0)
-    pi, pl16, pg = v("coi", 0, 1), v("coi", 1, 2), v("coi", 2, 3)
-    pcol, icol, g16, g15, gsh, psh = [v("col", k, k + 1) for k in range(6)]
-    iota(pi, [[0, 1]], 0, 1)
-    Q, QG = iota(v("Q", 0, 144), [[1, 144]], 0, 0), iota(v("QG", 0, 128), [[16, 8], [0, 16]], 0, 0)
-    JW = v("Q", 0, 128)
-    iota(v("IDT", 0, 512, 1, (0, 64, 1)), [[1, 32], [0, 16]], 0, 0)
-    iota(v("IDT", 0, 512, 1, (64, 128, 1)), [[0, 32], [1, 16]], 0, 0)
-    ts(pl16, pi, 15, A.bitwise_and)
-    cp(pcol, pi)
-    act(v("IDT", 512, 1024), v("IDT", 0, 512), F.Identity, bias=ts(v("col", 7, 8), pcol, 64.0, A.is_lt, 32.0, A.mult))
-    cp(icol, pl16)
-    ts(g16, pcol, icol, A.subtract)
-    ts(g15, g16, 15.0, A.add)
-    wrapc = ts(v("col", 6, 7), pcol, 112.0, A.is_ge, -128.0, A.mult)
-    ts(gsh, g16, wrapc, A.add, 16.0, A.add)
-    ts(psh, pcol, wrapc, A.add, 16.0, A.add)
-    l16 = iota(v("st", 192, 256), [[16, 64]], 0, 0)
-    lane = ts(v("st", 0, 64), l16, icol, A.add)
-    lane1 = act(v("st", 64, 128), lane, F.Identity, bias=float(DUMP - B))
-    lane2 = act(v("st", 128, 192), lane, F.Identity, bias=float(LT - FL - B))
-    jb = act(v("col", 8, 16), sub(lane, 0, 8), F.Identity, bias=0.5)
-    M = [v("MT", 128 * k, 128 * k + 128) for k in range(13)]
-    ONES, ID, NUS, NBG, SO, SH, MX, NSO, MR, MD, MI, MJ, MD1 = M
-    ONE = fill(v("PB", 64 * (NB - 2), 64 * NB), 1.0)
-    ring["PB"][1] = NB - 2
-    ts(ONES, QG, g16, A.is_equal)
-    ts(ID, JW, pcol, A.is_equal)
-    t0 = ts(new("PB", 128), JW, pcol, A.is_lt, -1.0, A.mult)
-    tt(NUS, t0, ONES, A.mult)
-    t1 = act(new("PB", 128), ID, F.Identity, scale=-(B + 1.0))
-    tt(NBG, t1, NUS, A.add)
-    fill(v("MT", 128 * 8, 128 * 12), 0.0)
-    for m, r, w in ((MR, 2, 1.0), (MR, 3, -0.5), (MR, 5, 0.5), (MD, 2, -1 / MARK), (MD, 5, -1 / MARK)):
-        act(sub(m, r, 128, 8), sub(ONES, r, 128, 8), F.Identity, scale=w)
-    iota(v("MT", MI[1] + 6, MI[2], 16, (0, 1, 1)), [[0, 8]], 1, 0)
-    iota(v("MT", MI[1] + 14, MI[2], 16, (64, 65, 1)), [[0, 8]], 1, 0)
-    fill(v("MT", MJ[1], MJ[2], 8, (0, 1, 1)), 16.0)
-    fill(v("MT", MJ[1] + 4, MJ[2], 8, (64, 65, 1)), 1.0)
-    ID8 = act(MD1, ID, F.Identity, scale=8.0)
-    MD2 = act(v("c8", 128, 256), MD, F.Identity, scale=MARK)
-    C80 = iota(v("c8", 0, 64), [[0, 64]], FL // 16, 0)
-    p0, p16 = (0, 1, 1), (0, 16, 1)
-    fill(v("WR", 0, 192, 1, p0), 0.0)
-    AB, FG, DQ, QM, XL, XR, BR, BG, BD, XM, C1, BR1 = range(12)
-    for z, r0, r1, w0, w1 in ((BR, 3, 11, 8, 7), (BR, 5, 13, 8, 7), (AB, 3, 11, 1, -1), (AB, 5, 13, 1, -1),
-                              (FG, 6, 14, 16, 1), (FG, 3, 11, -2048, 2048), (FG, 5, 13, -2048, 2048), (FG, 2, 10, 8192, -8192),
-                              (FG, 7, 9, 2048, 6144)):
-        iota(v("WR", 16 * z + r0, 16 * z + r1 + 1, r1 - r0, p0), [[w1 - w0, 2]], w0, 0)
-    for k, (z, r0, r1, d, w) in enumerate((
-            (BG, 1, 8, 6, 1), (BD, 0, 9, 8, 3584), (XL, 0, 5, 4, 1), (XR, 8, 13, 4, 1), (BR, 2, 10, 7, 1), (DQ, 0, 5, 4, 1),
-            (DQ, 8, 13, 4, -1), (QM, 0, 13, 4, 0.5), (XM, 0, 13, 4, 1), (BD, 1, 2, 1, 1), (C1, 1, 2, 1, -100),
-            (DQ, 1, 2, 1, RIGHT * 4096), (DQ, 9, 10, 1, -RIGHT * 4096), (QM, 6, 7, 1, 65536), (QM, 14, 15, 1, 4096),
-            (QM, 9, 10, 1, (RIGHT // 2 - DEAD) * 4096), (QM, 1, 2, 1, (REST - RIGHT // 2) * 4096))):
-        x = v("WR", 16 * z + r0, 16 * z + r1, d, p0)
-        if k % 4 == 3:
-            fill(x, float(w))
+    at(300)
+    fill(v("XT", 0, 4096), 1.0)
+    p0 = (0, 1, 1)
+    at(200)
+    fill(v("WR", 0, 16 * NW, 1, p0), 0.0)
+    for k, (a, b, d, w) in enumerate(RUNS):
+        x = v("WR", a, b, d, p0)
+        at(1000 if a % NW < EARLY else 8000 + 100 * k, "SG"[a % NW >= EARLY])
+        act(x, x, F.Identity, scale=0.0, bias=float(w))
+        if w == int(w):
+            iota(x, [[0, width(x)]], int(w), 0)
+            either()
+    at(100)
+    fill(v("OH", 0, 400, 1, p0), 0.0)
+    for a, b, d in ((15, 144, 16), (144, 272, 4), (150, 272, 16), (274, 400, 8), (286, 400, 16)):
+        if a == 15:
+            act(v("OH", a, b, d, p0), v("OH", a, b, d, p0), F.Sigmoid, bias=128.0)
+            ops[-1]["ns"] += 1500
         else:
-            act(x, x, F.Identity, bias=float(w))
-    rep = iota(v("WO", 0, 128, 1, p16), [[0, 8], [1, 16]], 0, -1)
-    rep = ts(v("WP", 0, 128, 1, p16), rep, 0.0, A.is_equal)
-    for z in range(12):
-        mm(v("P5", z, z + 1, 1, p16), [(v("WR", 16 * z, 16 * z + 16, 1, p0), v("PB", ONE[1], ONE[1] + 1, 1, p0))])
-    act(v("WP", 128, 140, 1, p16), v("P5", 0, 12, 1, p16), F.Identity)
-    mm(bank(5, 16, 12), [(rep, v("WP", 128, 140, 1, p16))])
-    act(v("col", 16, 28), bank(5, 16, 12), F.Identity)
-    W = [v("col", 16 + z, 17 + z) for z in range(12)]
-    ZM = [v("ZZ", 144 * z, 144 * z + 144) for z in range(7)]
-    ZS = ts(ZM[6], Q, g15, A.is_equal)
-    for z in range(6):
-        act(ZM[z], ZS, F.Identity, scale=W[z])
-    act(MX, ID, F.Identity)
-    act(sub(MX, 3, 128, 8), sub(ONES, 3, 128, 8), F.Identity, scale=W[C1])
-    act(sub(MX, 5, 128, 8), sub(ONES, 5, 128, 8), F.Identity, scale=W[C1])
-    ts(SO, QG, gsh, A.is_equal)
-    act(NSO, SO, F.Identity, scale=-1.0)
-    ts(SH, JW, psh, A.is_equal)
-    OF = act(v("OF", 0, 128), ONES, F.Identity)
-    act(v("KT", 4096, 5120), v("am", 0, 1024), F.Identity, scale=0.0, bias=0.5)
-    iota(v("Pc", 128, 136), [[0, 8]], 0, 0)
+            act(v("OH", a, b, d, p0), v("OH", a, b, d, p0), F.Identity, bias=1.0)
+    row = [v("OH", 15 - r, 143 - r, 1, p0) for r in range(16)]
+    rows_hi, rows_lo = v("OH", 144, 272, 1, p0), v("OH", 272, 400, 1, p0)
+    for a, b in ((0, EARLY), (EARLY, NW)):
+        at(11500 if a else 3500)
+        mm(bank(5, a, b - a), [(row[r], v("WR", NW * r + a, NW * r + b, 1, p0)) for r in range(16)])
+        act(v("col", 16 + a, 16 + b), bank(5, a, b - a), F.Identity)
+    Wt = [v("col", 16 + z, 17 + z) for z in range(NW)]
+    pcol, icol, g16, g15, B1, B2 = [v("col", k, k + 1) for k in range(6)]
+    at(4700)
+    act(B1, Wt[S1], F.Identity, scale=-1.0, bias=1.0)
+    act(B2, Wt[P6], F.Identity, bias=B1)
+    at(0)
+    hi0 = iota(v("raw", 0, 512, 1, p0), [[16, 32], [0, 16]], 0, 0)
+    lo0 = iota(v("raw", 512, 1024, 1, p0), [[0, 32], [1, 16]], 0, 0)
+    at(2400)
+    iota(pcol, [[0, 1]], 0, 1)
+    iota(v("Q", 0, 16), [[1, 16]], 112, 0)
+    Q, JW = iota(v("Q", 16, 160), [[1, 144]], 0, 0), v("Q", 16, 144)
+    at(4200, "V")
+    cp(icol, ts(v("coi", 1, 2), iota(v("coi", 0, 1), [[0, 1]], 0, 1), 15, A.bitwise_and))
+    act(g16, icol, F.Identity, scale=-1.0, bias=pcol)
+    act(g15, g16, F.Identity, bias=15.0)
+    const(v("QG", 0, 16), 112)
+    iota(v("QG", 16, 144), [[16, 8], [0, 16]], 0, 0)
+    at(7000)
+    l16 = iota(v("st", 192, 256), [[16, 64]], 16, 0)
+    lane16 = act(v("st", 0, 64), l16, F.Identity, bias=icol)
+    lane1 = act(v("st", 64, 128), lane16, F.Identity, bias=float(LANE - PAR - 16 - B))
+    at(13000)
+    jb = act(v("col", 8, 16), sub(lane16, 0, 8), F.Identity, bias=-15.5)
+    ones, ident, nones = [v("MT", 144 * k, 144 * k + 144) for k in range(3)]
+    NUS, NBG, MD, NID, IDB, ID4 = [v("MT", 432 + 128 * k, 560 + 128 * k) for k in range(6)]
+    ONES, SO, ID, SH, NON, NSO = [sub(m, a, a + 128) for m in (ones, ident, nones) for a in (16, 0)]
+    at(7500)
+    ONE, C64 = const(v("CB", 0, 128), 1), const(v("CB", 128, 192), 64)
+    at(13000)
+    CM, K7, K1 = const(v("CB", 192, 256), -20480), const(v("CB", 256, 257), 32 * (B - 1023)), const(v("CB", 258, 259), 4096)
+    at(3400, "V")
+    ts(ident, v("Q", 0, 144), pcol, A.is_equal)
+    act(NID, ID, F.Identity, scale=-1.0)
+    act(IDB, ID, F.Identity, scale=-2.0 ** 25)
+    at(4400, "V")
+    ts(ones, v("QG", 0, 144), g16, A.is_equal)
+    act(nones, ones, F.Identity, scale=-1.0)
+    select(MD, NON, [[0, 8], [1, 16]], A.not_equal, 0.0, -7, 0)
+    act(sub(MD, 5, 128, 16), sub(ONES, 5, 128, 16), F.Identity, scale=-2.0)
+    at(6000, "V")
+    select(NUS, NON, [[-1, 128]], A.is_gt, 0.0, 0, 1)
+    select(NBG, NUS, [[-1, 128]], A.not_equal, -(B + 1.0), 0, 1)
+    ZS = ts(v("ZZ", 0, 144), Q, g15, A.is_equal)
+    ZM = {}
+    for z in range(AB, CP + 1):
+        ZM[z] = act(v("ZZ", 144 * (z - AB + 1), 144 * (z - AB + 2)), ZS, F.Identity, scale=Wt[z])
+        at(12600 + 10 * z)
+    act(ID4, ID, F.Identity, scale=1008 / 4096.0)
+    lane1k = act(v("st", 128, 192), lane16, F.Identity, bias=LEFT - 16.0)
+    SF = act(v("SF", 0, 128), SH, F.Identity)
+    at(6500)
+    fill(v("KT", 4096, 4608), 0.5)
+    at(16500)
+    fill(v("DT", 4096, 4608), 64.0)
+    const(v("Pc", 128, 136), 0)
     for t in range(3):
-        iota(v("CW%d" % t, DEAD, DEAD + 8), [[0, 8]], int(MARK), 0)
-        iota(v("AW%d" % t, DEAD, DEAD + 8), [[0, 8]], 0, 0)
-    mm(bank(6), [(MJ, v("IDT", 0, 512))])
-    act(v("XT", 4096, 4608), bank(6), F.Identity, bias=W[BD])
-    act(v("XT", 4608, 5120), bank(6), F.Identity, bias=W[BG])
-    ts(v("cb", 0, 512), v("cmp", 0, 512), -8.0, A.add, 0.0, A.max)
-    for k, r in ((0, 0), (1, 8)):
-        dma("Y", T.XT[r::16, 0:4096], T.cb[:, 256 * k:256 * k + 256], [v("cb", 256 * k, 256 * k + 256)], [v("XT", 0, 4096, 1, (r, 128, 16))], 2600)
-    tt(v("cb", 512, 1024), v("cmp", 0, 512), v("cb", 0, 512), A.subtract)
-    for k, r in ((2, 4), (3, 12)):
-        dma("Y", T.XT[r::16, 0:4096], T.cb[:, 256 * k:256 * k + 256], [v("cb", 256 * k, 256 * k + 256)], [v("XT", 0, 4096, 1, (r, 128, 16))], 2600)
-    iota(v("RW0", 0, FL), [[0, FL]], 0, 0)
+        const(v("CW%d" % t, 0, 8), MARK)
+        const(v("AW%d" % (t + 1), 0, 8), 0)
+    at(2500)
+    mm(bank(6), [(rows_hi, hi0), (rows_lo, lo0)])
+    at(4800)
+    act(wide("IDT", 0), bank(6), F.Identity, scale=Wt[S1], bias=B1)
+    act(wide("IDT", 1), bank(6), F.Identity, scale=Wt[S1], bias=B2)
+    act(v("XT", 4096, 4608), bank(6), F.Identity, scale=B1, bias=Wt[BX])
+    at(2600)
+    act(wide("cb", 0), ts(v("ci", 0, 512), v("cmp", 0, 512), -7.5, A.add, ROUND, A.add), F.Identity, bias=-ROUND)
+    for k, rows in enumerate(((0, 8, 4, 12), (2, 10))):
+        if k:
+            at(3900)
+            tt(wide("cb", 1), v("cmp", 0, 512), wide("cb", 0), A.subtract)
+        for j, r in enumerate(rows):
+            a = 512 * k + 256 * (2 * j // len(rows))
+            dma("Y", T.XT[r::16, 0:4096], T.cb[:, a:a + 256], [v("cb", a, a + 256)], [v("XT", 0, 4096, 1, (r, 128, 16))], 2600)
+    at(7800)
+    const(v("RW0", PAR, FREE), 0)
+    const(v("RW0", NONE, LANE), 0)
 
+    at(6200)
     pf = cp(f(), v("pl", 0, 64))
     hf = f()
     add("V", lambda: g.vector.transpose(ap(hf), ap(pf)), [pf], [hf], 124)
-    d5 = ts(f(), hf, 3584.0, A.is_ge, 512.0, A.mult)
-    hx = cp(new("PU"), tt(f(), hf, d5, A.add))
-    ts(v("dd", 0, 1024), v("am", 0, 1024), 0.0, A.is_equal, MARK, A.mult)
+    dr = ts(new("PB"), hf, 3584.0, A.is_ge, 512.0, A.mult)
+    hx = cp(new("PU"), tt(f(), hf, dr, A.add))
+    at(3200)
+    ts(full("dd"), full("am"), 0.0, A.is_equal)
     for h in range(2):
-        mm(bank(2 + h), [(ID8, wide("cr", h)), (ID, wide("dd", h))])
-        act(wide("sg", h), bank(2 + h), F.Sign, bias=2.0 ** -40)
-        act(wide("Z0", h), bank(2 + h), F.Identity)
-    act(v("AW0", REST, REST + 1024), v("am", 0, 1024), F.Identity)
-    wrap(bank(7, 0, 64), ZS, v("dd", 0, 1024))
-    occ = ts(f(), bank(7, 0, 64), 16 * MARK - 1, A.is_lt)
-    tw, npo = lane2, None
+        at(4600 + 1100 * h)
+        mm(bank(2 + h), [(NID, wide("cr", h)), (IDB, wide("dd", h))])
+        act(wide("sg", h), bank(2 + h), F.Sign, scale=-1.0, bias=2.0 ** -40)
+        at(6900 + 100 * h, "V")
+        act(wide("Z0", h), bank(2 + h), F.Identity, scale=-8.0)
+    tw = lv = lvl = fr = None
 
     for t in range(3):
-        CW, AW, RW = "CW%d" % t, "AW%d" % t, "RW%d" % t
+        CW, RW = "CW%d" % t, "RW%d" % t
         zn = "Z0" if t == 0 else "Z"
+        aw = full("am") if t == 0 else v("AW%d" % t, 0, 1296)
         e = float(4 >> t)
         last = t == 2
-        for h in range(2):
-            act(wide("X", h), ind(v("XT", 0, 5120), half(hx, h)), F.Identity)
-            if t:
-                act(wide("sg", h), wide(zn, h), F.Sign, bias=2.0 ** -40)
-                act(wide("dd", h), wide(zn, h), F.Sigmoid, scale=8.0, bias=-8 * THR)
-                o = ops[-1]
-                ts(wide("dd", h), wide(zn, h), THR, A.is_ge)
-                o["alt"] = {"S": (o["fn"], o["ns"]), "V": (ops[-1]["fn"], ops.pop()["ns"])}
-        for h in range(2):
-            mm(bank(h), [(MI, wide("IDT", h))], last=False)
-            mm(bank(h), [(MR, wide("sg", h))], first=False, last=False)
-            mm(bank(h), [(MD2 if t else MD, wide("dd", h))], first=False, last=False)
-            mm(bank(h), [(MX, wide("X", h))], first=False)
-            act(wide(RW, h, LT), bank(h), F.Relu, bias=W[BR])
+        r0, r1 = STEP * t - 2500, STEP * t + STEP - 2500
         if t:
-            br = "br%d" % t
-            act(v(br, 0, 128), ind(v("X", 0, 1024), lvl), F.Identity, scale=W[XM])
-            mm(bank(7, 0, 128), [(SH, v(br, 0, 128))])
-            act(v(br, 128, 256), bank(7, 0, 128), F.Identity)
-            send([(v(RW, EO, EO + 256), v(br, 0, 256))], eng[0:4], "rr%d" % t)
-        fr = act(new("PB"), occ, F.Identity, scale=-1.0, bias=1.0)
+            at(r0 + 4700)
+            act(full("X"), ind(v("XT", 0, 4608), hx), F.Identity)
+            lanes = v("X", 0, 1024, 1, (6, 128, 8))
+            dma("Y", ap(lanes), T.IDT[6::8, :], [full("IDT")], [lanes], 2200)
+            for h in range(2):
+                at(r0 + 6500 + 1000 * h)
+                act(wide("sg", h), wide(zn, h), F.Sign, bias=2.0 ** -40)
+                step(wide("dd", h), wide(zn, h), True)
+        else:
+            at(8700)
+            for h in range(2):
+                tt(wide("X", h), ind(v("XT", 0, 4608), half(hx, h)), wide("IDT", h), A.mult)
+        for h in range(2):
+            at(r0 + 8800 + 500 * h)
+            mm(bank(h), [(ONES, wide("sg", h)), (MD, wide("dd", h))])
+            act(wide("W", h), bank(h), F.Sigmoid, scale=Wt[SC], bias=Wt[BI])
+        at(r0 + 10000)
+        if t:
+            ab = wrap(bank(7, 0, 64), ZM[AB], full("W"), [(NID, dr), (NID, fr)])
+        else:
+            ab = wrap(bank(7, 0, 64), ZM[AB], full("W"))
+            at(r0 + 13000)
+            fr = ts(new("PB"), ab, 0.5, A.is_lt)
+        at(r0 + (9300 if t else 13100))
+        occ = act(new("PB"), fr, F.Identity, scale=-1.0, bias=1.0)
         sc = scan(new("PB"), fr)
-        js = mm(bank(5, 0, 64), [(ONES, C80), (NBG, fr), (ONES, sc)])
-        mm(bank(5, 64, 1), [(ONES, sub(sc, 63, 64))])
-        jf = act(f(), js, F.Identity, bias=-2.0 * FL)
-        fc = act(c(), bank(5, 64, 1), F.Identity, bias=-float(B))
+        js = mm(bank(5, 0, 64), [(ONES, C64), (NBG, fr), (ONES, sc)])
+        fc = act(c(), mm(bank(5, 64, 1), [(ONES, sub(sc, 63, 64))]), F.Identity, bias=-float(B))
         base1 = tt(f(), js, lane1, A.min)
         more = []
         if t:
-            cn = "cn%d" % t
-            ca, cb, c1, d1 = [v(cn, k, k + 1) for k in range(4)]
-            more = [(ID, act(new("PB"), sub(ONE, 0, 64), F.Identity, scale=float(B + FL), bias=cb))]
-            a1 = ts(p(), jf, ca, A.is_lt, c1, A.mult)
-            a2 = ts(f(), jf, cb, A.is_lt, d1, A.mult)
-            vv = tt(f(), tt(p(), a1, a2, A.add), jf, A.add)
-            arr = ts(f(), jf, cb, A.is_lt)
-            e2 = tt(f(), act(f(), vv, F.Identity, scale=4096.0, bias=(FL + B - DEAD) * 4096.0), arr, A.mult)
+            at(r0 + 10200)
+            ca, cb, c1, d1 = [v("cn%d" % t, k, k + 1) for k in range(4)]
+            more = [(ID, act(new("PB"), sub(ONE, 0, 64), F.Identity, scale=B - 1023.0, bias=cb))]
+            a1 = ts(new("PB"), js, ca, A.is_le, c1, A.mult)
+            a2 = ts(new("PB"), js, cb, A.is_le, d1, A.mult)
+            a4 = ts(new("PB"), js, cb, A.is_le, 4096.0, A.mult)
+            base2 = tt(f(), mm(bank(5, 128, 64), [(NON, C64), (NBG, fr), (ONES, sc), (ID, a1), (NID, a2)]), tw, A.min)
+            mm(bank(5, 256, 64), [(ID, dr), (ID, lv), (ID, a4)])
+            mm(bank(5, 320, 64), [(ONES, sub(ONE, 0, 64)), (ID4, a4)])
+            delta = bank(5, 256, 128)
+            br = "br%d" % t
+            at(r0 + 13200)
+            gl = act(v(br, 256, 384), ind(full("X"), lvl), F.Identity, scale=Wt[GS], bias=Wt[GB])
+            for k, m in enumerate((ID, SH)):
+                mm(bank(6, 128 * k, 128), [(row[9], sub(hi0, 128 * k, 128 * k + 128)), (row[11], sub(lo0, 0, 128)), (m, gl)])
+            act(v(br, 0, 256), bank(6, 0, 256), F.Identity, bias=Wt[PO])
+            send(v(RW, 0, PAR), v(br, 0, 256), eng[0:4], "rr%d" % t)
         else:
-            cb, vv = -float(B + FL), jf
-        base2 = tt(f(), vv, tw, A.min)
-        rec = v(RW, LT, LT + 1024)
-        wrap(bank(7, 0, 64), ZM[AB], rec)
-        dis = ts(new("PB"), bank(7, 0, 64), 2.0, A.is_ge)
+            base2 = ts(f(), js, -2048.0, A.add, 1024.0 - B, A.min)
+            delta = tt(f(), dr, occ, A.mult)
+        at(r0 + (11000 if t else 13050))
+        dis = ts(new("PB"), ab, 2.0, A.is_ge) if t else tt(new("PB"), ab, act(f(), dr, F.Identity, bias=2.0), A.is_ge)
         sc = scan(new("PB"), dis)
-        xq = mm(bank(6, 0, 64), more + [(NBG, dis), (ONES, sc)])
-        ndc = mm(bank(5, 0, 1), [(ONES, sub(sc, 63, 64))])
-        off1 = ts(new("PU"), tt(f(), xq, base1, A.min), float(B), A.add)
-        nsb = ts(f(), xq, fc, A.is_ge, 16384.0, A.mult)
-        bb = tt(p(), xq, nsb, A.add)
-        ns = act(f(), nsb, F.Identity, scale=1 / 16384.0)
-        succ = act(f(), nsb, F.Identity, scale=-1 / 16384.0, bias=1.0)
-        cnw = act(c(), ndc, F.Identity, bias=cb)
-        off2 = ts(new("PU"), tt(f(), bb, base2, A.min), float(FL + B), A.add)
-        add("V", (lambda RW, rec, off1: lambda: g.vector.tensor_copy(ap(v(RW, 0, EO)).indirect(ap(off1)), ap(rec)))(RW, rec, off1),
-            [rec, off1], [v(RW, 0, EO)], 60 + 1024 * 3.8)
+        xq = mm(bank(7, 64, 64), more + [(NBG, dis), (ONES, sc)])
+        if not t:
+            off1 = ts(new("PU"), tt(f(), xq, base1, A.min), float(B), A.add)
+        nsb = ts(new("PB"), xq, fc, A.is_ge, 16384.0, A.mult)
+        bb = tt(p(), xq, nsb, A.add) if not t else tt(f(), xq, nsb, A.add)
+        if t:
+            off1 = ts(new("PU"), tt(p(), bb, base1, A.min), float(B), A.add)
+        off2 = ts(new("PU"), tt(f() if not t else p(), bb, base2, A.min), float(FREE + B), A.add)
+        at(r1 - 4100)
+        add("V", (lambda RW, off1: lambda: g.vector.tensor_tensor(ap(v(RW, PAR, RN)).indirect(ap(off1)), ap(full("X")), ap(full("W")), A.mult))(RW, off1),
+            [full("X"), full("W"), off1], [v(RW, PAR, RN)], 60 + 1024 * 3.8)
         for h in range(2):
-            act(wide("RG", h), ind(v(RW, 0, 4608), half(off2, h)), F.Identity)
+            at(r1, "SV"[h])
+            act(wide("RG", h), ind(v(RW, 0, RN), half(off2, h)), F.Identity)
         if t < 2:
-            iota(v("RW%d" % (t + 1), 0, FL), [[0, FL]], 0, 0)
-        wrap(bank(7, 0, 64), ZM[FG], rec)
-        wrap(bank(0, 0, 64), ZM[DQ], rec)
-        wrap(bank(1, 0, 64), ZM[QM], rec)
+            at(r1)
+            const(v("RW%d" % (t + 1), PAR, FREE), 0)
+            const(v("RW%d" % (t + 1), NONE, RN), 0)
+        at(r1 - 4000)
+        lw = act(new("PB"), wrap(bank(7, 192, 64), ZM[LW], full("W")), F.Identity)
+        df, rt = wrap(bank(7, 128, 64), ZM[DF], full("X")), wrap(bank(7, 256, 64), ZM[RT], full("X"), [(IDB, fr)])
+        dj = wrap(bank(7, 320, 64), ZM[DJ], full("X"), [(ID, nsb)])
         if t:
-            mm(bank(5, 64, 64), more + [(NUS, dis), (ONES, sc)])
-            lb = act(c(), fc, F.Identity, bias=B + 0.5)
-            acc = c()
-            act(f(), bank(5, 64, 64), F.Sign, bias=lb, scale=-1.0, acc=acc)
-            mm(bank(5, 128, 1), [(OF, acc)], slow=4)
-            lst = act(c(), bank(5, 128, 1), F.Identity, bias=512.0 + 2048, scale=0.5)
-        lw = ts(f(), bank(7, 0, 64), 8192.0, A.is_ge, -0.5, A.add)
-        tq = tt(f(), lw, bank(0, 0, 64), A.mult)
-        qw = tt(p(), bank(1, 0, 64), tq, A.add)
-        qo = tt(p(), bank(1, 0, 64), tq, A.subtract)
-        newc = ts(f(), jf, cnw, A.is_lt)
-        ep = tt(p() if t else f(), occ, qw, A.mult)
-        sqo = tt(f(), succ, qo, A.mult)
-        pair = tt(p() if t else f(), succ, newc, A.add)
-        wrap(bank(6, 0, 64), ZM[XL], v("X", 0, 1024))
-        wrap(bank(6, 64, 64), ZM[XR], v("X", 0, 1024))
-        xlr = cp(new("PU", 128), bank(6, 0, 128))
-        xl, xr = sub(xlr, 0, 64), sub(xlr, 64, 128)
+            co = mm(bank(7, 384, 64), [(ID, lw), (NID, nsb)])
+        at(r1 + 500)
+        qw = tt(f(), rt, tt(f(), df, lw, A.mult), A.add)
+        sj = ts(f(), dj, 0.0, A.is_equal)
         if t:
-            ep = tt(f(), ep, e2, A.add)
-            pair = tt(f(), pair, arr, A.subtract)
+            co = tt(f(), co, lane1k, A.add)
+        at(r0 + (7600 if t else 9600))
+        tt(full(CW, REST), ind(v("KT", 0, 4608), hx), full(zn), A.mult)
+        at(r0 + 11500)
+        act(full(CW, LEFT), full("sg"), F.Identity, bias=(MARK - e) / 2, scale=-(MARK + e) / 2)
+        act(full(CW, RIGHT), full("sg"), F.Identity, bias=(MARK + e) / 2, scale=(MARK - e) / 2)
+        for a in (LEFT, RIGHT):
+            dma("G", ap(full(CW, a)), ap(full(CW, REST)), [full(CW, REST)], [full(CW, a)], 4000)
+        at(r1 + 900)
+        q = wrap(bank(0, 0, 64), ZM[QO], full("RG"), [(IDB, occ)])
+        jn = wrap(bank(1, 0, 64), ZM[JN], full("RG"), [(ID, nsb), (ID, CM)])
+        tn = wrap(bank(6, 448, 64), ZM[TW], full("RG"))
+        if t:
+            cw = wrap(bank(7, 448, 64), ZM[CP], full("RG"), [(ID, nsb), (ID, CM)])
+        at(r1 + 2200)
+        q = tt(new("PI"), q, qw, A.max)
+        si = ts(new("PI"), q, 12, A.arith_shift_right)
+        sa = cp(new("PU"), si)
+        for h in range(2):
+            act(wide("G1", h), ind(v(CW, 0, 4096), half(sa, h)), F.Identity)
+        jq = ts(new("PI"), q, 4080, A.bitwise_and)
+        hl = new("PI", 128)
+        hi = ts(sub(hl, 0, 64), q, 4095, A.bitwise_and)
+        lo = ts(sub(hl, 64, 128), q, 12, A.arith_shift_right, 1023, A.bitwise_and)
         if not last:
-            on0 = tt(f(), occ, newc, A.add)
-        tt(v(CW, REST, REST + 1024), ind(v("KT", 0, 5120), hx), v(zn, 0, 1024), A.mult)
-        act(v(CW, 0, 1024), v("sg", 0, 1024), F.Identity, bias=(MARK - e) / 2, scale=-(MARK + e) / 2)
-        act(v(CW, RIGHT, RIGHT + 1024), v("sg", 0, 1024), F.Identity, bias=(MARK + e) / 2, scale=(MARK - e) / 2)
-        for a in (0, RIGHT):
-            dma("G", ap(v(CW, a, a + 1024)), ap(v(CW, REST, REST + 1024)), [v(CW, REST, REST + 1024)], [v(CW, a, a + 1024)], 4000)
-        act(v("SL", 0, 1024), ind(v("DT", 0, 4096), xl), F.Sigmoid)
-        act(v("SR", 0, 1024), ind(v("DT", 0, 4096), xr), F.Sigmoid)
-        for h in range(2):
-            mm(bank(2), [(ID, wide("sg", h))])
-            tt(bank(3), wide(AW, h, REST), bank(2), A.mult)
-            act(bank(2), bank(3), F.Identity, scale=-1.0)
-            tt(wide(AW, h), wide("SL", h), bank(3), A.mult)
-            tt(wide(AW, h, RIGHT), wide("SR", h), bank(2), A.mult)
-        rg = v("RG", 0, 1024)
-        pf_, pd, pr = bank(7, 0, 64), bank(0, 0, 64), bank(1, 0, 64)
-        wrap(pf_, ZM[FG], rg)
-        wrap(pd, ZM[DQ], rg)
-        wrap(pr, ZM[QM], rg)
-        lw = ts(f(), pf_, 8192.0, A.is_ge, -0.5, A.add)
-        idi = cp(new("PI"), pf_)
+            d0 = ts(f(), hi, 3584.0, A.is_ge, 512.0, A.mult)
+            hx = cp(new("PU"), tt(p(), hi, d0, A.add))
+        at(r1 + (2600 if last else 8000))
+        u16 = new("PU", 128)
         if t:
-            key = ts(new("PI"), idi, 8191, A.bitwise_and)
-            old = tt(p(), ts(p(), key, lst, A.is_ge), npo, A.mult)
-            pair = tt(f(), pair, old, A.max)
-        idn = ts(new("PI"), idi, 1023, A.bitwise_and)
-        gt = tt(f(), idn, lane, A.is_gt)
-        tq = tt(f(), lw, pd, A.mult)
-        qi = new("PI", 128)
-        qo = tt(p(), pr, tq, A.subtract)
-        qw = tt(p(), pr, tq, A.add)
-        tt(sub(qi, 0, 64), tt(p(), newc, qo, A.mult), ep, A.add)
-        tt(sub(qi, 64, 128), tt(p(), ns, qw, A.mult), sqo, A.add)
-        jj = ts(new("PI", 128), qi, 4, A.arith_shift_right, 255, A.bitwise_and)
-        sr = ts(new("PI", 128), qi, 12, A.arith_shift_right)
-        hi = ts(new("PI"), sub(qi, 0, 64), 4095, A.bitwise_and)
-        slot[0] = 0
-        fuse = tt(p(), tt(p(), sub(jj, 0, 64), sub(jj, 64, 128), A.is_equal), pair, A.mult)
-        mk = p(128)
-        lo = tt(sub(mk, 64, 128), fuse, gt, A.mult)
-        nup = tt(sub(mk, 0, 64), fuse, gt, A.is_le)
-        s16 = ts(new("PU", 128), tt(new("PF", 128), sr, mk, A.mult), float(DEAD), A.add)
-        sa, sb = sub(s16, 0, 64), sub(s16, 64, 128)
-        wn = SCRATCH[CW][1][1]
-        an = ("G1", 0) if last else ("AW%d" % (t + 1), REST)
+            cp(u16, tt(new("PF", 128), hl, delta, A.add))
+        else:
+            cp(sub(u16, 0, 64), tt(f(), hi, delta, A.add))
+            cp(sub(u16, 64, 128), sub(hl, 64, 128))
+        hp, sm = sub(u16, 0, 64), sub(u16, 64, 128)
+        at(r1 + 3300)
+        fuse = tt(f(), tt(p(), jn, jq, A.is_equal), sj, A.max)
+        at(r1 + (5400 if t else 3500))
+        if t:
+            cw = tt(p(), cw, co, A.max)
+        else:
+            cw = tt(p(), ts(p(), lo, 2.0, A.mult, float(LEFT + RIGHT), A.add), si, A.subtract)
+        sz = cp(new("PU"), tt(p(), cw, fuse, A.mult))
         for h in range(2):
-            act(wide("G1", h), ind(v(CW, 0, wn), half(sa, h)), F.Identity)
-        for h in range(2):
-            tt(wide("Z", h), ind(v(CW, 0, wn), half(sb, h)), wide("G1", h), A.min)
+            at(r1 + (5600 if t else 4000) + 1000 * h)
+            tt(wide("Z", h), ind(v(CW, 0, 4096), half(sz, h)), wide("G1", h), A.min)
+        ops[-1]["goal"] = True
+        at(r1 + 4400)
+        gt = tt(f() if last else p(), tn, lane16, A.is_gt)
+        nup = tt(f(), fuse, gt, A.is_le)
         if last:
+            so = cp(new("PU"), tt(p(), nup, lane16, A.mult))
+            sb = cp(new("PU"), tt(f(), tn, tt(f(), fuse, gt, A.mult), A.mult))
             h16 = cp(new("PU"), hi)
+        else:
+            sb = tt(f(), tn, fuse, A.mult)
+            tw = act(f(), tn, F.Identity, bias=1024.0 - B)
+            at(r1 + 8100)
+            sb = cp(new("PU"), sb)
+        if not last:
+            at(r1 + 4600)
+            dr = tt(new("PB"), nup, d0, A.mult)
+            sc = scan(new("PB"), dr)
+            y = mm(bank(6, 0, 64), [(NBG, dr), (ONES, sc)])
+            par = ts(new("PI"), q, 1, A.bitwise_and)
+            at(r1 + 5200)
+            lv = ts(new("PB"), y, 512.0 * (128 - B), A.is_lt, -512.0, A.mult)
+            x2 = new("PB", 128)
+            od = tt(sub(x2, 64, 128), par, lv, A.mult)
+            tt(sub(x2, 0, 64), lv, od, A.subtract)
+            sc = scan(new("PB", 128), x2)
+            at(r1 + 9200)
+            fr = tt(new("PB"), tt(p(), ts(p(), q, 4096.0, A.is_lt), nup, A.is_ge), lv, A.is_gt)
+            at(r1 + 5900)
+            e0, e1 = sub(sc, 63, 64), sub(sc, 127, 128)
+            mm(bank(6, 64, 1), [(ONES, K7), (ONES, e0)])
+            mm(bank(6, 65, 1), [(ONES, K7), (ONES, e0), (SO, e1), (NSO, e0)])
+            mm(bank(6, 66, 1), [(ONES, K1), (ONES, e0), (NSO, e0)])
+            mm(bank(6, 67, 1), [(NON, K1), (ONES, e0), (NSO, e0)])
+            cs = act(v("cs%d" % (t + 1), 0, 4), bank(6, 64, 4), F.Identity, scale=-1 / 512.0)
+            send(v("cn%d" % (t + 1), 0, 4), cs, eng[0:4], "rc%d" % (t + 1))
+            mm(bank(6, 128, 128), [(ONES, sc)])
+            mm(bank(6, 256, 128), [(NUS, x2), (ONES, sc)])
+            at(r1 + 9500)
+            act(v("Pc", 0, 128), bank(6, 256, 128), F.Identity, scale=-1 / 512.0)
+            acc = new("PF", 8)
+            for j in range(8):
+                act(v("junk", 128 * j, 128 * j + 128), bank(6, 128, 128), F.Sign, bias=sub(jb, j, j + 1), scale=1 / 512.0, acc=sub(acc, j, j + 1))
+            at(r1 + 11400)
+            b16 = ts(new("PU", 8), acc, 0.5, A.mult, 64.0, A.add)
+            cm = tt(new("PB", 128), ind(v("Pc", 0, 136), b16), JW, A.is_le)
+            b6 = act(new("PF", 8), acc, F.Identity, scale=8.0, bias=1024.0)
+            lvl = cp(new("PU", 8), ts(new("PI", 8), tt(new("PI", 8), wrap(bank(6, 384, 8), ZS, cm), b6, A.add), 1023, A.bitwise_and))
+        an = "AW%d" % (t + 1)
+        at(r1 + (4700 if last else 13600))
+        if SPARE[t]:
             for h in range(2):
-                act(wide("G2", h), ind(v(AW, 0, wn), half(sa, h)), F.Relu)
-                act(bank(h), wide("Z", h), F.Sigmoid, bias=THR, scale=-1.0)
+                act(wide("DG", h), ind(v("DT", 0, 4608), half(hp, h)), F.Identity)
+                step(wide("MG", h), wide("G1", h), True)
+                act(wide("FM", h), mm(bank(2 + h), [(ID, wide("DG", h)), (IDB, wide("MG", h))]), F.Sigmoid)
+        else:
+            act(full("FP"), ind(v("DT", 0, 4608), hp), F.Sigmoid)
             for h in range(2):
-                tt(wide("SL", h), wide("Z", h), bank(h), A.mult)
-                dma("Y", T.yc[:, H[h][0]:H[h][1]], ap(wide("SL", h)), [wide("SL", h)], [], 2400)
-                tt(wide("G1", h), ind(v(AW, 0, wn), half(sb, h)), wide("G2", h), A.max)
-                tt(wide("SR", h), ind(v("KT", 0, 4096), half(h16, h)), wide("G1", h), A.mult)
-                dma("Y", T.ya[:, H[h][0]:H[h][1]], ap(wide("SR", h)), [wide("SR", h)], [], 2400)
+                step(bank(2 + h), wide("G1", h), False)
+            at(r1 + (7500 if last else STEP + 600))
+            for h in range(2):
+                tt(wide("FM", h), wide("FP", h), bank(2 + h), A.mult)
+        at(r1 + (7600 if last else STEP + 700))
+        for h in range(2):
+            tt(wide(an, h, 16), ind(aw, half(sm, h)), wide("FM", h), A.mult)
+        if last:
+            for h in range(2):
+                at(r1 + 10000 + 100 * h)
+                act(wide("FP", h), ind(v(an, 0, 1040), half(so, h)), F.Identity)
+                tt(wide("FM", h), ind(v(an, 0, 1040), half(sb, h)), wide("FP", h), A.add)
+                tt(wide("Y1", h), ind(v("KT", 0, 4096), half(h16, h)), wide("FM", h), A.mult)
+                dma("Y", T.ya[:, H[h][0]:H[h][1]], ap(wide("Y1", h)), [wide("Y1", h)], [], 2400)
+                tt(wide("Y2", h), wide("Z", h), act(bank(h), wide("FM", h), F.Sign), A.mult)
+                dma("S", T.yc[:, H[h][0]:H[h][1]], ap(wide("Y2", h)), [wide("Y2", h)], [], 2400)
             break
-        d5 = ts(f(), hi, 3584.0, A.is_ge, 512.0, A.mult)
-        on = tt(p(), on0, nup, A.mult)
-        npair = tt(p(), pair, fuse, A.subtract)
-        dr = tt(new("PB"), d5, on, A.mult)
-        sc = scan(new("PB"), dr)
-        y = mm(bank(6, 0, 64), [(NBG, dr), (ONES, sc)])
-        hd = tt(p(), hi, d5, A.add)
-        l5 = ts(f(), y, 512.0 * (128 - B), A.is_lt, 512.0, A.mult)
-        lv = act(f(), l5, F.Identity, scale=1 / 512.0)
-        hx = cp(new("PU"), tt(f(), hd, l5, A.add))
-        occ = tt(f(), on, lv, A.subtract)
-        npo = tt(f(), npair, occ, A.mult)
-        tw = tt(f(), tt(p(), npo, tt(p(), idn, lane, A.subtract), A.mult), lane2, A.add)
-        an1 = v(an[0], an[1], an[1] + 1024)
-        act(an1, ind(v(AW, 0, wn), sa), F.Relu)
-        act(v("G2", 0, 1024), ind(v(AW, 0, wn), sb), F.Relu)
-        dma("G", ap(an1), ap(v("G2", 0, 1024)), [v("G2", 0, 1024)], [an1], 4000)
-        x2 = new("PB", 128)
-        od = tt(sub(x2, 64, 128), ts(new("PI"), hi, 1, A.bitwise_and), lv, A.mult)
-        tt(sub(x2, 0, 64), lv, od, A.subtract)
-        sc = scan(new("PB", 128), x2)
-        e0, e1 = sub(sc, 63, 64), sub(sc, 127, 128)
-        mm(bank(6, 128, 128), [(ONES, sc)])
-        mm(bank(7, 0, 1), [(ONES, e0)])
-        mm(bank(7, 1, 1), [(ONES, e0), (SO, e1), (NSO, e0)])
-        mm(bank(7, 2, 1), [(ONES, e0), (NSO, e0)])
-        mm(bank(7, 128, 128), [(NUS, x2), (ONES, sc)])
-        cs = "cs%d" % (t + 1)
-        act(v(cs, 0, 2), bank(7, 0, 2), F.Identity, bias=-float(B + FL))
-        act(v(cs, 2, 3), bank(7, 2, 1), F.Identity, bias=-128.0)
-        act(v(cs, 3, 4), bank(7, 2, 1), F.Identity, scale=-1.0, bias=EO + 128.0)
-        send([(v("cn%d" % (t + 1), 0, 4), v(cs, 0, 4))], eng[0:4], "rc%d" % (t + 1))
-        act(v("Pc", 0, 128), bank(7, 128, 128), F.Identity)
-        acc = new("PF", 8)
-        for j in range(8):
-            act(v("RG", 128 * j, 128 * j + 128), bank(6, 128, 128), F.Sign, bias=sub(jb, j, j + 1), scale=-1.0, acc=sub(acc, j, j + 1))
-        b16 = ts(new("PU", 8), acc, 0.5, A.mult, 64.0, A.add)
-        cm = tt(new("PB", 128), ind(v("Pc", 0, 136), b16), JW, A.is_le)
-        b6 = tt(new("PF", 8), ts(new("PF", 8), acc, 0.0, A.is_ge, -1024.0, A.mult), act(new("PF", 8), acc, F.Identity, scale=8.0, bias=1024.0), A.add)
-        wrap(bank(7, 0, 8), ZS, cm)
-        lvl = ts(new("PU", 8), tt(new("PF", 8), b6, bank(7, 0, 8), A.add), 1023.0, A.min)
         bc, ba = "bc%d" % (t + 1), "ba%d" % (t + 1)
-        act(v(bc, 0, 128), ind(v("Z", 0, 1024), lvl), F.Identity, scale=0.5)
-        act(v(ba, 0, 128), ind(v(an[0], an[1], an[1] + 1024), lvl), F.Identity)
-        for n in (bc, ba):
-            dma("Y", T[n][16:128, 128:256], T[n][0:112, 0:128], [v(n, 0, 128)], [v(n, 128, 256, 1, (16, 128, 1))], 2200)
-            dma("Y", T[n][0:16, 128:256], T[n][112:128, 0:128], [v(n, 0, 128)], [v(n, 128, 256, 1, (0, 16, 1))], 2200)
-        send([(v("CW%d" % (t + 1), EO, EO + 256), v(bc, 0, 256))], eng[0:4], "rd%d" % (t + 1))
-        send([(v("AW%d" % (t + 1), EO, EO + 256), v(ba, 0, 256))], eng[0:4], "ra%d" % (t + 1))
+        at(r1 + 13300)
+        act(v(bc, 0, 128), ind(full("Z"), lvl), F.Identity, scale=0.5)
+        dma("Y", T[bc][16:128, 128:256], T[bc][0:112, 0:128], [v(bc, 0, 128)], [v(bc, 128, 256, 1, (16, 128, 1))], 2200)
+        dma("Y", T[bc][0:16, 128:256], T[bc][112:128, 0:128], [v(bc, 0, 128)], [v(bc, 128, 256, 1, (0, 16, 1))], 2200)
+        send(v("CW%d" % (t + 1), ARR, ARR + 256), v(bc, 0, 256), eng[0:4], "rd%d" % (t + 1))
+        at(r1 + STEP + 4000)
+        act(full("Y1"), ind(v(an, 0, 1040), sb), F.Identity)
+        tt(v(ba, 0, 128), ind(full("Y1"), lvl), act(new("PF", 128), ind(full(an, 16), lvl), F.Identity), A.add)
+        dma("G", ap(full(an, 16)), ap(full("Y1")), [full("Y1")], [full(an, 16)], 4000)
+        act(v(ba, 128, 256), mm(bank(5, 384, 128), [(SF, v(ba, 0, 128))], 4), F.Identity)
+        send(v(an, 1024 + ARR, 1024 + ARR + 256), v(ba, 0, 256), eng[0:4], "ra%d" % (t + 1))
     return ops
 
 
-HOP, TRIES, FOUND = 80, 12000, {}
+HOP, TRIES, HEAT, SEED, FOUND = 120, 30000, 120.0, 1, {}
+PULL, PULL2, BACK, RESET = 1e-4, 0.1, 0.97, 0.02
 
 
 def meet(a, b):
     if a[0] != b[0] or a[2] <= b[1] or b[2] <= a[1]:
         return False
-    if a[3] == b[3] and a[3] > 1 and (a[1] - b[1]) % a[3]:
+    if (a[3] > 1 or b[3] > 1) and not set(range(a[1], a[2], a[3])) & set(range(b[1], b[2], b[3])):
         return False
     if a[4] and b[4]:
         if a[4][1] <= b[4][0] or b[4][1] <= a[4][0]:
@@ -566,13 +657,194 @@ def meet(a, b):
     return True
 
 
+def edges(ops):
+    pre = [dict() for _ in ops]
+    seen = {}
+    for j, o in enumerate(ops):
+        if "after" in o:
+            pre[j][o["after"]] = False
+        use = [(x, False) for x in o["rd"]] + [(x, True) for x in o["wr"]]
+        for x, w in use:
+            for i, y, wy in seen.get(x[0], []):
+                if (w or wy) and meet(x, y):
+                    pre[j][i] = ops[i]["q"] != "P" or o["q"] != "P"
+        for x, w in use:
+            seen.setdefault(x[0], []).append((j, x, w))
+    done = [0] * len(ops)
+    for j in range(len(ops)):
+        far = 0
+        for i in pre[j]:
+            if pre[j][i] and ops[i]["q"] != "R":
+                far |= done[i]
+        for i in list(pre[j]):
+            if far >> i & 1:
+                del pre[j][i]
+        done[j] = far
+        for i in pre[j]:
+            if pre[j][i]:
+                done[j] |= 1 << i
+    return pre
+
+
+def place(seq, cut, key, fore, how, banks, first, start, end):
+    start, end, key = list(start), list(end), list(key)
+    line = {q: ([], []) for q in "VSPGYR"}
+    held = {}
+    for j in sorted(seq[:cut], key=lambda i: start[i]):
+        S, E = line[how[j][0]]
+        S.append(start[j])
+        E.append(end[j])
+        for b in banks[j]:
+            held.setdefault(b, []).append((start[j], end[j], how[j][0]))
+    todo = seq[cut:]
+    for j in todo:
+        for i, d in fore[j]:
+            if key[i] >= key[j]:
+                key[j] = key[i] + 1e-3
+    todo.sort(key=lambda i: key[i])
+    for j in todo:
+        s = first[j]
+        for i, d in fore[j]:
+            if end[i] + d > s:
+                s = end[i] + d
+        q, ns = how[j]
+        S, E = line[q]
+        k = len(S)
+        while k and E[k - 1] > s:
+            k -= 1
+        while True:
+            while k < len(S) and S[k] < s + ns:
+                if E[k] > s:
+                    s = E[k]
+                k += 1
+            s0 = s
+            for b in banks[j]:
+                for a, z, q2 in held.get(b, ()):
+                    if q2 != q and a < s + ns + HOP and z + HOP > s:
+                        s = z + HOP
+            if s == s0:
+                break
+        while k and S[k - 1] > s:
+            k -= 1
+        S.insert(k, s)
+        E.insert(k, s + ns)
+        for b in banks[j]:
+            held.setdefault(b, []).append((s, s + ns, q))
+        start[j], end[j] = s, s + ns
+    return start, end, key, seq[:cut] + todo
+
+
 def order(ops):
+    n = len(ops)
+    pre = edges(ops)
+    banks = [sorted({x[0] for x in o["rd"] + o["wr"] if SCRATCH[x[0]][0] == "psum" and x[0] != "P4"}) for o in ops]
+    if n not in FOUND:
+        rng = np.random.RandomState(SEED)
+        lat = [o.get("lat", 0) for o in ops]
+        fore = [[(i, lat[i] + HOP if pre[j][i] else 0) for i in pre[j]] for j in range(n)]
+        back = [[] for _ in ops]
+        for j in range(n):
+            for i, d in fore[j]:
+                back[i].append((j, d))
+        alt = [[(q, x[1]) for q, x in o["alt"].items()] if "alt" in o else None for o in ops]
+        flex = [i for i in range(n) if alt[i]]
+        tags = {}
+        for i, o in enumerate(ops):
+            tags.setdefault(o["tag"], []).append(i)
+        tags = list(tags.values())
+        how = [(o["q"], o["ns"]) for o in ops]
+        tail = [0.0] * n
+        for i in range(n - 1, -1, -1):
+            tail[i] = how[i][1] + max([tail[j] + d for j, d in back[i]] + [lat[i]])
+        key, zero = [float(o["when"]) for o in ops], [0.0] * n
+        now = top = None
+        big = [i for i in range(n) if ops[i]["ns"] > 3000]
+        held, seq, begins, ends = [], list(range(n)), zero, zero
+        for k in range(TRIES):
+            ky, hw, u = list(key), list(how), float(rng.rand())
+            if k and held and u < 0.7:
+                i, j = held[int(rng.randint(len(held)))]
+                m = int(rng.randint(5))
+                if m < 2 and alt[(i, j)[m]]:
+                    x = (i, j)[m]
+                    hw[x] = alt[x][int(rng.randint(len(alt[x])))]
+                elif m == 2:
+                    ky[i] = ky[j] + 1 + float(rng.exponential(500))
+                elif m == 3:
+                    d, todo, got = ky[j] - ky[i] + 1 + float(rng.exponential(300)), [j], {j}
+                    while todo:
+                        x = todo.pop()
+                        ky[x] -= d
+                        for y, _ in fore[x]:
+                            if y not in got and ky[y] > ky[x] - 300 and len(got) < 12:
+                                got.add(y)
+                                todo.append(y)
+                else:
+                    ky[j] = ky[i] - 1
+            elif k and u < 0.8:
+                x = flex[int(rng.randint(len(flex)))]
+                hw[x] = alt[x][int(rng.randint(len(alt[x])))]
+            elif k and u < 0.87:
+                for i in rng.randint(0, n, 2):
+                    ky[int(i)] += float(rng.normal()) * 1500
+            elif k and u < 0.95:
+                d = float(rng.normal()) * 2500
+                for i in tags[int(rng.randint(len(tags)))]:
+                    ky[i] += d
+            elif k and u < BACK:
+                ky = [-x for x in place(seq[::-1], 0, [-x for x in ends], back, hw, banks, lat, zero, zero)[1]]
+            low = min([min(a, b) for a, b, x, y in zip(key, ky, how, hw) if a != b or x != y] or [-1e9])
+            cut = 0
+            while k and key[seq[cut]] < low:
+                cut += 1
+            st, en, ky, sq = place(seq, cut, ky, fore, hw, banks, zero, begins, ends)
+            if rng.rand() < RESET:
+                ky, sq = list(st), sorted(sq, key=lambda i: st[i])
+            end = max(en[i] + lat[i] for i in range(n)) + PULL * sum(st) + PULL2 * sum(st[i] for i in big)
+            if now is None or end <= now - HEAT * (1.02 - k / TRIES) * float(np.log(rng.rand())):
+                now, key, how, begins, ends, seq = end, ky, hw, st, en, sq
+                if top is None or end < top[0]:
+                    top = (end, st, hw)
+                before, last = [[] for _ in ops], {}
+                for i in sorted(seq, key=lambda i: st[i]):
+                    for r in [hw[i][0]] + banks[i]:
+                        if r in last:
+                            before[i].append(last[r])
+                        last[r] = i
+                j, held = max(range(n), key=lambda i: en[i] + lat[i]), []
+                while j is not None:
+                    nx = [i for i, d in fore[j] if en[i] + d > st[j] - 0.5]
+                    if not nx:
+                        nx = [i for i in before[j] if en[i] + HOP > st[j] - 0.5]
+                        held += [(i, j) for i in nx[:1]]
+                    j = nx[0] if nx else None
+        FOUND[n] = top
+    start = FOUND[n][1]
+    for o, (q, ns) in zip(ops, FOUND[n][2]):
+        if "alt" in o:
+            o["q"], o["fn"], o["ns"] = q, o["alt"][q][0], ns
+    seq = sorted(range(n), key=lambda i: (start[i], i))
+    last = {}
+    for j in seq:
+        for b in banks[j]:
+            for q, i in last.setdefault(b, {}).items():
+                if q != ops[j]["q"]:
+                    pre[j][i] = True
+            last[b][ops[j]["q"]] = j
+    post = [[] for _ in ops]
+    for j in range(n):
+        for i in pre[j]:
+            post[i].append(j)
+    return pre, post, seq, start
+
+
+def order_old(ops):
     n = len(ops)
     pre = [dict() for _ in ops]
     seen = {}
     for j, o in enumerate(ops):
         if "after" in o:
-            pre[j][ops.index(o["after"])] = False
+            pre[j][o["after"]] = False
         for x, w in [(x, False) for x in o["rd"]] + [(x, True) for x in o["wr"]]:
             ps = SCRATCH[x[0]][0] == "psum"
             for i, y, wy in seen.get(x[0], []):
@@ -583,7 +855,7 @@ def order(ops):
                     pre[j][i] = True
                 elif (w or wy) and meet(x, y):
                     pre[j][i] = pre[j].get(i, False) or not same or o["q"] != "P"
-                elif ps and w and wy:
+                elif ps and w and wy and o["q"] == "P":
                     pre[j][i] = pre[j].get(i, False)
         for x, w in [(x, False) for x in o["rd"]] + [(x, True) for x in o["wr"]]:
             seen.setdefault(x[0], []).append((j, x, w))
@@ -616,7 +888,8 @@ def order(ops):
         back = [[(i, lat[i] + HOP if pre[j][i] else 0) for i in pre[j]] for j in range(n)]
 
         def flip(i):
-            ops[i]["q"] = "V" if ops[i]["q"] == "S" else "S"
+            a, b = list(ops[i]["alt"])[0], list(ops[i]["alt"])[-1]
+            ops[i]["q"] = b if ops[i]["q"] == a else a
             ops[i]["fn"], ops[i]["ns"] = ops[i]["alt"][ops[i]["q"]]
         for k in range(TRIES):
             tr, fl = dict(pr), []

@@ -1,3 +1,4 @@
+import math
 import numpy as np
 from concourse.bass import DstId, RemoteDMATransfer
 from concourse.mybir import AluOpType as A, AxisListType, ActivationFunctionType as F
@@ -14,15 +15,17 @@ SCRATCH = {
     "AW1": ("sbuf", [128, 1296], "float32"), "AW2": ("sbuf", [128, 1296], "float32"), "AW3": ("sbuf", [128, 1040], "float32"),
     "MT": ("sbuf", [128, 144 * 3 + 128 * 6], "bfloat16"), "ZZ": ("sbuf", [128, 144 * 11], "bfloat16"),
     "Q": ("sbuf", [128, 160], "float32"), "QG": ("sbuf", [128, 144], "float32"), "SF": ("sbuf", [128, 128], "float32"),
-    "WR": ("sbuf", [128, 320], "bfloat16"), "OH": ("sbuf", [128, 144 + 256], "bfloat16"), "raw": ("sbuf", [128, 1024], "bfloat16"),
+    "WR": ("sbuf", [128, 320], "bfloat16"), "OH": ("sbuf", [128, 144 + 256], "bfloat16"), "raw": ("sbuf", [128, 1536], "bfloat16"),
     "col": ("sbuf", [128, 96], "float32"), "coi": ("sbuf", [128, 8], "int32"),
     "st": ("sbuf", [128, 64 * 4], "float32"), "Pc": ("sbuf", [128, 136], "float32"), "CB": ("sbuf", [128, 64 * 6], "bfloat16"),
     "junk": ("sbuf", [128, 1024], "bfloat16"),
     "PF": ("sbuf", [128, 64 * NF], "float32"), "PI": ("sbuf", [128, 64 * NI], "int32"),
     "PU": ("sbuf", [128, 64 * NU], "uint16"), "PB": ("sbuf", [128, 64 * NB], "bfloat16"),
 }
-SPARE, STEP, LAT = [False, False, False], 18500, 0.8
-for _n in ("am", "cr", "Z0", "sg", "dd", "X", "W", "RG", "IDT", "DG", "MG"):
+SPARE, PICK, STEP, LAT = [False, False, False], [False, False, False], 18500, 0.6
+GATHER, SCATTER = 1.56, 3.8
+GUESSES = [(1.56, 3.8, 1.0, 120, 0, 0), (2.0, 5.4, 0.9, 100, 0, 0), (1.25, 2.6, 1.6, 170, 200, 250)]
+for _n in ("am", "cr", "Z0", "sg", "dd", "X", "W", "RG", "DG", "MG"):
     SCRATCH[_n] = ("sbuf", [128, 1024], "bfloat16")
 for _n in ("Z", "G1", "FP", "FM", "Y1", "Y2"):
     SCRATCH[_n] = ("sbuf", [128, 1024], "float32")
@@ -35,11 +38,11 @@ for _t in (1, 2):
     SCRATCH["br%d" % _t] = ("sbuf", [128, 384], "bfloat16")
 for _b in range(8):
     SCRATCH["P%d" % _b] = ("psum", [128, 512], "float32")
-NDMA = 44
+NDMA = 48
 SEMAPHORES = ["V", "S", "P", "G", "sent"] + ["d%d" % _k for _k in range(NDMA)] + ["rc1", "rc2", "rr1", "rr2", "rd1", "rd2", "ra1", "ra2"]
 
-SC, BI, BX, S1, P6, AB, LW, DF, RT, DJ, QO, JN, TW, CP, GS, GB, PO = range(17)
-NW = 17
+SC, BI, BX, AB, LW, DF, RT, DJ, QO, JN, TW, CP, GS, GB, PO = range(15)
+NW = 15
 K4, M4, ROUND = 4096, 1 << 22, 1.5 * 2 ** 27
 WEIGHTS = {
     AB: {5: 1, 7: 1}, LW: {1: 1024},
@@ -52,8 +55,8 @@ WEIGHTS = {
     SC: {4: 256, 8: 256, 10: 256, 1: 256, 0: -256, 12: -256, 2: -256, 5: 128, 7: -128, 15: None},
     BI: {4: 128, 8: 128, 10: 128, 1: 128, 0: -128, 12: -128, 2: -128, 5: 1920, 7: 1920, 6: 128, 14: 128, 3: 128,
          9: -128, 11: -128, 13: 128, 15: None},
-    BX: {0: 3584, 4: 3584, 8: 3584, 12: 3584, 3: 1, 6: 1, 14: 1, 5: None, 7: None, 9: None, 11: None, 15: None},
-    GS: {0: 1, 2: 1}, GB: {0: -3584}, PO: {9: 16}, S1: {6: 1, 14: 1}, P6: {6: 512},
+    BX: {0: 3584, 4: 3584, 8: 3584, 12: 3584, 3: 1, 6: None, 14: None, 5: None, 7: None, 9: None, 11: None, 15: None},
+    GS: {0: 1, 2: 1}, GB: {0: -3584}, PO: {9: 16},
 }
 
 
@@ -79,7 +82,7 @@ def cover(w):
     return runs
 
 
-EARLY = 6
+EARLY = 4
 RUNS = cover({z: WEIGHTS[z] for z in range(EARLY)}) + cover({z: WEIGHTS[z] for z in range(EARLY, NW)})
 
 
@@ -155,7 +158,7 @@ def plan(T, g, core, topo):
 
     def vns(out, a, b=None):
         if a[0] == "ind":
-            return 60 + width(out) * 1.56
+            return 60 + width(out) * GATHER
         n = width(out)
         if b is not None:
             return 60 + max(64, n * (1 if psum(a) or psum(b) else 2))
@@ -172,6 +175,9 @@ def plan(T, g, core, topo):
     def tt(out, a, b, op):
         add("V", lambda: g.vector.tensor_tensor(ap(out), src(a), ap(b), op), parts(a, b), [out], vns(out, a, b), ind=width(out) * (a[0] == "ind"))
         return out
+
+    def scatter(win, off, a, b):
+        add("V", lambda: g.vector.tensor_tensor(ap(win).indirect(ap(off)), ap(a), ap(b), A.mult), [a, b, off], [win], 60 + width(a) * SCATTER, sca=width(a))
 
     def cp(out, a):
         add("V", lambda: g.vector.tensor_copy(ap(out), src(a)), parts(a), [out], vns(out, a))
@@ -195,7 +201,7 @@ def plan(T, g, core, topo):
         if acc is not None:
             kw["accum_out"] = ap(acc)
         add("S", lambda: g.scalar.activation(ap(out), src(a), f, **kw), parts(a, bias, scale), [out] + parts(acc),
-            100 + max(64, width(out) * (1.56 if a[0] == "ind" else 1)), ind=width(out) * (a[0] == "ind"), sig=f == F.Sigmoid)
+            80 + max(64, width(out) * (GATHER if a[0] == "ind" else 1)), ind=width(out) * (a[0] == "ind"), sig=f == F.Sigmoid)
         if f == F.Identity:
             ts(out, a, 1.0 if scale is None else scale, A.mult, 0.0 if bias is None else bias, A.add)
             either()
@@ -296,7 +302,10 @@ def plan(T, g, core, topo):
     dma("S", T.DT[:, 0:4096], T.dam[:, :], [], [v("DT", 0, 4096)], 5800)
 
     at(300)
-    fill(v("XT", 0, 4096), 1.0)
+    fill(full("W"), 1.0)
+    for r, d in ((1, 4), (3, 4), (6, 8)):
+        x, y = v("XT", 0, 4096, 1, (r, 128, d)), v("W", 0, 4096 // d)
+        dma("Y", ap(x), ap(y), [y], [x], 3000)
     p0 = (0, 1, 1)
     at(200)
     fill(v("WR", 0, 16 * NW, 1, p0), 0.0)
@@ -309,7 +318,7 @@ def plan(T, g, core, topo):
             either()
     at(100)
     fill(v("OH", 0, 400, 1, p0), 0.0)
-    for a, b, d in ((15, 144, 16), (144, 272, 4), (150, 272, 16), (274, 400, 8), (286, 400, 16)):
+    for a, b, d in ((15, 144, 16), (144, 272, 4), (274, 400, 8)):
         if a == 15:
             act(v("OH", a, b, d, p0), v("OH", a, b, d, p0), F.Sigmoid, bias=128.0)
             ops[-1]["ns"] += 1500
@@ -318,22 +327,26 @@ def plan(T, g, core, topo):
     row = [v("OH", 15 - r, 143 - r, 1, p0) for r in range(16)]
     rows_hi, rows_lo = v("OH", 144, 272, 1, p0), v("OH", 272, 400, 1, p0)
     for a, b in ((0, EARLY), (EARLY, NW)):
-        at(11500 if a else 3500)
+        at(13500 if a else 4500)
         mm(bank(5, a, b - a), [(row[r], v("WR", NW * r + a, NW * r + b, 1, p0)) for r in range(16)])
         act(v("col", 16 + a, 16 + b), bank(5, a, b - a), F.Identity)
     Wt = [v("col", 16 + z, 17 + z) for z in range(NW)]
-    pcol, icol, g16, g15, B1, B2 = [v("col", k, k + 1) for k in range(6)]
-    at(4700)
-    act(B1, Wt[S1], F.Identity, scale=-1.0, bias=1.0)
-    act(B2, Wt[P6], F.Identity, bias=B1)
+    pcol, icol, g16, g15 = [v("col", k, k + 1) for k in range(4)]
+    at(1100)
+    p32 = (0, 32, 1)
+    iota(v("raw", 0, 512, 1, p32), [[16, 32], [0, 16]], 0, 0)
+    iota(v("raw", 1024, 1536, 1, p32), [[0, 32], [1, 16]], 0, 0)
+    hi0, lo0 = v("raw", 0, 512, 1, p0), v("raw", 1024, 1536, 1, p0)
+    at(6000)
+    act(v("raw", 512, 1024, 1, p32), v("raw", 0, 512, 1, p32), F.Identity, bias=512.0)
+    iota(v("raw", 512, 1024, 1, p32), [[16, 32], [0, 16]], 512, 0)
+    either()
     at(0)
-    hi0 = iota(v("raw", 0, 512, 1, p0), [[16, 32], [0, 16]], 0, 0)
-    lo0 = iota(v("raw", 512, 1024, 1, p0), [[0, 32], [1, 16]], 0, 0)
-    at(2400)
     iota(pcol, [[0, 1]], 0, 1)
     iota(v("Q", 0, 16), [[1, 16]], 112, 0)
     Q, JW = iota(v("Q", 16, 160), [[1, 144]], 0, 0), v("Q", 16, 144)
-    at(4200, "V")
+    at(1000, "V")
+    const(v("RW0", PAR, FREE), 0)
     cp(icol, ts(v("coi", 1, 2), iota(v("coi", 0, 1), [[0, 1]], 0, 1), 15, A.bitwise_and))
     act(g16, icol, F.Identity, scale=-1.0, bias=pcol)
     act(g15, g16, F.Identity, bias=15.0)
@@ -352,14 +365,15 @@ def plan(T, g, core, topo):
     ONE, C64 = const(v("CB", 0, 128), 1), const(v("CB", 128, 192), 64)
     at(13000)
     CM, K7, K1 = const(v("CB", 192, 256), -20480), const(v("CB", 256, 257), 32 * (B - 1023)), const(v("CB", 258, 259), 4096)
-    at(3400, "V")
+    at(1500, "V")
     ts(ident, v("Q", 0, 144), pcol, A.is_equal)
     act(NID, ID, F.Identity, scale=-1.0)
     act(IDB, ID, F.Identity, scale=-2.0 ** 25)
-    at(4400, "V")
+    at(3000, "V")
     ts(ones, v("QG", 0, 144), g16, A.is_equal)
     act(nones, ones, F.Identity, scale=-1.0)
-    select(MD, NON, [[0, 8], [1, 16]], A.not_equal, 0.0, -7, 0)
+    act(MD, ONES, F.Identity, scale=-1.0)
+    fill(sub(MD, 7, 128, 16), 0.0)
     act(sub(MD, 5, 128, 16), sub(ONES, 5, 128, 16), F.Identity, scale=-2.0)
     at(6000, "V")
     select(NUS, NON, [[-1, 128]], A.is_gt, 0.0, 0, 1)
@@ -373,20 +387,17 @@ def plan(T, g, core, topo):
     lane1k = act(v("st", 128, 192), lane16, F.Identity, bias=LEFT - 16.0)
     SF = act(v("SF", 0, 128), SH, F.Identity)
     at(6500)
-    fill(v("KT", 4096, 4608), 0.5)
+    act(v("KT", 4096, 4608), wide("am", 0), F.Identity, scale=0.0, bias=0.5)
     at(16500)
-    fill(v("DT", 4096, 4608), 64.0)
+    const(v("DT", 4096, 4608), 64)
     const(v("Pc", 128, 136), 0)
     for t in range(3):
         const(v("CW%d" % t, 0, 8), MARK)
         const(v("AW%d" % (t + 1), 0, 8), 0)
-    at(2500)
+    at(5600)
     mm(bank(6), [(rows_hi, hi0), (rows_lo, lo0)])
-    at(4800)
-    act(wide("IDT", 0), bank(6), F.Identity, scale=Wt[S1], bias=B1)
-    act(wide("IDT", 1), bank(6), F.Identity, scale=Wt[S1], bias=B2)
-    act(v("XT", 4096, 4608), bank(6), F.Identity, scale=B1, bias=Wt[BX])
-    at(2600)
+    act(v("XT", 4096, 4608), bank(6), F.Identity, bias=Wt[BX])
+    at(2300)
     act(wide("cb", 0), ts(v("ci", 0, 512), v("cmp", 0, 512), -7.5, A.add, ROUND, A.add), F.Identity, bias=-ROUND)
     for k, rows in enumerate(((0, 8, 4, 12), (2, 10))):
         if k:
@@ -396,22 +407,21 @@ def plan(T, g, core, topo):
             a = 512 * k + 256 * (2 * j // len(rows))
             dma("Y", T.XT[r::16, 0:4096], T.cb[:, a:a + 256], [v("cb", a, a + 256)], [v("XT", 0, 4096, 1, (r, 128, 16))], 2600)
     at(7800)
-    const(v("RW0", PAR, FREE), 0)
     const(v("RW0", NONE, LANE), 0)
 
-    at(6200)
+    at(4500)
     pf = cp(f(), v("pl", 0, 64))
     hf = f()
     add("V", lambda: g.vector.transpose(ap(hf), ap(pf)), [pf], [hf], 124)
     dr = ts(new("PB"), hf, 3584.0, A.is_ge, 512.0, A.mult)
     hx = cp(new("PU"), tt(f(), hf, dr, A.add))
-    at(3200)
+    at(1700)
     ts(full("dd"), full("am"), 0.0, A.is_equal)
     for h in range(2):
-        at(4600 + 1100 * h)
+        at(2400 + 1100 * h)
         mm(bank(2 + h), [(NID, wide("cr", h)), (IDB, wide("dd", h))])
         act(wide("sg", h), bank(2 + h), F.Sign, scale=-1.0, bias=2.0 ** -40)
-        at(6900 + 100 * h, "V")
+        at(5500 + 100 * h, "V")
         act(wide("Z0", h), bank(2 + h), F.Identity, scale=-8.0)
     tw = lv = lvl = fr = None
 
@@ -422,19 +432,17 @@ def plan(T, g, core, topo):
         e = float(4 >> t)
         last = t == 2
         r0, r1 = STEP * t - 2500, STEP * t + STEP - 2500
+        at(r0 + 4700 if t else 8000)
+        for a, b in H if not t else [(0, 1024)]:
+            act(v("X", a, b), ind(v("XT", 0, 4608), sub(hx, a // 16, b // 16)), F.Identity)
+        for r, a, b, a2 in ((6, 0, 1024, 0), (14, 0, 512, 1024), (14, 512, 1024, 1024)):
+            x, y = v("X", a, b, 1, (r, 128, 16)), v("raw", a2, a2 + b - a, 1, (0, 8, 1))
+            dma("Y", ap(x), ap(y), [y], [x], 2200)
         if t:
-            at(r0 + 4700)
-            act(full("X"), ind(v("XT", 0, 4608), hx), F.Identity)
-            lanes = v("X", 0, 1024, 1, (6, 128, 8))
-            dma("Y", ap(lanes), T.IDT[6::8, :], [full("IDT")], [lanes], 2200)
             for h in range(2):
                 at(r0 + 6500 + 1000 * h)
                 act(wide("sg", h), wide(zn, h), F.Sign, bias=2.0 ** -40)
                 step(wide("dd", h), wide(zn, h), True)
-        else:
-            at(8700)
-            for h in range(2):
-                tt(wide("X", h), ind(v("XT", 0, 4608), half(hx, h)), wide("IDT", h), A.mult)
         for h in range(2):
             at(r0 + 8800 + 500 * h)
             mm(bank(h), [(ONES, wide("sg", h)), (MD, wide("dd", h))])
@@ -486,8 +494,8 @@ def plan(T, g, core, topo):
             off1 = ts(new("PU"), tt(p(), bb, base1, A.min), float(B), A.add)
         off2 = ts(new("PU"), tt(f() if not t else p(), bb, base2, A.min), float(FREE + B), A.add)
         at(r1 - 4100)
-        add("V", (lambda RW, off1: lambda: g.vector.tensor_tensor(ap(v(RW, PAR, RN)).indirect(ap(off1)), ap(full("X")), ap(full("W")), A.mult))(RW, off1),
-            [full("X"), full("W"), off1], [v(RW, PAR, RN)], 60 + 1024 * 3.8)
+        for a, b in H if t else [(0, 1024)]:
+            scatter(v(RW, PAR, RN), sub(off1, a // 16, b // 16), v("X", a, b), v("W", a, b))
         for h in range(2):
             at(r1, "SV"[h])
             act(wide("RG", h), ind(v(RW, 0, RN), half(off2, h)), F.Identity)
@@ -499,14 +507,14 @@ def plan(T, g, core, topo):
         lw = act(new("PB"), wrap(bank(7, 192, 64), ZM[LW], full("W")), F.Identity)
         df, rt = wrap(bank(7, 128, 64), ZM[DF], full("X")), wrap(bank(7, 256, 64), ZM[RT], full("X"), [(IDB, fr)])
         dj = wrap(bank(7, 320, 64), ZM[DJ], full("X"), [(ID, nsb)])
-        if t:
+        if t == 1:
             co = mm(bank(7, 384, 64), [(ID, lw), (NID, nsb)])
         at(r1 + 500)
         qw = tt(f(), rt, tt(f(), df, lw, A.mult), A.add)
         sj = ts(f(), dj, 0.0, A.is_equal)
-        if t:
+        if t == 1:
             co = tt(f(), co, lane1k, A.add)
-        at(r0 + (7600 if t else 9600))
+        at(r0 + (7600 if t else 9000))
         tt(full(CW, REST), ind(v("KT", 0, 4608), hx), full(zn), A.mult)
         at(r0 + 11500)
         act(full(CW, LEFT), full("sg"), F.Identity, bias=(MARK - e) / 2, scale=-(MARK + e) / 2)
@@ -517,7 +525,7 @@ def plan(T, g, core, topo):
         q = wrap(bank(0, 0, 64), ZM[QO], full("RG"), [(IDB, occ)])
         jn = wrap(bank(1, 0, 64), ZM[JN], full("RG"), [(ID, nsb), (ID, CM)])
         tn = wrap(bank(6, 448, 64), ZM[TW], full("RG"))
-        if t:
+        if t == 1:
             cw = wrap(bank(7, 448, 64), ZM[CP], full("RG"), [(ID, nsb), (ID, CM)])
         at(r1 + 2200)
         q = tt(new("PI"), q, qw, A.max)
@@ -543,15 +551,15 @@ def plan(T, g, core, topo):
         at(r1 + 3300)
         fuse = tt(f(), tt(p(), jn, jq, A.is_equal), sj, A.max)
         at(r1 + (5400 if t else 3500))
-        if t:
+        if t == 1:
             cw = tt(p(), cw, co, A.max)
-        else:
+        elif t == 0:
             cw = tt(p(), ts(p(), lo, 2.0, A.mult, float(LEFT + RIGHT), A.add), si, A.subtract)
-        sz = cp(new("PU"), tt(p(), cw, fuse, A.mult))
-        for h in range(2):
-            at(r1 + (5600 if t else 4000) + 1000 * h)
-            tt(wide("Z", h), ind(v(CW, 0, 4096), half(sz, h)), wide("G1", h), A.min)
-        ops[-1]["goal"] = True
+        if not last:
+            sz = cp(new("PU"), tt(p(), cw, fuse, A.mult))
+            for h in range(2):
+                at(r1 + (5600 if t else 4000) + 1000 * h)
+                tt(wide("Z", h), ind(v(CW, 0, 4096), half(sz, h)), wide("G1", h), A.min)
         at(r1 + 4400)
         gt = tt(f() if last else p(), tn, lane16, A.is_gt)
         nup = tt(f(), fuse, gt, A.is_le)
@@ -604,26 +612,38 @@ def plan(T, g, core, topo):
             for h in range(2):
                 act(wide("DG", h), ind(v("DT", 0, 4608), half(hp, h)), F.Identity)
                 step(wide("MG", h), wide("G1", h), True)
-                act(wide("FM", h), mm(bank(2 + h), [(ID, wide("DG", h)), (IDB, wide("MG", h))]), F.Sigmoid)
-        else:
+                act(bank(2 + h) if PICK[t] else wide("FM", h), mm(bank(2 + h), [(ID, wide("DG", h)), (IDB, wide("MG", h))]), F.Sigmoid)
+        if PICK[t]:
+            act(full("Y2"), ind(aw, sm), F.Identity)
+        if not SPARE[t]:
             act(full("FP"), ind(v("DT", 0, 4608), hp), F.Sigmoid)
             for h in range(2):
                 step(bank(2 + h), wide("G1", h), False)
             at(r1 + (7500 if last else STEP + 600))
             for h in range(2):
-                tt(wide("FM", h), wide("FP", h), bank(2 + h), A.mult)
+                tt(bank(2 + h) if PICK[t] else wide("FM", h), wide("FP", h), bank(2 + h), A.mult)
         at(r1 + (7600 if last else STEP + 700))
-        for h in range(2):
-            tt(wide(an, h, 16), ind(aw, half(sm, h)), wide("FM", h), A.mult)
+        if PICK[t]:
+            for h in range(2):
+                tt(wide(an, h, 16), wide("Y2", h), bank(2 + h), A.mult)
+        else:
+            tt(full(an, 16), ind(aw, sm), full("FM"), A.mult)
         if last:
+            at(r1 + 6000)
+            for h in range(2):
+                tt(wide("AW1", h, 16), wide("G1", h), bank(2 + h), A.mult)
+            at(r1 + 8000)
+            for h in range(2):
+                act(wide("Z", h), ind(v("AW1", 0, 1040), half(so, h)), F.Identity)
+                tt(wide("Y2", h), ind(v("AW1", 0, 1040), half(sb, h)), wide("Z", h), A.add)
+                dma("Y", T.yc[:, H[h][0]:H[h][1]], ap(wide("Y2", h)), [wide("Y2", h)], [], 2400)
             for h in range(2):
                 at(r1 + 10000 + 100 * h)
                 act(wide("FP", h), ind(v(an, 0, 1040), half(so, h)), F.Identity)
                 tt(wide("FM", h), ind(v(an, 0, 1040), half(sb, h)), wide("FP", h), A.add)
-                tt(wide("Y1", h), ind(v("KT", 0, 4096), half(h16, h)), wide("FM", h), A.mult)
-                dma("Y", T.ya[:, H[h][0]:H[h][1]], ap(wide("Y1", h)), [wide("Y1", h)], [], 2400)
-                tt(wide("Y2", h), wide("Z", h), act(bank(h), wide("FM", h), F.Sign), A.mult)
-                dma("S", T.yc[:, H[h][0]:H[h][1]], ap(wide("Y2", h)), [wide("Y2", h)], [], 2400)
+                for a, b in ((512, 832), (832, 1024)) if h else ((0, 512),):
+                    tt(v("Y1", a, b), ind(v("KT", 0, 4096), sub(h16, a // 16, b // 16)), v("FM", a, b), A.mult)
+                    dma("Y", T.ya[:, a:b], ap(v("Y1", a, b)), [v("Y1", a, b)], [], 2000 + b - a)
             break
         bc, ba = "bc%d" % (t + 1), "ba%d" % (t + 1)
         at(r1 + 13300)
@@ -640,7 +660,7 @@ def plan(T, g, core, topo):
     return ops
 
 
-HOP, TRIES, HEAT, SEED, FOUND = 120, 30000, 120.0, 1, {}
+HOP, TRIES, MOVES, HEAT, SEED, FOUND = 120, 3000, 120000, 110.0, 1, {}
 PULL, PULL2, BACK, RESET = 1e-4, 0.1, 0.97, 0.02
 
 
@@ -652,7 +672,7 @@ def meet(a, b):
     if a[4] and b[4]:
         if a[4][1] <= b[4][0] or b[4][1] <= a[4][0]:
             return False
-        if a[4][2] == b[4][2] and (a[4][0] - b[4][0]) % a[4][2]:
+        if not set(range(*a[4])) & set(range(*b[4])):
             return False
     return True
 
@@ -689,39 +709,42 @@ def edges(ops):
 def place(seq, cut, key, fore, how, banks, first, start, end):
     start, end, key = list(start), list(end), list(key)
     line = {q: ([], []) for q in "VSPGYR"}
-    held = {}
-    for j in sorted(seq[:cut], key=lambda i: start[i]):
-        S, E = line[how[j][0]]
-        S.append(start[j])
+    held = {"P%d" % b: [] for b in range(8)}
+    for s, j in sorted([(start[j], j) for j in seq[:cut]]):
+        q = how[j][0]
+        S, E = line[q]
+        S.append(s)
         E.append(end[j])
         for b in banks[j]:
-            held.setdefault(b, []).append((start[j], end[j], how[j][0]))
-    todo = seq[cut:]
-    for j in todo:
+            held[b].append((s - HOP, end[j] + HOP, q))
+    todo = []
+    for j in seq[cut:]:
+        x = key[j]
         for i, d in fore[j]:
-            if key[i] >= key[j]:
-                key[j] = key[i] + 1e-3
-    todo.sort(key=lambda i: key[i])
-    for j in todo:
+            if key[i] >= x:
+                x = key[j] = key[i] + 1e-3
+        todo.append((x, j))
+    todo.sort()
+    for x, j in todo:
         s = first[j]
         for i, d in fore[j]:
             if end[i] + d > s:
                 s = end[i] + d
         q, ns = how[j]
         S, E = line[q]
-        k = len(S)
+        k = m = len(S)
         while k and E[k - 1] > s:
             k -= 1
         while True:
-            while k < len(S) and S[k] < s + ns:
+            while k < m and S[k] < s + ns:
                 if E[k] > s:
                     s = E[k]
                 k += 1
             s0 = s
             for b in banks[j]:
-                for a, z, q2 in held.get(b, ()):
-                    if q2 != q and a < s + ns + HOP and z + HOP > s:
-                        s = z + HOP
+                for a, z, q2 in held[b][-24:]:
+                    if z > s and a < s + ns and q2 != q:
+                        s = z
             if s == s0:
                 break
         while k and S[k - 1] > s:
@@ -729,9 +752,118 @@ def place(seq, cut, key, fore, how, banks, first, start, end):
         S.insert(k, s)
         E.insert(k, s + ns)
         for b in banks[j]:
-            held.setdefault(b, []).append((s, s + ns, q))
-        start[j], end[j] = s, s + ns
-    return start, end, key, seq[:cut] + todo
+            held[b].append((s - HOP, s + ns + HOP, q))
+        start[j] = s
+        end[j] = s + ns
+    return start, end, key, seq[:cut] + [j for x, j in todo]
+
+
+def polish(ops, pre, start, how, banks):
+    n, gap = len(ops), 24
+    rng = np.random.RandomState(SEED)
+    up, down = [list(e) for e in pre], [[] for _ in ops]
+    for j in range(n):
+        for i in up[j]:
+            down[i].append(j)
+    alt = [list(o["alt"]) if "alt" in o else None for o in ops]
+    flex, outs, big = [i for i in range(n) if alt[i]], [i for i in range(n) if not down[i]], [i for i in range(n) if "sca" in ops[i]]
+    how = [x[0] for x in how]
+    cases = []
+    for gather, scatter, slow, hop, pool, issue in GUESSES:
+        lat = [o.get("lat", 0) * slow for o in ops]
+        ns = [{q: x[1] + o.get("ind", 0) * (gather - GATHER) + o.get("sca", 0) * (scatter - SCATTER) + pool * (q == "G")
+               + issue * (q in "YS" and "lat" in o) for q, x in o.get("alt", {o["q"]: (0, o["ns"])}).items()} for o in ops]
+        cases.append((ns, [[(i, lat[i] + hop if pre[j][i] else 0) for i in pre[j]] for j in range(n)], lat, hop))
+
+    def run(seq, how, a, states):
+        c, new = a // gap, []
+        for (dur, fore, lat, hop), (end, marks) in zip(cases, states):
+            free, held = dict(marks[c][0]), dict(marks[c][1])
+            end, marks = list(end), marks[:c + 1]
+            for k in range(c * gap, n):
+                if k % gap == 0 and k > c * gap:
+                    marks.append((dict(free), dict(held)))
+                j = seq[k]
+                q = how[j]
+                s = free[q]
+                for i, d in fore[j]:
+                    if end[i] + d > s:
+                        s = end[i] + d
+                for b in banks[j]:
+                    z, q2 = held[b]
+                    if q2 != q and z > s:
+                        s = z
+                s += dur[j][q]
+                for b in banks[j]:
+                    held[b] = (s + hop, q)
+                free[q] = end[j] = s
+            new.append((end, marks))
+        return new
+
+    seq = sorted(range(n), key=lambda i: (start[i], i))
+    now = top = pos = None
+    state = run(seq, how, 0, [([0.0] * n, [({q: 0.0 for q in "VSPGYR"}, {"P%d" % b: (0.0, "P") for b in range(8)})]) for c in cases])
+    held = []
+    for k, u in enumerate(rng.rand(MOVES, 6).tolist()):
+        sq, hw, st = seq, how, state
+        if k:
+            if u[0] < 0.75 and held:
+                (i, j), m = held[int(u[1] * len(held))], int(u[2] * 4)
+            elif u[0] < 0.85:
+                i = j = flex[int(u[1] * len(flex))]
+                m = 2
+            else:
+                a = int(u[1] * (n - 1))
+                i, j, m = seq[a], seq[min(n - 1, a + 1 + int(u[2] * u[2] * 60))], int(u[0] * 1000) % 2
+            if m >= 2 and alt[(i, j)[m - 2]]:
+                x = (i, j)[m - 2]
+                hw = list(how)
+                hw[x] = alt[x][int(u[3] * len(alt[x]))]
+                if hw[x] == how[x]:
+                    continue
+                a = pos[x]
+            else:
+                m, a, b = m % 2, pos[i], pos[j]
+                got, todo = {(j, i)[m]}, [(j, i)[m]]
+                while todo:
+                    for w in (up, down)[m][todo.pop()]:
+                        if a <= pos[w] <= b and w not in got:
+                            got.add(w)
+                            todo.append(w)
+                if a >= b or (i, j)[m] in got:
+                    continue
+                inn, out = [w for w in seq[a:b + 1] if w in got], [w for w in seq[a:b + 1] if w not in got]
+                sq = seq[:a] + (out + inn if m else inn + out) + seq[b + 1:]
+            st = run(sq, hw, a, state)
+        val = PULL * sum(st[0][0])
+        for case, (en, marks) in zip(cases, st):
+            val += (max([en[i] + case[2][i] for i in outs]) + PULL2 * sum([en[i] for i in big])) / len(cases)
+        if now is None or val <= now - HEAT * (1.01 - k / MOVES) ** 2 * math.log(u[4]):
+            now, seq, how, state = val, sq, hw, st
+            if u[3] < 0.03:
+                seq = sorted(seq, key=lambda i: st[0][0][i] - cases[0][0][i][hw[i]])
+                state = run(seq, how, 0, state)
+            if top is None or val < top[0]:
+                top = (val, seq, [state[0][0][i] - cases[0][0][i][hw[i]] for i in range(n)], hw)
+            pos = [0] * n
+            for a, i in enumerate(seq):
+                pos[i] = a
+            (dur, fore, lat, hop), end = cases[int(u[5] * len(cases))], state[int(u[5] * len(cases))][0]
+            j, held = max(outs, key=lambda i: end[i] + lat[i]), []
+            while j is not None:
+                s, nx = end[j] - dur[j][how[j]] - 0.5, None
+                for i, d in fore[j]:
+                    if end[i] + d > s:
+                        nx = i
+                a, q = pos[j] - 1, how[j]
+                while nx is None and s > 0 and a >= 0:
+                    i = seq[a]
+                    if end[i] > s and how[i] == q or end[i] + hop > s and how[i] != q and set(banks[i]) & set(banks[j]):
+                        nx = i
+                        held.append((i, j))
+                    a -= 1
+                j = nx
+    return top
 
 
 def order(ops):
@@ -758,7 +890,7 @@ def order(ops):
             tail[i] = how[i][1] + max([tail[j] + d for j, d in back[i]] + [lat[i]])
         key, zero = [float(o["when"]) for o in ops], [0.0] * n
         now = top = None
-        big = [i for i in range(n) if ops[i]["ns"] > 3000]
+        big = [i for i in range(n) if ops[i]["q"] == "V" and ops[i]["ns"] > 1900]
         held, seq, begins, ends = [], list(range(n)), zero, zero
         for k in range(TRIES):
             ky, hw, u = list(key), list(how), float(rng.rand())
@@ -818,12 +950,11 @@ def order(ops):
                         nx = [i for i in before[j] if en[i] + HOP > st[j] - 0.5]
                         held += [(i, j) for i in nx[:1]]
                     j = nx[0] if nx else None
-        FOUND[n] = top
-    start = FOUND[n][1]
-    for o, (q, ns) in zip(ops, FOUND[n][2]):
+        FOUND[n] = polish(ops, pre, top[1], top[2], banks)
+    seq, start = FOUND[n][1:3]
+    for o, q in zip(ops, FOUND[n][3]):
         if "alt" in o:
-            o["q"], o["fn"], o["ns"] = q, o["alt"][q][0], ns
-    seq = sorted(range(n), key=lambda i: (start[i], i))
+            o["q"], o["fn"], o["ns"] = q, o["alt"][q][0], o["alt"][q][1]
     last = {}
     for j in seq:
         for b in banks[j]:

import math
import numpy as np
from concourse.bass import DstId, RemoteDMATransfer
from concourse.mybir import AluOpType as A, AxisListType, ActivationFunctionType as F

NF, NI, NU, NB = 100, 40, 40, 60
B = 8191
PAR, FREE, NONE, LANE, RN = 256, 1280, 2304, 2320, 3344
ARR, LEFT, RIGHT, REST = 16, 1024, 2048, 3072
MARK, THR = 1024.0, 32.0
SCRATCH = {
    "KT": ("sbuf", [128, 4624], "bfloat16"), "DT": ("sbuf", [128, 4608], "bfloat16"), "XT": ("sbuf", [128, 4608], "bfloat16"),
    "cmp": ("sbuf", [128, 512], "int32"), "ci": ("sbuf", [128, 512], "float32"), "cb": ("sbuf", [128, 1024], "bfloat16"),
    "pl": ("sbuf", [128, 64], "int32"),
    "AW1": ("sbuf", [128, 1296], "float32"), "AW2": ("sbuf", [128, 1296], "float32"), "AW3": ("sbuf", [128, 1040], "float32"),
    "MT": ("sbuf", [128, 144 * 3 + 128 * 6], "bfloat16"), "ZZ": ("sbuf", [128, 144 * 11], "bfloat16"),
    "Q": ("sbuf", [128, 160], "float32"), "QG": ("sbuf", [128, 144], "float32"), "SF": ("sbuf", [128, 128], "float32"),
    "WR": ("sbuf", [128, 320], "bfloat16"), "OH": ("sbuf", [128, 144 + 256], "bfloat16"), "raw": ("sbuf", [128, 1536], "bfloat16"),
    "col": ("sbuf", [128, 96], "float32"), "coi": ("sbuf", [128, 8], "int32"),
    "st": ("sbuf", [128, 64 * 4], "float32"), "Pc": ("sbuf", [128, 136], "float32"), "CB": ("sbuf", [128, 64 * 6], "bfloat16"),
    "junk": ("sbuf", [128, 1024], "bfloat16"),
    "PF": ("sbuf", [128, 64 * NF], "float32"), "PI": ("sbuf", [128, 64 * NI], "int32"),
    "PU": ("sbuf", [128, 64 * NU], "uint16"), "PB": ("sbuf", [128, 64 * NB], "bfloat16"),
}
SPARE, PICK, STEP, LAT = [False, False, False], [False, False, False], 18500, 0.6
GATHER, SCATTER = 1.56, 3.8
GUESSES = [(1.56, 3.8, 1.0, 120, 0, 0), (2.0, 5.4, 0.9, 100, 0, 0), (1.25, 2.6, 1.6, 170, 200, 250)]
for _n in ("am", "cr", "Z0", "sg", "dd", "X", "W", "RG", "DG", "MG"):
    SCRATCH[_n] = ("sbuf", [128, 1024], "bfloat16")
for _n in ("Z", "G1", "FP", "FM", "Y1", "Y2"):
    SCRATCH[_n] = ("sbuf", [128, 1024], "float32")
for _t in range(3):
    SCRATCH["CW%d" % _t] = ("sbuf", [128, 4096], "float32")
    SCRATCH["RW%d" % _t] = ("sbuf", [128, RN], "bfloat16")
for _t in (1, 2):
    SCRATCH["cs%d" % _t] = SCRATCH["cn%d" % _t] = ("sbuf", [128, 4], "float32")
    SCRATCH["bc%d" % _t] = SCRATCH["ba%d" % _t] = ("sbuf", [128, 256], "float32")
    SCRATCH["br%d" % _t] = ("sbuf", [128, 384], "bfloat16")
for _b in range(8):
    SCRATCH["P%d" % _b] = ("psum", [128, 512], "float32")
NDMA = 48
SEMAPHORES = ["V", "S", "P", "G", "sent"] + ["d%d" % _k for _k in range(NDMA)] + ["rc1", "rc2", "rr1", "rr2", "rd1", "rd2", "ra1", "ra2"]

SC, BI, BX, AB, LW, DF, RT, DJ, QO, JN, TW, CP, GS, GB, PO = range(15)
NW = 15
K4, M4, ROUND = 4096, 1 << 22, 1.5 * 2 ** 27
WEIGHTS = {
    AB: {5: 1, 7: 1}, LW: {1: 1024},
    DF: {0: 2 ** -10, 2: 2 ** -10, 4: -2 ** -10, 10: -2 ** -10, 1: -K4},
    RT: {4: 1, 10: 1, 6: K4, 14: K4, 1: -M4, 3: 3 * M4},
    DJ: {0: 1, 4: -1},
    QO: {0: 1, 2: 1, 4: 1, 10: 1, 6: K4, 14: K4, 9: K4, 11: K4, 1: M4, 3: M4},
    JN: {8: 1, 12: 1, 3: K4}, TW: {6: 1, 14: 1, 3: 16},
    CP: {6: 1, 14: 1, 3: 7168, 1: -1024, 13: -1024},
    SC: {4: 256, 8: 256, 10: 256, 1: 256, 0: -256, 12: -256, 2: -256, 5: 128, 7: -128, 15: None},
    BI: {4: 128, 8: 128, 10: 128, 1: 128, 0: -128, 12: -128, 2: -128, 5: 1920, 7: 1920, 6: 128, 14: 128, 3: 128,
         9: -128, 11: -128, 13: 128, 15: None},
    BX: {0: 3584, 4: 3584, 8: 3584, 12: 3584, 3: 1, 6: None, 14: None, 5: None, 7: None, 9: None, 11: None, 15: None},
    GS: {0: 1, 2: 1}, GB: {0: -3584}, PO: {9: 16},
}


def cover(w):
    at = {NW * r + z: x for z in w for r, x in w[z].items()}
    vals = sorted(set(at.values()) - {None}, key=lambda x: (-list(at.values()).count(x), x))
    runs = []
    for k, x in enumerate(vals):
        need = {i for i in at if at[i] == x}
        free = {i for i in at if at[i] is None or at[i] in vals[k:]}
        while need:
            best = (0,)
            for a in sorted(need):
                for d in range(1, 16 * NW):
                    b, hit, last = a, 0, a
                    while b in free:
                        if b in need:
                            hit, last = hit + 1, b
                        b += d
                    best = max(best, (hit, a - last, a, last, -d))
            runs.append((best[2], best[3] + 1, -best[4], x))
            need -= set(range(best[2], best[3] + 1, -best[4]))
    return runs


EARLY = 4
RUNS = cover({z: WEIGHTS[z] for z in range(EARLY)}) + cover({z: WEIGHTS[z] for z in range(EARLY, NW)})


def v(name, c0, c1, step=1, p=None):
    return (name, c0, c1, step, p)


def sub(x, a, b, step=1):
    return (x[0], x[1] + a, x[1] + b, step, x[4])


def width(x):
    return (x[2] - x[1] + x[3] - 1) // x[3]


def plan(T, g, core, topo):
    ops, tag, when = [], [0], [0, "S"]
    rank = T.rank_of(core)
    nxt = T.cores[(rank + 1) % len(T.cores)]
    rid, pid = topo.addr(nxt)[0], topo.addr(nxt)[1]
    eng = topo.engines(core, nxt)

    def bits(es):
        m = 0
        for e in es:
            m |= 1 << e
        return m

    def ap(x):
        if not isinstance(x, tuple):
            return x
        p = x[4] or (0, 128, 1)
        ps = slice(p[0], p[1], p[2]) if p[2] != 1 else slice(p[0], p[1])
        cs = slice(x[1], x[2], x[3]) if x[3] != 1 else slice(x[1], x[2])
        return T[x[0]][ps, cs]

    def src(x):
        return ap(x[1]).indirect(ap(x[2])) if x[0] == "ind" else ap(x)

    def ind(win, off):
        return ("ind", win, off)

    def parts(*xs):
        r = []
        for x in xs:
            if isinstance(x, tuple):
                r += [x[1], x[2]] if x[0] == "ind" else [x]
        return r

    def two(x):
        return SCRATCH[x[0]][2] in ("bfloat16", "uint16")

    def psum(x):
        return SCRATCH[x[0]][0] == "psum"

    def add(q, fn, rd, wr, ns, **kw):
        o = {"q": q, "fn": fn, "rd": rd, "wr": wr, "ns": ns, "tag": tag[0], "when": when[0]}
        when[0] += 10
        o.update(kw)
        ops.append(o)
        return o

    def either():
        b = ops.pop()
        a = ops[-1]
        a.setdefault("alt", {a["q"]: (a["fn"], a["ns"])})[b["q"]] = (b["fn"], b["ns"])
        if b["q"] == when[1]:
            a["q"], a["fn"], a["ns"] = b["q"], b["fn"], b["ns"]

    def at(ns, q="S"):
        when[0], when[1] = ns, q
        tag[0] += 1

    def vns(out, a, b=None):
        if a[0] == "ind":
            return 60 + width(out) * GATHER
        n = width(out)
        if b is not None:
            return 60 + max(64, n * (1 if psum(a) or psum(b) else 2))
        return 60 + max(64, n * (0.5 if two(a) and two(out) else 1))

    def ts(out, a, s1, op0, s2=None, op1=None):
        if op1 is None:
            fn = lambda: g.vector.tensor_scalar(ap(out), src(a), ap(s1), None, op0)
        else:
            fn = lambda: g.vector.tensor_scalar(ap(out), src(a), ap(s1), ap(s2), op0, op1)
        add("V", fn, parts(a, s1, s2), [out], vns(out, a))
        return out

    def tt(out, a, b, op):
        add("V", lambda: g.vector.tensor_tensor(ap(out), src(a), ap(b), op), parts(a, b), [out], vns(out, a, b), ind=width(out) * (a[0] == "ind"))
        return out

    def scatter(win, off, a, b):
        add("V", lambda: g.vector.tensor_tensor(ap(win).indirect(ap(off)), ap(a), ap(b), A.mult), [a, b, off], [win], 60 + width(a) * SCATTER, sca=width(a))

    def cp(out, a):
        add("V", lambda: g.vector.tensor_copy(ap(out), src(a)), parts(a), [out], vns(out, a))
        return out

    def fill(out, c):
        add("V", lambda: g.vector.memset(ap(out), c), [], [out], 60 + max(64, width(out) * (0.5 if two(out) else 1)))
        return out

    def scan(out, a):
        one = sub(ONE, 0, width(a))
        add("V", lambda: g.vector.tensor_tensor_scan(ap(out), ap(one), ap(a), 0.0, A.mult, A.add), [one, a], [out], 60 + max(64, width(a) * 0.5))
        return out

    def act(out, a, f, bias=None, scale=None, acc=None):
        kw = {}
        if bias is not None:
            kw["bias"] = ap(bias)
        if scale is not None:
            kw["scale"] = ap(scale)
        if acc is not None:
            kw["accum_out"] = ap(acc)
        add("S", lambda: g.scalar.activation(ap(out), src(a), f, **kw), parts(a, bias, scale), [out] + parts(acc),
            80 + max(64, width(out) * (GATHER if a[0] == "ind" else 1)), ind=width(out) * (a[0] == "ind"), sig=f == F.Sigmoid)
        if f == F.Identity:
            ts(out, a, 1.0 if scale is None else scale, A.mult, 0.0 if bias is None else bias, A.add)
            either()
        return out

    def step(out, a, up):
        act(out, a, F.Sigmoid, scale=8.0 if up else -8.0, bias=-8 * THR if up else 8 * THR)
        ts(out, a, THR, A.is_ge if up else A.is_lt)
        either()
        return out

    def mm(out, pairs, slow=1):
        def fn():
            for k, (l, r) in enumerate(pairs):
                i = g.tensor.matmul(ap(out), ap(l), ap(r), k == 0, k == len(pairs) - 1)
            return i
        add("P", fn, [x for pr in pairs for x in pr], [out], 30 + len(pairs) * (6 + max(64, width(out)) * slow))
        return out

    def wrap(out, z, wide, more=()):
        n = width(wide)
        return mm(out, list(more) + [(sub(z, 15 - i, 143 - i), sub(wide, i, n, 16)) for i in range(16)])

    def iota(out, pat, base, cm):
        kw = {} if SCRATCH[out[0]][2] == "int32" else {"allow_small_or_imprecise_dtypes": True}
        add("G", lambda: g.iota(ap(out), pat, base, cm, **kw), [], [out], 330 + 2 * width(out))
        return out

    def select(out, a, pat, op, other, base, cm):
        add("G", lambda: g.affine_select(ap(out), ap(a), pat, op, other, base, cm), [a], [out], 380 + 2 * width(out))
        return out

    def const(out, c):
        iota(out, [[0, width(out)]], int(c), 0)
        fill(out, float(c))
        either()
        return out

    nd = [0]

    def dma(q, out, a, rd, wr, lat):
        k = nd[0]
        nd[0] += 1
        if q == "G":
            return add(q, lambda: g.dma_start(out, a, accum_op=A.add), rd + wr, wr, 1100, sem="d%d" % k, inc=16, lat=lat * LAT)
        e = g.sync if q == "Y" else g.scalar
        return add(q, lambda: e.dma_start(out, a), rd, wr, 150, sem="d%d" % k, inc=16, lat=lat * LAT)

    def send(d, s, es, rsem):
        add("G", lambda: g.remote_dma(ap(d), ap(s), T.sem[rsem], T.sem.sent, pid, rid, bits(es)), [s], [], 600, sent=len(es))
        add("R", None, [], [d], 0, sem=rsem, inc=len(es), lat=2200 * LAT, after=len(ops) - 1)

    ring = {"PF": 0, "PI": 0, "PU": 0, "PB": 0, "col": 40}

    def new(pool, n=64):
        x = v(pool, 64 * ring[pool], 64 * ring[pool] + n)
        ring[pool] += (n + 63) // 64
        return x

    def f():
        return new("PF")

    slot = [0]

    def p(n=64):
        if slot[0] + n > 512:
            slot[0] = 0
        slot[0] += n
        return v("P4", slot[0] - n, slot[0])

    def c():
        ring["col"] += 1
        return v("col", ring["col"] - 1, ring["col"])

    H = [(0, 512), (512, 1024)]

    def wide(name, h, base=0):
        return v(name, base + H[h][0], base + H[h][1])

    def full(name, base=0):
        return v(name, base, base + 1024)

    def half(off, h):
        return sub(off, 32 * h, 32 * h + 32)

    def bank(b, a=0, n=512):
        return v("P%d" % b, a, a + n)

    dma("Y", T.cmp[:, 0:256], T.lf[:, :], [], [v("cmp", 0, 256)], 2300)
    dma("Y", T.cmp[:, 256:512], T.rt[:, :], [], [v("cmp", 256, 512)], 2300)
    dma("S", T.am[:, :], T.amp[:, :], [], [full("am")], 2500)
    dma("S", T.cr[:, :], T.cro[:, :], [], [full("cr")], 2600)
    for b in range(2):
        for u in range(2):
            a = 32 * b + 16 * u
            dma("Y", T.pl[:, a:a + 16], T.place[u::2, 512 * b:512 * b + 512], [], [v("pl", a, a + 16)], 2400)
    dma("S", T.KT[:, 0:4096], T.kap[:, :], [], [v("KT", 0, 4096)], 4300)
    dma("S", T.DT[:, 0:4096], T.dam[:, :], [], [v("DT", 0, 4096)], 5800)

    at(300)
    fill(full("W"), 1.0)
    for r, d in ((1, 4), (3, 4), (6, 8)):
        x, y = v("XT", 0, 4096, 1, (r, 128, d)), v("W", 0, 4096 // d)
        dma("Y", ap(x), ap(y), [y], [x], 3000)
    p0 = (0, 1, 1)
    at(200)
    fill(v("WR", 0, 16 * NW, 1, p0), 0.0)
    for k, (a, b, d, w) in enumerate(RUNS):
        x = v("WR", a, b, d, p0)
        at(1000 if a % NW < EARLY else 8000 + 100 * k, "SG"[a % NW >= EARLY])
        act(x, x, F.Identity, scale=0.0, bias=float(w))
        if w == int(w):
            iota(x, [[0, width(x)]], int(w), 0)
            either()
    at(100)
    fill(v("OH", 0, 400, 1, p0), 0.0)
    for a, b, d in ((15, 144, 16), (144, 272, 4), (274, 400, 8)):
        if a == 15:
            act(v("OH", a, b, d, p0), v("OH", a, b, d, p0), F.Sigmoid, bias=128.0)
            ops[-1]["ns"] += 1500
        else:
            act(v("OH", a, b, d, p0), v("OH", a, b, d, p0), F.Identity, bias=1.0)
    row = [v("OH", 15 - r, 143 - r, 1, p0) for r in range(16)]
    rows_hi, rows_lo = v("OH", 144, 272, 1, p0), v("OH", 272, 400, 1, p0)
    for a, b in ((0, EARLY), (EARLY, NW)):
        at(13500 if a else 4500)
        mm(bank(5, a, b - a), [(row[r], v("WR", NW * r + a, NW * r + b, 1, p0)) for r in range(16)])
        act(v("col", 16 + a, 16 + b), bank(5, a, b - a), F.Identity)
    Wt = [v("col", 16 + z, 17 + z) for z in range(NW)]
    pcol, icol, g16, g15 = [v("col", k, k + 1) for k in range(4)]
    at(1100)
    p32 = (0, 32, 1)
    iota(v("raw", 0, 512, 1, p32), [[16, 32], [0, 16]], 0, 0)
    iota(v("raw", 1024, 1536, 1, p32), [[0, 32], [1, 16]], 0, 0)
    hi0, lo0 = v("raw", 0, 512, 1, p0), v("raw", 1024, 1536, 1, p0)
    at(6000)
    act(v("raw", 512, 1024, 1, p32), v("raw", 0, 512, 1, p32), F.Identity, bias=512.0)
    iota(v("raw", 512, 1024, 1, p32), [[16, 32], [0, 16]], 512, 0)
    either()
    at(0)
    iota(pcol, [[0, 1]], 0, 1)
    iota(v("Q", 0, 16), [[1, 16]], 112, 0)
    Q, JW = iota(v("Q", 16, 160), [[1, 144]], 0, 0), v("Q", 16, 144)
    at(1000, "V")
    const(v("RW0", PAR, FREE), 0)
    cp(icol, ts(v("coi", 1, 2), iota(v("coi", 0, 1), [[0, 1]], 0, 1), 15, A.bitwise_and))
    act(g16, icol, F.Identity, scale=-1.0, bias=pcol)
    act(g15, g16, F.Identity, bias=15.0)
    const(v("QG", 0, 16), 112)
    iota(v("QG", 16, 144), [[16, 8], [0, 16]], 0, 0)
    at(7000)
    l16 = iota(v("st", 192, 256), [[16, 64]], 16, 0)
    lane16 = act(v("st", 0, 64), l16, F.Identity, bias=icol)
    lane1 = act(v("st", 64, 128), lane16, F.Identity, bias=float(LANE - PAR - 16 - B))
    at(13000)
    jb = act(v("col", 8, 16), sub(lane16, 0, 8), F.Identity, bias=-15.5)
    ones, ident, nones = [v("MT", 144 * k, 144 * k + 144) for k in range(3)]
    NUS, NBG, MD, NID, IDB, ID4 = [v("MT", 432 + 128 * k, 560 + 128 * k) for k in range(6)]
    ONES, SO, ID, SH, NON, NSO = [sub(m, a, a + 128) for m in (ones, ident, nones) for a in (16, 0)]
    at(7500)
    ONE, C64 = const(v("CB", 0, 128), 1), const(v("CB", 128, 192), 64)
    at(13000)
    CM, K7, K1 = const(v("CB", 192, 256), -20480), const(v("CB", 256, 257), 32 * (B - 1023)), const(v("CB", 258, 259), 4096)
    at(1500, "V")
    ts(ident, v("Q", 0, 144), pcol, A.is_equal)
    act(NID, ID, F.Identity, scale=-1.0)
    act(IDB, ID, F.Identity, scale=-2.0 ** 25)
    at(3000, "V")
    ts(ones, v("QG", 0, 144), g16, A.is_equal)
    act(nones, ones, F.Identity, scale=-1.0)
    act(MD, ONES, F.Identity, scale=-1.0)
    fill(sub(MD, 7, 128, 16), 0.0)
    act(sub(MD, 5, 128, 16), sub(ONES, 5, 128, 16), F.Identity, scale=-2.0)
    at(6000, "V")
    select(NUS, NON, [[-1, 128]], A.is_gt, 0.0, 0, 1)
    select(NBG, NUS, [[-1, 128]], A.not_equal, -(B + 1.0), 0, 1)
    ZS = ts(v("ZZ", 0, 144), Q, g15, A.is_equal)
    ZM = {}
    for z in range(AB, CP + 1):
        ZM[z] = act(v("ZZ", 144 * (z - AB + 1), 144 * (z - AB + 2)), ZS, F.Identity, scale=Wt[z])
        at(12600 + 10 * z)
    act(ID4, ID, F.Identity, scale=1008 / 4096.0)
    lane1k = act(v("st", 128, 192), lane16, F.Identity, bias=LEFT - 16.0)
    SF = act(v("SF", 0, 128), SH, F.Identity)
    at(6500)
    act(v("KT", 4096, 4608), wide("am", 0), F.Identity, scale=0.0, bias=0.5)
    at(16500)
    const(v("DT", 4096, 4608), 64)
    const(v("Pc", 128, 136), 0)
    for t in range(3):
        const(v("CW%d" % t, 0, 8), MARK)
        const(v("AW%d" % (t + 1), 0, 8), 0)
    at(5600)
    mm(bank(6), [(rows_hi, hi0), (rows_lo, lo0)])
    act(v("XT", 4096, 4608), bank(6), F.Identity, bias=Wt[BX])
    at(2300)
    act(wide("cb", 0), ts(v("ci", 0, 512), v("cmp", 0, 512), -7.5, A.add, ROUND, A.add), F.Identity, bias=-ROUND)
    for k, rows in enumerate(((0, 8, 4, 12), (2, 10))):
        if k:
            at(3900)
            tt(wide("cb", 1), v("cmp", 0, 512), wide("cb", 0), A.subtract)
        for j, r in enumerate(rows):
            a = 512 * k + 256 * (2 * j // len(rows))
            dma("Y", T.XT[r::16, 0:4096], T.cb[:, a:a + 256], [v("cb", a, a + 256)], [v("XT", 0, 4096, 1, (r, 128, 16))], 2600)
    at(7800)
    const(v("RW0", NONE, LANE), 0)

    at(4500)
    pf = cp(f(), v("pl", 0, 64))
    hf = f()
    add("V", lambda: g.vector.transpose(ap(hf), ap(pf)), [pf], [hf], 124)
    dr = ts(new("PB"), hf, 3584.0, A.is_ge, 512.0, A.mult)
    hx = cp(new("PU"), tt(f(), hf, dr, A.add))
    at(1700)
    ts(full("dd"), full("am"), 0.0, A.is_equal)
    for h in range(2):
        at(2400 + 1100 * h)
        mm(bank(2 + h), [(NID, wide("cr", h)), (IDB, wide("dd", h))])
        act(wide("sg", h), bank(2 + h), F.Sign, scale=-1.0, bias=2.0 ** -40)
        at(5500 + 100 * h, "V")
        act(wide("Z0", h), bank(2 + h), F.Identity, scale=-8.0)
    tw = lv = lvl = fr = None

    for t in range(3):
        CW, RW = "CW%d" % t, "RW%d" % t
        zn = "Z0" if t == 0 else "Z"
        aw = full("am") if t == 0 else v("AW%d" % t, 0, 1296)
        e = float(4 >> t)
        last = t == 2
        r0, r1 = STEP * t - 2500, STEP * t + STEP - 2500
        at(r0 + 4700 if t else 8000)
        for a, b in H if not t else [(0, 1024)]:
            act(v("X", a, b), ind(v("XT", 0, 4608), sub(hx, a // 16, b // 16)), F.Identity)
        for r, a, b, a2 in ((6, 0, 1024, 0), (14, 0, 512, 1024), (14, 512, 1024, 1024)):
            x, y = v("X", a, b, 1, (r, 128, 16)), v("raw", a2, a2 + b - a, 1, (0, 8, 1))
            dma("Y", ap(x), ap(y), [y], [x], 2200)
        if t:
            for h in range(2):
                at(r0 + 6500 + 1000 * h)
                act(wide("sg", h), wide(zn, h), F.Sign, bias=2.0 ** -40)
                step(wide("dd", h), wide(zn, h), True)
        for h in range(2):
            at(r0 + 8800 + 500 * h)
            mm(bank(h), [(ONES, wide("sg", h)), (MD, wide("dd", h))])
            act(wide("W", h), bank(h), F.Sigmoid, scale=Wt[SC], bias=Wt[BI])
        at(r0 + 10000)
        if t:
            ab = wrap(bank(7, 0, 64), ZM[AB], full("W"), [(NID, dr), (NID, fr)])
        else:
            ab = wrap(bank(7, 0, 64), ZM[AB], full("W"))
            at(r0 + 13000)
            fr = ts(new("PB"), ab, 0.5, A.is_lt)
        at(r0 + (9300 if t else 13100))
        occ = act(new("PB"), fr, F.Identity, scale=-1.0, bias=1.0)
        sc = scan(new("PB"), fr)
        js = mm(bank(5, 0, 64), [(ONES, C64), (NBG, fr), (ONES, sc)])
        fc = act(c(), mm(bank(5, 64, 1), [(ONES, sub(sc, 63, 64))]), F.Identity, bias=-float(B))
        base1 = tt(f(), js, lane1, A.min)
        more = []
        if t:
            at(r0 + 10200)
            ca, cb, c1, d1 = [v("cn%d" % t, k, k + 1) for k in range(4)]
            more = [(ID, act(new("PB"), sub(ONE, 0, 64), F.Identity, scale=B - 1023.0, bias=cb))]
            a1 = ts(new("PB"), js, ca, A.is_le, c1, A.mult)
            a2 = ts(new("PB"), js, cb, A.is_le, d1, A.mult)
            a4 = ts(new("PB"), js, cb, A.is_le, 4096.0, A.mult)
            base2 = tt(f(), mm(bank(5, 128, 64), [(NON, C64), (NBG, fr), (ONES, sc), (ID, a1), (NID, a2)]), tw, A.min)
            mm(bank(5, 256, 64), [(ID, dr), (ID, lv), (ID, a4)])
            mm(bank(5, 320, 64), [(ONES, sub(ONE, 0, 64)), (ID4, a4)])
            delta = bank(5, 256, 128)
            br = "br%d" % t
            at(r0 + 13200)
            gl = act(v(br, 256, 384), ind(full("X"), lvl), F.Identity, scale=Wt[GS], bias=Wt[GB])
            for k, m in enumerate((ID, SH)):
                mm(bank(6, 128 * k, 128), [(row[9], sub(hi0, 128 * k, 128 * k + 128)), (row[11], sub(lo0, 0, 128)), (m, gl)])
            act(v(br, 0, 256), bank(6, 0, 256), F.Identity, bias=Wt[PO])
            send(v(RW, 0, PAR), v(br, 0, 256), eng[0:4], "rr%d" % t)
        else:
            base2 = ts(f(), js, -2048.0, A.add, 1024.0 - B, A.min)
            delta = tt(f(), dr, occ, A.mult)
        at(r0 + (11000 if t else 13050))
        dis = ts(new("PB"), ab, 2.0, A.is_ge) if t else tt(new("PB"), ab, act(f(), dr, F.Identity, bias=2.0), A.is_ge)
        sc = scan(new("PB"), dis)
        xq = mm(bank(7, 64, 64), more + [(NBG, dis), (ONES, sc)])
        if not t:
            off1 = ts(new("PU"), tt(f(), xq, base1, A.min), float(B), A.add)
        nsb = ts(new("PB"), xq, fc, A.is_ge, 16384.0, A.mult)
        bb = tt(p(), xq, nsb, A.add) if not t else tt(f(), xq, nsb, A.add)
        if t:
            off1 = ts(new("PU"), tt(p(), bb, base1, A.min), float(B), A.add)
        off2 = ts(new("PU"), tt(f() if not t else p(), bb, base2, A.min), float(FREE + B), A.add)
        at(r1 - 4100)
        for a, b in H if t else [(0, 1024)]:
            scatter(v(RW, PAR, RN), sub(off1, a // 16, b // 16), v("X", a, b), v("W", a, b))
        for h in range(2):
            at(r1, "SV"[h])
            act(wide("RG", h), ind(v(RW, 0, RN), half(off2, h)), F.Identity)
        if t < 2:
            at(r1)
            const(v("RW%d" % (t + 1), PAR, FREE), 0)
            const(v("RW%d" % (t + 1), NONE, RN), 0)
        at(r1 - 4000)
        lw = act(new("PB"), wrap(bank(7, 192, 64), ZM[LW], full("W")), F.Identity)
        df, rt = wrap(bank(7, 128, 64), ZM[DF], full("X")), wrap(bank(7, 256, 64), ZM[RT], full("X"), [(IDB, fr)])
        dj = wrap(bank(7, 320, 64), ZM[DJ], full("X"), [(ID, nsb)])
        if t == 1:
            co = mm(bank(7, 384, 64), [(ID, lw), (NID, nsb)])
        at(r1 + 500)
        qw = tt(f(), rt, tt(f(), df, lw, A.mult), A.add)
        sj = ts(f(), dj, 0.0, A.is_equal)
        if t == 1:
            co = tt(f(), co, lane1k, A.add)
        at(r0 + (7600 if t else 9000))
        tt(full(CW, REST), ind(v("KT", 0, 4608), hx), full(zn), A.mult)
        at(r0 + 11500)
        act(full(CW, LEFT), full("sg"), F.Identity, bias=(MARK - e) / 2, scale=-(MARK + e) / 2)
        act(full(CW, RIGHT), full("sg"), F.Identity, bias=(MARK + e) / 2, scale=(MARK - e) / 2)
        for a in (LEFT, RIGHT):
            dma("G", ap(full(CW, a)), ap(full(CW, REST)), [full(CW, REST)], [full(CW, a)], 4000)
        at(r1 + 900)
        q = wrap(bank(0, 0, 64), ZM[QO], full("RG"), [(IDB, occ)])
        jn = wrap(bank(1, 0, 64), ZM[JN], full("RG"), [(ID, nsb), (ID, CM)])
        tn = wrap(bank(6, 448, 64), ZM[TW], full("RG"))
        if t == 1:
            cw = wrap(bank(7, 448, 64), ZM[CP], full("RG"), [(ID, nsb), (ID, CM)])
        at(r1 + 2200)
        q = tt(new("PI"), q, qw, A.max)
        si = ts(new("PI"), q, 12, A.arith_shift_right)
        sa = cp(new("PU"), si)
        for h in range(2):
            act(wide("G1", h), ind(v(CW, 0, 4096), half(sa, h)), F.Identity)
        jq = ts(new("PI"), q, 4080, A.bitwise_and)
        hl = new("PI", 128)
        hi = ts(sub(hl, 0, 64), q, 4095, A.bitwise_and)
        lo = ts(sub(hl, 64, 128), q, 12, A.arith_shift_right, 1023, A.bitwise_and)
        if not last:
            d0 = ts(f(), hi, 3584.0, A.is_ge, 512.0, A.mult)
            hx = cp(new("PU"), tt(p(), hi, d0, A.add))
        at(r1 + (2600 if last else 8000))
        u16 = new("PU", 128)
        if t:
            cp(u16, tt(new("PF", 128), hl, delta, A.add))
        else:
            cp(sub(u16, 0, 64), tt(f(), hi, delta, A.add))
            cp(sub(u16, 64, 128), sub(hl, 64, 128))
        hp, sm = sub(u16, 0, 64), sub(u16, 64, 128)
        at(r1 + 3300)
        fuse = tt(f(), tt(p(), jn, jq, A.is_equal), sj, A.max)
        at(r1 + (5400 if t else 3500))
        if t == 1:
            cw = tt(p(), cw, co, A.max)
        elif t == 0:
            cw = tt(p(), ts(p(), lo, 2.0, A.mult, float(LEFT + RIGHT), A.add), si, A.subtract)
        if not last:
            sz = cp(new("PU"), tt(p(), cw, fuse, A.mult))
            for h in range(2):
                at(r1 + (5600 if t else 4000) + 1000 * h)
                tt(wide("Z", h), ind(v(CW, 0, 4096), half(sz, h)), wide("G1", h), A.min)
        at(r1 + 4400)
        gt = tt(f() if last else p(), tn, lane16, A.is_gt)
        nup = tt(f(), fuse, gt, A.is_le)
        if last:
            so = cp(new("PU"), tt(p(), nup, lane16, A.mult))
            sb = cp(new("PU"), tt(f(), tn, tt(f(), fuse, gt, A.mult), A.mult))
            h16 = cp(new("PU"), hi)
        else:
            sb = tt(f(), tn, fuse, A.mult)
            tw = act(f(), tn, F.Identity, bias=1024.0 - B)
            at(r1 + 8100)
            sb = cp(new("PU"), sb)
        if not last:
            at(r1 + 4600)
            dr = tt(new("PB"), nup, d0, A.mult)
            sc = scan(new("PB"), dr)
            y = mm(bank(6, 0, 64), [(NBG, dr), (ONES, sc)])
            par = ts(new("PI"), q, 1, A.bitwise_and)
            at(r1 + 5200)
            lv = ts(new("PB"), y, 512.0 * (128 - B), A.is_lt, -512.0, A.mult)
            x2 = new("PB", 128)
            od = tt(sub(x2, 64, 128), par, lv, A.mult)
            tt(sub(x2, 0, 64), lv, od, A.subtract)
            sc = scan(new("PB", 128), x2)
            at(r1 + 9200)
            fr = tt(new("PB"), tt(p(), ts(p(), q, 4096.0, A.is_lt), nup, A.is_ge), lv, A.is_gt)
            at(r1 + 5900)
            e0, e1 = sub(sc, 63, 64), sub(sc, 127, 128)
            mm(bank(6, 64, 1), [(ONES, K7), (ONES, e0)])
            mm(bank(6, 65, 1), [(ONES, K7), (ONES, e0), (SO, e1), (NSO, e0)])
            mm(bank(6, 66, 1), [(ONES, K1), (ONES, e0), (NSO, e0)])
            mm(bank(6, 67, 1), [(NON, K1), (ONES, e0), (NSO, e0)])
            cs = act(v("cs%d" % (t + 1), 0, 4), bank(6, 64, 4), F.Identity, scale=-1 / 512.0)
            send(v("cn%d" % (t + 1), 0, 4), cs, eng[0:4], "rc%d" % (t + 1))
            mm(bank(6, 128, 128), [(ONES, sc)])
            mm(bank(6, 256, 128), [(NUS, x2), (ONES, sc)])
            at(r1 + 9500)
            act(v("Pc", 0, 128), bank(6, 256, 128), F.Identity, scale=-1 / 512.0)
            acc = new("PF", 8)
            for j in range(8):
                act(v("junk", 128 * j, 128 * j + 128), bank(6, 128, 128), F.Sign, bias=sub(jb, j, j + 1), scale=1 / 512.0, acc=sub(acc, j, j + 1))
            at(r1 + 11400)
            b16 = ts(new("PU", 8), acc, 0.5, A.mult, 64.0, A.add)
            cm = tt(new("PB", 128), ind(v("Pc", 0, 136), b16), JW, A.is_le)
            b6 = act(new("PF", 8), acc, F.Identity, scale=8.0, bias=1024.0)
            lvl = cp(new("PU", 8), ts(new("PI", 8), tt(new("PI", 8), wrap(bank(6, 384, 8), ZS, cm), b6, A.add), 1023, A.bitwise_and))
        an = "AW%d" % (t + 1)
        at(r1 + (4700 if last else 13600))
        if SPARE[t]:
            for h in range(2):
                act(wide("DG", h), ind(v("DT", 0, 4608), half(hp, h)), F.Identity)
                step(wide("MG", h), wide("G1", h), True)
                act(bank(2 + h) if PICK[t] else wide("FM", h), mm(bank(2 + h), [(ID, wide("DG", h)), (IDB, wide("MG", h))]), F.Sigmoid)
        if PICK[t]:
            act(full("Y2"), ind(aw, sm), F.Identity)
        if not SPARE[t]:
            act(full("FP"), ind(v("DT", 0, 4608), hp), F.Sigmoid)
            for h in range(2):
                step(bank(2 + h), wide("G1", h), False)
            at(r1 + (7500 if last else STEP + 600))
            for h in range(2):
                tt(bank(2 + h) if PICK[t] else wide("FM", h), wide("FP", h), bank(2 + h), A.mult)
        at(r1 + (7600 if last else STEP + 700))
        if PICK[t]:
            for h in range(2):
                tt(wide(an, h, 16), wide("Y2", h), bank(2 + h), A.mult)
        else:
            tt(full(an, 16), ind(aw, sm), full("FM"), A.mult)
        if last:
            at(r1 + 6000)
            for h in range(2):
                tt(wide("AW1", h, 16), wide("G1", h), bank(2 + h), A.mult)
            at(r1 + 8000)
            for h in range(2):
                act(wide("Z", h), ind(v("AW1", 0, 1040), half(so, h)), F.Identity)
                tt(wide("Y2", h), ind(v("AW1", 0, 1040), half(sb, h)), wide("Z", h), A.add)
                dma("Y", T.yc[:, H[h][0]:H[h][1]], ap(wide("Y2", h)), [wide("Y2", h)], [], 2400)
            for h in range(2):
                at(r1 + 10000 + 100 * h)
                act(wide("FP", h), ind(v(an, 0, 1040), half(so, h)), F.Identity)
                tt(wide("FM", h), ind(v(an, 0, 1040), half(sb, h)), wide("FP", h), A.add)
                for a, b in ((512, 832), (832, 1024)) if h else ((0, 512),):
                    tt(v("Y1", a, b), ind(v("KT", 0, 4096), sub(h16, a // 16, b // 16)), v("FM", a, b), A.mult)
                    dma("Y", T.ya[:, a:b], ap(v("Y1", a, b)), [v("Y1", a, b)], [], 2000 + b - a)
            break
        bc, ba = "bc%d" % (t + 1), "ba%d" % (t + 1)
        at(r1 + 13300)
        act(v(bc, 0, 128), ind(full("Z"), lvl), F.Identity, scale=0.5)
        dma("Y", T[bc][16:128, 128:256], T[bc][0:112, 0:128], [v(bc, 0, 128)], [v(bc, 128, 256, 1, (16, 128, 1))], 2200)
        dma("Y", T[bc][0:16, 128:256], T[bc][112:128, 0:128], [v(bc, 0, 128)], [v(bc, 128, 256, 1, (0, 16, 1))], 2200)
        send(v("CW%d" % (t + 1), ARR, ARR + 256), v(bc, 0, 256), eng[0:4], "rd%d" % (t + 1))
        at(r1 + STEP + 4000)
        act(full("Y1"), ind(v(an, 0, 1040), sb), F.Identity)
        tt(v(ba, 0, 128), ind(full("Y1"), lvl), act(new("PF", 128), ind(full(an, 16), lvl), F.Identity), A.add)
        dma("G", ap(full(an, 16)), ap(full("Y1")), [full("Y1")], [full(an, 16)], 4000)
        act(v(ba, 128, 256), mm(bank(5, 384, 128), [(SF, v(ba, 0, 128))], 4), F.Identity)
        send(v(an, 1024 + ARR, 1024 + ARR + 256), v(ba, 0, 256), eng[0:4], "ra%d" % (t + 1))
    return ops


HOP, TRIES, MOVES, HEAT, SEED, FOUND = 120, 3000, 120000, 110.0, 1, {}
PULL, PULL2, BACK, RESET = 1e-4, 0.1, 0.97, 0.02


def meet(a, b):
    if a[0] != b[0] or a[2] <= b[1] or b[2] <= a[1]:
        return False
    if (a[3] > 1 or b[3] > 1) and not set(range(a[1], a[2], a[3])) & set(range(b[1], b[2], b[3])):
        return False
    if a[4] and b[4]:
        if a[4][1] <= b[4][0] or b[4][1] <= a[4][0]:
            return False
        if not set(range(*a[4])) & set(range(*b[4])):
            return False
    return True


def edges(ops):
    pre = [dict() for _ in ops]
    seen = {}
    for j, o in enumerate(ops):
        if "after" in o:
            pre[j][o["after"]] = False
        use = [(x, False) for x in o["rd"]] + [(x, True) for x in o["wr"]]
        for x, w in use:
            for i, y, wy in seen.get(x[0], []):
                if (w or wy) and meet(x, y):
                    pre[j][i] = ops[i]["q"] != "P" or o["q"] != "P"
        for x, w in use:
            seen.setdefault(x[0], []).append((j, x, w))
    done = [0] * len(ops)
    for j in range(len(ops)):
        far = 0
        for i in pre[j]:
            if pre[j][i] and ops[i]["q"] != "R":
                far |= done[i]
        for i in list(pre[j]):
            if far >> i & 1:
                del pre[j][i]
        done[j] = far
        for i in pre[j]:
            if pre[j][i]:
                done[j] |= 1 << i
    return pre


def place(seq, cut, key, fore, how, banks, first, start, end):
    start, end, key = list(start), list(end), list(key)
    line = {q: ([], []) for q in "VSPGYR"}
    held = {"P%d" % b: [] for b in range(8)}
    for s, j in sorted([(start[j], j) for j in seq[:cut]]):
        q = how[j][0]
        S, E = line[q]
        S.append(s)
        E.append(end[j])
        for b in banks[j]:
            held[b].append((s - HOP, end[j] + HOP, q))
    todo = []
    for j in seq[cut:]:
        x = key[j]
        for i, d in fore[j]:
            if key[i] >= x:
                x = key[j] = key[i] + 1e-3
        todo.append((x, j))
    todo.sort()
    for x, j in todo:
        s = first[j]
        for i, d in fore[j]:
            if end[i] + d > s:
                s = end[i] + d
        q, ns = how[j]
        S, E = line[q]
        k = m = len(S)
        while k and E[k - 1] > s:
            k -= 1
        while True:
            while k < m and S[k] < s + ns:
                if E[k] > s:
                    s = E[k]
                k += 1
            s0 = s
            for b in banks[j]:
                for a, z, q2 in held[b][-24:]:
                    if z > s and a < s + ns and q2 != q:
                        s = z
            if s == s0:
                break
        while k and S[k - 1] > s:
            k -= 1
        S.insert(k, s)
        E.insert(k, s + ns)
        for b in banks[j]:
            held[b].append((s - HOP, s + ns + HOP, q))
        start[j] = s
        end[j] = s + ns
    return start, end, key, seq[:cut] + [j for x, j in todo]


def polish(ops, pre, start, how, banks):
    n, gap = len(ops), 24
    rng = np.random.RandomState(SEED)
    up, down = [list(e) for e in pre], [[] for _ in ops]
    for j in range(n):
        for i in up[j]:
            down[i].append(j)
    alt = [list(o["alt"]) if "alt" in o else None for o in ops]
    flex, outs, big = [i for i in range(n) if alt[i]], [i for i in range(n) if not down[i]], [i for i in range(n) if "sca" in ops[i]]
    how = [x[0] for x in how]
    cases = []
    for gather, scatter, slow, hop, pool, issue in GUESSES:
        lat = [o.get("lat", 0) * slow for o in ops]
        ns = [{q: x[1] + o.get("ind", 0) * (gather - GATHER) + o.get("sca", 0) * (scatter - SCATTER) + pool * (q == "G")
               + issue * (q in "YS" and "lat" in o) for q, x in o.get("alt", {o["q"]: (0, o["ns"])}).items()} for o in ops]
        cases.append((ns, [[(i, lat[i] + hop if pre[j][i] else 0) for i in pre[j]] for j in range(n)], lat, hop))

    def run(seq, how, a, states):
        c, new = a // gap, []
        for (dur, fore, lat, hop), (end, marks) in zip(cases, states):
            free, held = dict(marks[c][0]), dict(marks[c][1])
            end, marks = list(end), marks[:c + 1]
            for k in range(c * gap, n):
                if k % gap == 0 and k > c * gap:
                    marks.append((dict(free), dict(held)))
                j = seq[k]
                q = how[j]
                s = free[q]
                for i, d in fore[j]:
                    if end[i] + d > s:
                        s = end[i] + d
                for b in banks[j]:
                    z, q2 = held[b]
                    if q2 != q and z > s:
                        s = z
                s += dur[j][q]
                for b in banks[j]:
                    held[b] = (s + hop, q)
                free[q] = end[j] = s
            new.append((end, marks))
        return new

    seq = sorted(range(n), key=lambda i: (start[i], i))
    now = top = pos = None
    state = run(seq, how, 0, [([0.0] * n, [({q: 0.0 for q in "VSPGYR"}, {"P%d" % b: (0.0, "P") for b in range(8)})]) for c in cases])
    held = []
    for k, u in enumerate(rng.rand(MOVES, 6).tolist()):
        sq, hw, st = seq, how, state
        if k:
            if u[0] < 0.75 and held:
                (i, j), m = held[int(u[1] * len(held))], int(u[2] * 4)
            elif u[0] < 0.85:
                i = j = flex[int(u[1] * len(flex))]
                m = 2
            else:
                a = int(u[1] * (n - 1))
                i, j, m = seq[a], seq[min(n - 1, a + 1 + int(u[2] * u[2] * 60))], int(u[0] * 1000) % 2
            if m >= 2 and alt[(i, j)[m - 2]]:
                x = (i, j)[m - 2]
                hw = list(how)
                hw[x] = alt[x][int(u[3] * len(alt[x]))]
                if hw[x] == how[x]:
                    continue
                a = pos[x]
            else:
                m, a, b = m % 2, pos[i], pos[j]
                got, todo = {(j, i)[m]}, [(j, i)[m]]
                while todo:
                    for w in (up, down)[m][todo.pop()]:
                        if a <= pos[w] <= b and w not in got:
                            got.add(w)
                            todo.append(w)
                if a >= b or (i, j)[m] in got:
                    continue
                inn, out = [w for w in seq[a:b + 1] if w in got], [w for w in seq[a:b + 1] if w not in got]
                sq = seq[:a] + (out + inn if m else inn + out) + seq[b + 1:]
            st = run(sq, hw, a, state)
        val = PULL * sum(st[0][0])
        for case, (en, marks) in zip(cases, st):
            val += (max([en[i] + case[2][i] for i in outs]) + PULL2 * sum([en[i] for i in big])) / len(cases)
        if now is None or val <= now - HEAT * (1.01 - k / MOVES) ** 2 * math.log(u[4]):
            now, seq, how, state = val, sq, hw, st
            if u[3] < 0.03:
                seq = sorted(seq, key=lambda i: st[0][0][i] - cases[0][0][i][hw[i]])
                state = run(seq, how, 0, state)
            if top is None or val < top[0]:
                top = (val, seq, [state[0][0][i] - cases[0][0][i][hw[i]] for i in range(n)], hw)
            pos = [0] * n
            for a, i in enumerate(seq):
                pos[i] = a
            (dur, fore, lat, hop), end = cases[int(u[5] * len(cases))], state[int(u[5] * len(cases))][0]
            j, held = max(outs, key=lambda i: end[i] + lat[i]), []
            while j is not None:
                s, nx = end[j] - dur[j][how[j]] - 0.5, None
                for i, d in fore[j]:
                    if end[i] + d > s:
                        nx = i
                a, q = pos[j] - 1, how[j]
                while nx is None and s > 0 and a >= 0:
                    i = seq[a]
                    if end[i] > s and how[i] == q or end[i] + hop > s and how[i] != q and set(banks[i]) & set(banks[j]):
                        nx = i
                        held.append((i, j))
                    a -= 1
                j = nx
    return top


def order(ops):
    n = len(ops)
    pre = edges(ops)
    banks = [sorted({x[0] for x in o["rd"] + o["wr"] if SCRATCH[x[0]][0] == "psum" and x[0] != "P4"}) for o in ops]
    if n not in FOUND:
        rng = np.random.RandomState(SEED)
        lat = [o.get("lat", 0) for o in ops]
        fore = [[(i, lat[i] + HOP if pre[j][i] else 0) for i in pre[j]] for j in range(n)]
        back = [[] for _ in ops]
        for j in range(n):
            for i, d in fore[j]:
                back[i].append((j, d))
        alt = [[(q, x[1]) for q, x in o["alt"].items()] if "alt" in o else None for o in ops]
        flex = [i for i in range(n) if alt[i]]
        tags = {}
        for i, o in enumerate(ops):
            tags.setdefault(o["tag"], []).append(i)
        tags = list(tags.values())
        how = [(o["q"], o["ns"]) for o in ops]
        tail = [0.0] * n
        for i in range(n - 1, -1, -1):
            tail[i] = how[i][1] + max([tail[j] + d for j, d in back[i]] + [lat[i]])
        key, zero = [float(o["when"]) for o in ops], [0.0] * n
        now = top = None
        big = [i for i in range(n) if ops[i]["q"] == "V" and ops[i]["ns"] > 1900]
        held, seq, begins, ends = [], list(range(n)), zero, zero
        for k in range(TRIES):
            ky, hw, u = list(key), list(how), float(rng.rand())
            if k and held and u < 0.7:
                i, j = held[int(rng.randint(len(held)))]
                m = int(rng.randint(5))
                if m < 2 and alt[(i, j)[m]]:
                    x = (i, j)[m]
                    hw[x] = alt[x][int(rng.randint(len(alt[x])))]
                elif m == 2:
                    ky[i] = ky[j] + 1 + float(rng.exponential(500))
                elif m == 3:
                    d, todo, got = ky[j] - ky[i] + 1 + float(rng.exponential(300)), [j], {j}
                    while todo:
                        x = todo.pop()
                        ky[x] -= d
                        for y, _ in fore[x]:
                            if y not in got and ky[y] > ky[x] - 300 and len(got) < 12:
                                got.add(y)
                                todo.append(y)
                else:
                    ky[j] = ky[i] - 1
            elif k and u < 0.8:
                x = flex[int(rng.randint(len(flex)))]
                hw[x] = alt[x][int(rng.randint(len(alt[x])))]
            elif k and u < 0.87:
                for i in rng.randint(0, n, 2):
                    ky[int(i)] += float(rng.normal()) * 1500
            elif k and u < 0.95:
                d = float(rng.normal()) * 2500
                for i in tags[int(rng.randint(len(tags)))]:
                    ky[i] += d
            elif k and u < BACK:
                ky = [-x for x in place(seq[::-1], 0, [-x for x in ends], back, hw, banks, lat, zero, zero)[1]]
            low = min([min(a, b) for a, b, x, y in zip(key, ky, how, hw) if a != b or x != y] or [-1e9])
            cut = 0
            while k and key[seq[cut]] < low:
                cut += 1
            st, en, ky, sq = place(seq, cut, ky, fore, hw, banks, zero, begins, ends)
            if rng.rand() < RESET:
                ky, sq = list(st), sorted(sq, key=lambda i: st[i])
            end = max(en[i] + lat[i] for i in range(n)) + PULL * sum(st) + PULL2 * sum(st[i] for i in big)
            if now is None or end <= now - HEAT * (1.02 - k / TRIES) * float(np.log(rng.rand())):
                now, key, how, begins, ends, seq = end, ky, hw, st, en, sq
                if top is None or end < top[0]:
                    top = (end, st, hw)
                before, last = [[] for _ in ops], {}
                for i in sorted(seq, key=lambda i: st[i]):
                    for r in [hw[i][0]] + banks[i]:
                        if r in last:
                            before[i].append(last[r])
                        last[r] = i
                j, held = max(range(n), key=lambda i: en[i] + lat[i]), []
                while j is not None:
                    nx = [i for i, d in fore[j] if en[i] + d > st[j] - 0.5]
                    if not nx:
                        nx = [i for i in before[j] if en[i] + HOP > st[j] - 0.5]
                        held += [(i, j) for i in nx[:1]]
                    j = nx[0] if nx else None
        FOUND[n] = polish(ops, pre, top[1], top[2], banks)
    seq, start = FOUND[n][1:3]
    for o, q in zip(ops, FOUND[n][3]):
        if "alt" in o:
            o["q"], o["fn"], o["ns"] = q, o["alt"][q][0], o["alt"][q][1]
    last = {}
    for j in seq:
        for b in banks[j]:
            for q, i in last.setdefault(b, {}).items():
                if q != ops[j]["q"]:
                    pre[j][i] = True
            last[b][ops[j]["q"]] = j
    post = [[] for _ in ops]
    for j in range(n):
        for i in pre[j]:
            post[i].append(j)
    return pre, post, seq, start


def order_old(ops):
    n = len(ops)
    pre = [dict() for _ in ops]
    seen = {}
    for j, o in enumerate(ops):
        if "after" in o:
            pre[j][o["after"]] = False
        for x, w in [(x, False) for x in o["rd"]] + [(x, True) for x in o["wr"]]:
            ps = SCRATCH[x[0]][0] == "psum"
            for i, y, wy in seen.get(x[0], []):
                if i == j:
                    continue
                same = ops[i]["q"] == o["q"] and "sem" not in ops[i]
                if ps and (not same or "alt" in o or "alt" in ops[i]):
                    pre[j][i] = True
                elif (w or wy) and meet(x, y):
                    pre[j][i] = pre[j].get(i, False) or not same or o["q"] != "P"
                elif ps and w and wy and o["q"] == "P":
                    pre[j][i] = pre[j].get(i, False)
        for x, w in [(x, False) for x in o["rd"]] + [(x, True) for x in o["wr"]]:
            seen.setdefault(x[0], []).append((j, x, w))
    done = [0] * n
    for j in range(n):
        far = 0
        for i in pre[j]:
            if pre[j][i] and ops[i]["q"] != "R":
                far |= done[i]
        for i in list(pre[j]):
            if far >> i & 1:
                del pre[j][i]
        done[j] = far
        for i in pre[j]:
            if pre[j][i]:
                done[j] |= 1 << i
    post = [[] for _ in ops]
    for j in range(n):
        for i in pre[j]:
            post[i].append(j)
    tail = [0.0] * n
    for i in range(n - 1, -1, -1):
        tail[i] = ops[i]["ns"] + ops[i].get("lat", 0) + max([tail[j] + HOP for j in post[i]] or [0])
    if n not in FOUND:
        rng = np.random.RandomState(7)
        best, pr = None, dict(enumerate(tail))
        flex = [i for i in range(n) if "alt" in ops[i]]
        top, lat = None, [o.get("lat", 0) for o in ops]
        fore = [[(j, lat[i] + HOP if pre[j][i] else 0) for j in post[i]] for i in range(n)]
        back = [[(i, lat[i] + HOP if pre[j][i] else 0) for i in pre[j]] for j in range(n)]

        def flip(i):
            a, b = list(ops[i]["alt"])[0], list(ops[i]["alt"])[-1]
            ops[i]["q"] = b if ops[i]["q"] == a else a
            ops[i]["fn"], ops[i]["ns"] = ops[i]["alt"][ops[i]["q"]]
        for k in range(TRIES):
            tr, fl = dict(pr), []
            if k % 2:
                a = int(rng.randint(n))
                for i in rng.randint(max(0, a - 60), min(n, a + 60), int(rng.randint(1, 12))):
                    tr[int(i)] += float(rng.normal()) * (300, 1000, 3000)[k % 3]
            elif k:
                a = int(rng.randint(len(flex)))
                fl = set(flex[int(i)] for i in rng.randint(max(0, a - 8), min(len(flex), a + 8), int(rng.randint(1, 4))))
                for i in fl:
                    flip(i)
            if k % 4 == 1 and best:
                seq, start = issue(ops, back, lat, {i: best[2][i] + ops[i]["ns"] + (tr[i] - pr[i]) for i in range(n)}, 0.3)
                tr = {i: start[i] + ops[i]["ns"] for i in range(n)}
            seq, start = issue(ops, fore, [0] * n, tr, 0.5)
            end = max(start[i] + ops[i]["ns"] + lat[i] for i in seq) + 2e-4 * sum(start)
            if best is None or end <= best[0] + 300.0 * (1 - k / TRIES) * float(rng.rand()) ** 2:
                best, pr = (end, seq, start), tr
                if top is None or end < top[0]:
                    top = best + ([o["q"] for o in ops],)
            else:
                for i in fl:
                    flip(i)
        FOUND[n] = top
    for o, q in zip(ops, FOUND[n][3]):
        if "alt" in o:
            o["q"] = q
            o["fn"], o["ns"] = o["alt"][q]
    return pre, post, FOUND[n][1], FOUND[n][2]


def issue(ops, post, first, tail, look):
    n = len(ops)
    left = [0] * n
    for p in post:
        for j, d in p:
            left[j] += 1
    ready = list(first)
    qs, ns = [o["q"] for o in ops], [o["ns"] for o in ops]
    free = {q: 0.0 for q in qs}
    pool = {q: [] for q in free}
    soonest = {q: 1e18 for q in free}
    for i in range(n):
        if not left[i]:
            pool[qs[i]].append(i)
            soonest[qs[i]] = min(soonest[qs[i]], ready[i])
    seq, start = [], [0.0] * n
    for _ in range(n):
        when, q = min((max(soonest[q], free[q]), q) for q in free)
        mine = pool[q]
        i = max([k for k in mine if ready[k] <= when + 1], key=tail.get)
        a, b = when + ns[i] * look, tail[i] + ns[i]
        soon = [k for k in mine if ready[k] < a and tail[k] > b]
        if soon:
            i = max(soon, key=tail.get)
        s = max(ready[i], free[q])
        start[i] = s
        e = free[q] = s + ns[i]
        mine.remove(i)
        soonest[q] = min([ready[k] for k in mine] or [1e18])
        seq.append(i)
        for j, d in post[i]:
            if e + d > ready[j]:
                ready[j] = e + d
            left[j] -= 1
            if not left[j]:
                pool[qs[j]].append(j)
                if ready[j] < soonest[qs[j]]:
                    soonest[qs[j]] = ready[j]
    return seq, start


def rank_program(g, core, T, topo):
    if T.rank_of(core) is None:
        return
    ops = plan(T, g, core, topo)
    pre, post, seq, start = order(ops)
    queue = {"V": g.vector, "S": g.scalar, "P": g.tensor, "G": g, "Y": g.sync}
    count = {"V": 0, "S": 0, "P": 0, "G": 0}
    mark, known, clock = {}, {q: {} for q in queue}, {}
    sent = 0
    for j in seq:
        o = ops[j]
        q = o["q"]
        if q == "R":
            mark[j] = (o["sem"], o["inc"])
            clock[j] = {o["sem"]: o["inc"]}
            continue
        need = {}
        for i in pre[j]:
            if pre[j][i]:
                s, k = mark[i]
                if known[q].get(s, 0) < k and need.get(s, (0, 0))[0] < k:
                    need[s] = (k, i)
        for s in sorted(need, key=lambda s: -start[need[s][1]]):
            k, i = need[s]
            if known[q].get(s, 0) < k:
                queue[q].wait_ge(T.sem[s], k)
                for s2, k2 in clock[i].items():
                    known[q][s2] = max(known[q].get(s2, 0), k2)
        if q == "G" and known[q].get(q, 0) < count[q]:
            g.wait_ge(T.sem[q], count[q])
            known[q][q] = count[q]
        ins = o["fn"]()
        clock[j] = dict(known[q])
        if "sem" in o:
            ins.then_inc(T.sem[o["sem"]], o["inc"])
            mark[j] = (o["sem"], o["inc"])
            clock[j][o["sem"]] = o["inc"]
        elif "sent" in o:
            sent += o["sent"]
        elif q == "G" or any(pre[k][j] for k in post[j]):
            count[q] += 1
            ins.then_inc(T.sem[q], 1)
            mark[j] = (q, count[q])
            clock[j][q] = count[q]
    for q in count:
        if count[q]:
            g.wait_ge(T.sem[q], count[q])
    g.wait_ge(T.sem.sent, sent)
    for o in ops:
        if "sem" in o:
            g.sync.wait_ge(T.sem[o["sem"]], o["inc"])
